import numpy as np
import ml_dtypes


def mxq(x, axis, fmt="e4m3"):
    dtype, down = {"e4m3": (ml_dtypes.float8_e4m3fn, 7), "e5m2": (ml_dtypes.float8_e5m2, 14)}[fmt]
    v = np.moveaxis(np.asarray(x, np.float32).astype(ml_dtypes.bfloat16).astype(np.float64), axis, -1)
    blocks = v.reshape(v.shape[:-1] + (-1, 32))
    amax = np.abs(blocks).max(-1, keepdims=True)
    byte = np.maximum(np.where(amax > 0, np.frexp(amax)[1] - 1 + 127, 0) - down, 1)
    scale = np.exp2(byte - 127.0)
    codes = (blocks / scale).astype(np.float32).astype(dtype).astype(np.float64)
    return np.moveaxis((codes * scale).reshape(v.shape), -1, axis)


WIDE = False


def mx_kscale(k, group=512):
    if not WIDE:
        return np.ones(k)
    levels = np.array([10, -10, 5, -5, 0])
    if group != 512:
        return np.exp2(np.random.permutation(np.resize(levels, k // group))).repeat(group)
    if k % 512:
        return np.exp2(np.random.permutation(np.resize(levels, k // 32))).repeat(32)
    a = np.empty((k // 512, 16))
    for p in range(k // 512):
        a[p, :8] = np.random.permutation(np.resize(levels, 8))
        for g in range(8):
            far = levels[np.abs(levels - a[p, g]) >= 10]
            a[p, g + 8] = far[np.random.randint(len(far))]
    return np.exp2(a.ravel()).repeat(32)


def f64(x):
    return np.asarray(x).astype(np.float64)


def striped(idx):
    return np.tile(np.asarray(idx).reshape(-1, 16).T, (8, 1)).astype(np.uint16)


def unstriped(offs):
    return offs[:16].T.reshape(-1).astype(np.int64)


H, KV, D, NQ, N = 8, 2, 128, 512, 512
CAP = 2.0


def setup_inputs():
    n = np.random.standard_normal
    s = mx_kscale(D, 0)[:, None]
    u = mx_kscale(N)
    t = np.random.uniform(0.5, 2.0, N) * u
    v = n((KV, N, 128))
    return {
        "qT": (n((H, D, NQ)) * s * (0.70 / np.sqrt(D))).astype(np.float32),
        "kT": (n((KV, D, N)) / s).astype(np.float32),
        "t": t.reshape(N, 1).astype(np.float32),
        "v": (v / t[:, None]).astype(np.float32),
        "kb": (0.5 * n((N, 1))).astype(np.float32),
        "mask": (np.arange(N)[:, None] <= np.sort(np.random.randint(N // 4, N, NQ))[None, :]).astype(np.float32),
    }


def reference(qT, kT, t, v, kb, mask):
    a = np.repeat(mxq(f64(kT), 1, "e4m3"), H // KV, 0).transpose(0, 2, 1) @ mxq(f64(qT), 1, "e4m3")
    a = a + f64(kb)
    a = CAP * np.tanh(a / CAP)
    p = a / (1.0 + np.exp(-a))
    p = p * f64(mask)
    w = p * f64(t)
    y = mxq(w, 1, "e4m3").transpose(0, 2, 1) @ np.repeat(mxq(f64(v), 1, "e4m3"), H // KV, 0)
    y = y / 16.0
    return y

@@ -1,0 +1,270 @@
+from contextlib import ExitStack
+
+import concourse.mybir as mybir
+
+H, KV, D, NQ, NT = 8, 2, 128, 512, 512
+FLOPS = 2 * 2 * H * NQ * NT * D
+
+F32 = mybir.dt.float32
+BF16 = mybir.dt.bfloat16
+U32 = mybir.dt.uint32
+I32 = mybir.dt.int32
+U8 = mybir.dt.uint8
+FP8X4 = mybir.dt.float8_e4m3fn_x4
+ACT = mybir.ActivationFunctionType
+ALU = mybir.AluOpType
+
+P = 128
+PACK = 4
+ROWS = 32
+N = 128
+HALF = 256
+
+HEADS = ((2, 3, 4, 5), (0, 1, 6, 7))
+UNITS = (
+    (0, 0, 0, 256), (2, 0, 0, 256), (0, 0, 256, 256), (2, 0, 256, 256),
+    (1, 0, 0, 512), (3, 0, 0, 512), (0, 1, 0, 512), (1, 1, 0, 512),
+    (3, 1, 0, 512), (2, 1, 0, 256), (2, 1, 256, 128), (2, 1, 384, 128),
+)
+BANKS = (2, 1, 2, 1)
+SCALAR_EVAC = 2
+
+
+def tile_rows_a_silu_kb_mask_cap_kernel(tc, qT, kT, t, v, kb, mask, out):
+    nc = tc.nc
+    with ExitStack() as ctx:
+        keep = ctx.enter_context(tc.tile_pool(name="keep", bufs=1))
+        work = ctx.enter_context(tc.tile_pool(name="work", bufs=3))
+        psum = ctx.enter_context(tc.psum_pool(name="psum", bufs=1))
+        ctx.enter_context(tc.manual_schedule())
+
+        k_raw = keep.tile([P, PACK, NT], F32, name="k_raw")
+        k_bf = keep.tile([P, PACK, N, PACK], BF16, name="k_bf", align_bytes=64)
+        k_mx = keep.tile([P, NT + NT // 4], U32, name="k_mx", align_bytes=64)
+        k_codes = k_mx[:, 0:NT]
+        k_scales = k_mx[:, NT : NT + NT // 4].bitcast(U8)
+        q_raw = [keep.tile([P, PACK, w], F32, name="q_raw%d" % i) for i, w in enumerate((HALF, HALF, NQ))]
+        q_bf = keep.tile([P, 2 * NQ, PACK], BF16, name="q_bf", align_bytes=64)
+        q_codes = keep.tile([P, 2 * NQ], U32, name="q_codes", align_bytes=64)
+        q_scales = keep.tile([P, 2 * NQ], U8, name="q_scales", align_bytes=64)
+        v_raw = keep.tile([P, KV, PACK, D], F32, name="v_raw")
+        v_bf = keep.tile([P, KV, D, PACK], BF16, name="v_bf", align_bytes=64)
+        v_codes = keep.tile([P, KV * D], U32, name="v_codes", align_bytes=64)
+        v_scales = keep.tile([P, KV * D], U8, name="v_scales", align_bytes=64)
+        m_raw = [keep.tile([P, PACK, HALF], F32, name="m_raw%d" % i) for i in range(2)]
+        mt = keep.tile([P, 2, NQ, 2], F32, name="mt")
+        kb_sb = keep.tile([P, PACK], F32, name="kb_sb")
+        kb_half = keep.tile([P, PACK], F32, name="kb_half")
+        t_sb = keep.tile([P, PACK], F32, name="t_sb")
+        warm = keep.tile([P, 2], F32, name="warm")
+        score_banks = [
+            [psum.tile([P, NQ], F32, name="sc%d_%d" % (g, b)) for b in range(BANKS[g])] for g in range(4)
+        ]
+        y_banks = [psum.tile([P, PACK, D], F32, name="y%d" % b) for b in range(2)]
+
+        def features(ap):
+            return ap.rearrange("h (p j) n -> (h p) j n", j=PACK)
+
+        def tokens(ap):
+            return ap.rearrange("(p j) n -> p j n", j=PACK)
+
+        nc.sync.dma_start(out=k_raw[0:ROWS], in_=features(kT[0:1]))
+        nc.scalar.dma_start(out=k_raw[2 * ROWS : 3 * ROWS], in_=features(kT[1:2]))
+        nc.sync.dma_start(out=q_raw[0][:], in_=features(qT[2:6, :, 0:HALF]))
+        nc.scalar.dma_start(out=kb_sb[:], in_=kb.rearrange("(p j) o -> p (j o)", j=PACK))
+        nc.sync.dma_start(out=q_raw[1][:], in_=features(qT[2:6, :, HALF:NQ]))
+        nc.sync.dma_start(out=t_sb[:], in_=t.rearrange("(p j) o -> p (j o)", j=PACK))
+        nc.sync.dma_start(out=m_raw[0][:], in_=tokens(mask[:, 0:HALF]))
+        nc.sync.dma_start(out=v_raw[:], in_=v.rearrange("g (p j) e -> p g j e", j=PACK))
+        nc.sync.dma_start(out=m_raw[1][:], in_=tokens(mask[:, HALF:NQ]))
+        nc.sync.dma_start(out=q_raw[2][0 : 2 * ROWS], in_=features(qT[0:2]))
+        nc.sync.dma_start(out=q_raw[2][2 * ROWS : P], in_=features(qT[6:8]))
+
+        nc.vector.memset(warm[:, 0:1], 0.0)
+        nc.scalar.activation(out=warm[:, 1:2], in_=warm[:, 0:1], func=ACT.Silu)
+        nc.vector.memset(k_mx[:, NT : NT + NT // 4], 0)
+        nc.vector.memset(k_raw[ROWS : 2 * ROWS], 0.0)
+
+        kp = 3 * ROWS
+
+        def k_cast_views(a):
+            dst = k_bf[0:kp, 2 * a : 2 * a + 2].rearrange("p r s j -> p s r j")
+            src = k_raw[0:kp].rearrange("p j (s r) -> p s r j", r=PACK)[:, :, 2 * a : 2 * a + 2, :]
+            return dst, src
+
+        def k_quant(r):
+            nc.vector.quantize_mx(
+                out=k_codes[0:kp, r * N : (r + 1) * N].bitcast(FP8X4),
+                scales=k_scales[0:kp, r * N : (r + 1) * N],
+                in_=k_bf[0:kp, r].rearrange("p s j -> p (s j)"),
+            )
+
+        def interleave(dst, src):
+            nc.vector.tensor_copy(
+                out=dst.rearrange("p (c i) j -> p c j i", i=4),
+                in_=src.rearrange("p j (c i) -> p c j i", i=4),
+            )
+
+        def q_quant(c0, w):
+            nc.vector.quantize_mx(
+                out=q_codes[:, c0 : c0 + w].bitcast(FP8X4),
+                scales=q_scales[:, c0 : c0 + w],
+                in_=q_bf[:, c0 : c0 + w, :].rearrange("p n j -> p (n j)"),
+            )
+
+        def mask_times_t(i):
+            for r in range(PACK):
+                nc.vector.tensor_scalar(
+                    out=m_raw[i][:, r, :], in0=m_raw[i][:, r, :], scalar1=t_sb[:, r : r + 1], scalar2=None, op0=ALU.mult
+                )
+
+        def mask_pairs(i):
+            nc.vector.tensor_copy(
+                out=mt[:, :, i * HALF : (i + 1) * HALF, :],
+                in_=m_raw[i][:].rearrange("p (a e) n -> p a n e", e=2),
+            )
+
+        dst, src = k_cast_views(0)
+        nc.vector.tensor_copy(out=dst, in_=src)
+        dst, src = k_cast_views(1)
+        nc.scalar.copy(out=dst, in_=src)
+        nc.vector.tensor_scalar(out=kb_half[:], in0=kb_sb[:], scalar1=0.5, scalar2=None, op0=ALU.mult)
+        k_quant(0)
+        k_quant(1)
+        interleave(q_bf[:, 0:N, :], q_raw[0][:, :, 0:N])
+        interleave(q_bf[:, N:HALF, :], q_raw[0][:, :, N:HALF])
+        q_quant(0, N)
+        q_quant(N, N)
+        k_quant(2)
+        k_quant(3)
+        nc.sync.dma_start(out=k_mx[ROWS : 2 * ROWS].bitcast(I32), in_=k_mx[0:ROWS].bitcast(I32))
+        nc.sync.dma_start(out=k_mx[3 * ROWS : P].bitcast(I32), in_=k_mx[2 * ROWS : 3 * ROWS].bitcast(I32))
+        interleave(q_bf[:, HALF:NQ, :], q_raw[1][:])
+        mask_times_t(0)
+        q_quant(HALF, HALF)
+        mask_pairs(0)
+        for g in range(KV):
+            interleave(v_bf[:, g], v_raw[:, g])
+
+        def v_quant():
+            nc.vector.quantize_mx(
+                out=v_codes[:].bitcast(FP8X4), scales=v_scales[:], in_=v_bf[:].rearrange("p g e j -> p (g e j)")
+            )
+
+        def late_q_cast():
+            interleave(q_bf[:, NQ : 2 * NQ, :], q_raw[2][:])
+
+        def late_mask():
+            v_quant()
+            mask_times_t(1)
+
+        extras_after_weights = {0: [late_mask], 1: [lambda: mask_pairs(1)], 2: [late_q_cast], 3: [lambda: q_quant(NQ, NQ)]}
+
+        n_units = len(UNITS)
+        order = [(0, 0), (0, 1)]
+        for i in range(1, n_units):
+            order += [(i, 0), (i - 1, 2), (i, 1), (i - 1, 3)]
+        order += [(n_units - 1, 2), (n_units - 1, 3)]
+        uses = [0, 0, 0, 0]
+        bank_of = {}
+        last = None
+        for i, r in order:
+            g = UNITS[i][0]
+            assert (g, uses[g] % BANKS[g]) != last
+            last = (g, uses[g] % BANKS[g])
+            bank_of[(i, r)] = score_banks[g][uses[g] % BANKS[g]]
+            uses[g] += 1
+
+        capped, gated, w_bf, w_codes, w_scales = {}, {}, {}, {}, {}
+
+        def scores(i, r):
+            g, s, q0, w = UNITS[i]
+            rows = slice(g * ROWS, (g + 1) * ROWS)
+            for c in range(0, w, N):
+                cols = slice(s * NQ + q0 + c, s * NQ + q0 + c + N)
+                nc.tensor.matmul_mx(
+                    out=bank_of[(i, r)][:, c : c + N],
+                    lhsT=k_codes[rows, r * N : (r + 1) * N].bitcast(FP8X4),
+                    lhsT_scale=k_scales[rows, r * N : (r + 1) * N],
+                    rhs=q_codes[rows, cols].bitcast(FP8X4),
+                    rhs_scale=q_scales[rows, cols],
+                    start=True,
+                    stop=True,
+                )
+
+        def cap(i, r):
+            w = UNITS[i][3]
+            if r == 0:
+                capped[i] = work.tile([P, PACK, w], F32, name="capped")
+            nc.scalar.activation(
+                out=capped[i][:, r, :], in_=bank_of[(i, r)][:, 0:w], func=ACT.Tanh, scale=0.5, bias=kb_half[:, r : r + 1]
+            )
+
+        def silu(i, a):
+            w = UNITS[i][3]
+            if a == 0:
+                gated[i] = work.tile([P, 2, w, 2], F32, name="gated")
+            nc.scalar.activation(
+                out=gated[i][:, a],
+                in_=capped[i][:, 2 * a : 2 * a + 2, :].rearrange("p e n -> p n e"),
+                func=ACT.Silu,
+                scale=2.0,
+            )
+
+        def weights(i):
+            q0, w = UNITS[i][2], UNITS[i][3]
+            w_bf[i] = work.tile([P, w, PACK], BF16, name="w_bf", align_bytes=64)
+            nc.vector.tensor_tensor(
+                out=w_bf[i][:].rearrange("p n (a e) -> p n a e", e=2),
+                in0=gated[i][:].rearrange("p a n e -> p n a e"),
+                in1=mt[:, :, q0 : q0 + w, :].rearrange("p a n e -> p n a e"),
+                op=ALU.mult,
+            )
+
+        def w_quant(i):
+            w = UNITS[i][3]
+            w_codes[i] = work.tile([P, w], U32, name="w_codes", align_bytes=64)
+            w_scales[i] = work.tile([P, w], U8, name="w_scales", align_bytes=64)
+            nc.vector.quantize_mx(
+                out=w_codes[i][:].bitcast(FP8X4), scales=w_scales[i][:], in_=w_bf[i][:].rearrange("p n j -> p (n j)")
+            )
+
+        def finish(i):
+            g, s, q0, w = UNITS[i]
+            head = HEADS[s][g]
+            e_cols = slice(head // 4 * D, (head // 4 + 1) * D)
+            y = y_banks[i % 2]
+            tiles = w // N
+            for c in range(tiles):
+                nc.tensor.matmul_mx(
+                    out=y[:, c, :],
+                    lhsT=w_codes[i][:, c * N : (c + 1) * N].bitcast(FP8X4),
+                    lhsT_scale=w_scales[i][:, c * N : (c + 1) * N],
+                    rhs=v_codes[:, e_cols].bitcast(FP8X4),
+                    rhs_scale=v_scales[:, e_cols],
+                    start=True,
+                    stop=True,
+                )
+            res = work.tile([P, tiles, D], F32, name="res")
+            if i >= n_units - SCALAR_EVAC:
+                nc.scalar.activation(out=res[:], in_=y[:, 0:tiles, :], func=ACT.Copy, scale=1.0 / 16.0)
+            else:
+                nc.vector.tensor_scalar(out=res[:], in0=y[:, 0:tiles, :], scalar1=1.0 / 16.0, scalar2=None, op0=ALU.mult)
+            nc.sync.dma_start(out=out[head, q0 : q0 + w, :].rearrange("(c p) e -> p c e", p=P), in_=res[:])
+
+        scores(*order[0])
+        scores(*order[1])
+        for n, (i, r) in enumerate(order):
+            cap(i, r)
+            if n + 2 < len(order):
+                scores(*order[n + 2])
+            if r >= 2:
+                silu(i, r - 2)
+            if r == 3:
+                weights(i)
+                for extra in extras_after_weights.get(i, []):
+                    extra()
+                if i > 0:
+                    finish(i - 1)
+                w_quant(i)
+        finish(n_units - 1)

@@ -22,12 +22,12 @@ HALF = 256
 
 HEADS = ((2, 3, 4, 5), (0, 1, 6, 7))
 UNITS = (
-    (0, 0, 0, 256), (2, 0, 0, 256), (0, 0, 256, 256), (2, 0, 256, 256),
-    (1, 0, 0, 512), (3, 0, 0, 512), (0, 1, 0, 512), (1, 1, 0, 512),
-    (3, 1, 0, 512), (2, 1, 0, 256), (2, 1, 256, 128), (2, 1, 384, 128),
+    (0, 0, 0), (2, 0, 0), (0, 0, 1), (1, 0, 0), (3, 0, 0), (2, 0, 1), (1, 0, 1), (3, 0, 1),
+    (0, 1, 0), (1, 1, 0), (3, 1, 0), (2, 1, 0), (1, 1, 1), (3, 1, 1), (0, 1, 1), (2, 1, 1),
 )
 BANKS = (2, 1, 2, 1)
 SCALAR_EVAC = 2
+EARLY_UNITS = 8
 
 
 def tile_rows_a_silu_kb_mask_cap_kernel(tc, qT, kT, t, v, kb, mask, out):
@@ -58,7 +58,7 @@ def tile_rows_a_silu_kb_mask_cap_kernel(tc, qT, kT, t, v, kb, mask, out):
         t_sb = keep.tile([P, PACK], F32, name="t_sb")
         warm = keep.tile([P, 2], F32, name="warm")
         score_banks = [
-            [psum.tile([P, NQ], F32, name="sc%d_%d" % (g, b)) for b in range(BANKS[g])] for g in range(4)
+            [psum.tile([P, 2, HALF], F32, name="sc%d_%d" % (g, b)) for b in range(BANKS[g])] for g in range(4)
         ]
         y_banks = [psum.tile([P, PACK, D], F32, name="y%d" % b) for b in range(2)]
 
@@ -76,9 +76,6 @@ def tile_rows_a_silu_kb_mask_cap_kernel(tc, qT, kT, t, v, kb, mask, out):
         nc.sync.dma_start(out=t_sb[:], in_=t.rearrange("(p j) o -> p (j o)", j=PACK))
         nc.sync.dma_start(out=m_raw[0][:], in_=tokens(mask[:, 0:HALF]))
         nc.sync.dma_start(out=v_raw[:], in_=v.rearrange("g (p j) e -> p g j e", j=PACK))
-        nc.sync.dma_start(out=m_raw[1][:], in_=tokens(mask[:, HALF:NQ]))
-        nc.sync.dma_start(out=q_raw[2][0 : 2 * ROWS], in_=features(qT[0:2]))
-        nc.sync.dma_start(out=q_raw[2][2 * ROWS : P], in_=features(qT[6:8]))
 
         nc.vector.memset(warm[:, 0:1], 0.0)
         nc.scalar.activation(out=warm[:, 1:2], in_=warm[:, 0:1], func=ACT.Silu)
@@ -139,6 +136,9 @@ def tile_rows_a_silu_kb_mask_cap_kernel(tc, qT, kT, t, v, kb, mask, out):
         k_quant(3)
         nc.sync.dma_start(out=k_mx[ROWS : 2 * ROWS].bitcast(I32), in_=k_mx[0:ROWS].bitcast(I32))
         nc.sync.dma_start(out=k_mx[3 * ROWS : P].bitcast(I32), in_=k_mx[2 * ROWS : 3 * ROWS].bitcast(I32))
+        nc.sync.dma_start(out=m_raw[1][:], in_=tokens(mask[:, HALF:NQ]))
+        nc.sync.dma_start(out=q_raw[2][0 : 2 * ROWS], in_=features(qT[0:2]))
+        nc.sync.dma_start(out=q_raw[2][2 * ROWS : P], in_=features(qT[6:8]))
         interleave(q_bf[:, HALF:NQ, :], q_raw[1][:])
         mask_times_t(0)
         q_quant(HALF, HALF)
@@ -151,120 +151,151 @@ def tile_rows_a_silu_kb_mask_cap_kernel(tc, qT, kT, t, v, kb, mask, out):
                 out=v_codes[:].bitcast(FP8X4), scales=v_scales[:], in_=v_bf[:].rearrange("p g e j -> p (g e j)")
             )
 
-        def late_q_cast():
-            interleave(q_bf[:, NQ : 2 * NQ, :], q_raw[2][:])
+        def late_q_cast(half):
+            interleave(q_bf[:, NQ + half * HALF : NQ + (half + 1) * HALF, :], q_raw[2][:, :, half * HALF : (half + 1) * HALF])
 
         def late_mask():
             v_quant()
             mask_times_t(1)
 
-        extras_after_weights = {0: [late_mask], 1: [lambda: mask_pairs(1)], 2: [late_q_cast], 3: [lambda: q_quant(NQ, NQ)]}
+        after_weights = {0: late_mask, 1: lambda: mask_pairs(1), 4: lambda: late_q_cast(0), 7: lambda: late_q_cast(1)}
+        after_quant = {4: lambda: q_quant(NQ, HALF), 7: lambda: q_quant(NQ + HALF, HALF)}
 
-        n_units = len(UNITS)
-        order = [(0, 0), (0, 1)]
-        for i in range(1, n_units):
-            order += [(i, 0), (i - 1, 2), (i, 1), (i - 1, 3)]
-        order += [(n_units - 1, 2), (n_units - 1, 3)]
+        last = len(UNITS) - 1
+        visits = [(0, 0)]
+        for i in range(1, last + 1):
+            visits += [(i, 0), (i - 1, 1)]
+        visits.append((last, 1))
         uses = [0, 0, 0, 0]
         bank_of = {}
-        last = None
-        for i, r in order:
+        for i, a in visits:
             g = UNITS[i][0]
-            assert (g, uses[g] % BANKS[g]) != last
-            last = (g, uses[g] % BANKS[g])
-            bank_of[(i, r)] = score_banks[g][uses[g] % BANKS[g]]
+            bank_of[(i, a)] = score_banks[g][uses[g] % BANKS[g]]
             uses[g] += 1
 
         capped, gated, w_bf, w_codes, w_scales = {}, {}, {}, {}, {}
 
-        def scores(i, r):
-            g, s, q0, w = UNITS[i]
-            rows = slice(g * ROWS, (g + 1) * ROWS)
-            for c in range(0, w, N):
-                cols = slice(s * NQ + q0 + c, s * NQ + q0 + c + N)
-                nc.tensor.matmul_mx(
-                    out=bank_of[(i, r)][:, c : c + N],
-                    lhsT=k_codes[rows, r * N : (r + 1) * N].bitcast(FP8X4),
-                    lhsT_scale=k_scales[rows, r * N : (r + 1) * N],
-                    rhs=q_codes[rows, cols].bitcast(FP8X4),
-                    rhs_scale=q_scales[rows, cols],
-                    start=True,
-                    stop=True,
-                )
+        def scores(*pairs):
+            for e in range(2):
+                for c in range(0, HALF, N):
+                    for i, a in pairs:
+                        g, s, half = UNITS[i]
+                        r = 2 * a + e
+                        rows = slice(g * ROWS, (g + 1) * ROWS)
+                        cols = slice(s * NQ + half * HALF + c, s * NQ + half * HALF + c + N)
+                        nc.tensor.matmul_mx(
+                            out=bank_of[(i, a)][:, e, c : c + N],
+                            lhsT=k_codes[rows, r * N : (r + 1) * N].bitcast(FP8X4),
+                            lhsT_scale=k_scales[rows, r * N : (r + 1) * N],
+                            rhs=q_codes[rows, cols].bitcast(FP8X4),
+                            rhs_scale=q_scales[rows, cols],
+                            start=True,
+                            stop=True,
+                        )
 
         def cap(i, r):
-            w = UNITS[i][3]
             if r == 0:
-                capped[i] = work.tile([P, PACK, w], F32, name="capped")
+                capped[i] = work.tile([P, PACK, HALF], F32, name="capped")
+                gated[i] = work.tile([P, 2, HALF, 2], F32, name="gated")
             nc.scalar.activation(
-                out=capped[i][:, r, :], in_=bank_of[(i, r)][:, 0:w], func=ACT.Tanh, scale=0.5, bias=kb_half[:, r : r + 1]
+                out=capped[i][:, r, :], in_=bank_of[(i, r // 2)][:, r % 2, :], func=ACT.Tanh, scale=0.5, bias=kb_half[:, r : r + 1]
             )
 
-        def silu(i, a):
-            w = UNITS[i][3]
-            if a == 0:
-                gated[i] = work.tile([P, 2, w, 2], F32, name="gated")
+        def silu(i, a, c0=0, w=HALF):
             nc.scalar.activation(
-                out=gated[i][:, a],
-                in_=capped[i][:, 2 * a : 2 * a + 2, :].rearrange("p e n -> p n e"),
+                out=gated[i][:, a, c0 : c0 + w, :],
+                in_=capped[i][:, 2 * a : 2 * a + 2, c0 : c0 + w].rearrange("p e n -> p n e"),
                 func=ACT.Silu,
                 scale=2.0,
             )
 
-        def weights(i):
-            q0, w = UNITS[i][2], UNITS[i][3]
-            w_bf[i] = work.tile([P, w, PACK], BF16, name="w_bf", align_bytes=64)
+        def weights(i, c0=0, w=HALF):
+            q0 = UNITS[i][2] * HALF + c0
+            w_bf[(i, c0)] = work.tile([P, w, PACK], BF16, name="w_bf", align_bytes=64)
             nc.vector.tensor_tensor(
-                out=w_bf[i][:].rearrange("p n (a e) -> p n a e", e=2),
-                in0=gated[i][:].rearrange("p a n e -> p n a e"),
+                out=w_bf[(i, c0)][:].rearrange("p n (a e) -> p n a e", e=2),
+                in0=gated[i][:, :, c0 : c0 + w, :].rearrange("p a n e -> p n a e"),
                 in1=mt[:, :, q0 : q0 + w, :].rearrange("p a n e -> p n a e"),
                 op=ALU.mult,
             )
 
-        def w_quant(i):
-            w = UNITS[i][3]
-            w_codes[i] = work.tile([P, w], U32, name="w_codes", align_bytes=64)
-            w_scales[i] = work.tile([P, w], U8, name="w_scales", align_bytes=64)
+        def w_quant(i, c0=0, w=HALF):
+            w_codes[(i, c0)] = work.tile([P, w], U32, name="w_codes", align_bytes=64, bufs=4)
+            w_scales[(i, c0)] = work.tile([P, w], U8, name="w_scales", align_bytes=64, bufs=4)
             nc.vector.quantize_mx(
-                out=w_codes[i][:].bitcast(FP8X4), scales=w_scales[i][:], in_=w_bf[i][:].rearrange("p n j -> p (n j)")
+                out=w_codes[(i, c0)][:].bitcast(FP8X4),
+                scales=w_scales[(i, c0)][:],
+                in_=w_bf[(i, c0)][:].rearrange("p n j -> p (n j)"),
             )
 
-        def finish(i):
-            g, s, q0, w = UNITS[i]
+        results = [0]
+
+        def finish(i, c0=0, w=HALF):
+            g, s, half = UNITS[i]
             head = HEADS[s][g]
+            q0 = half * HALF + c0
             e_cols = slice(head // 4 * D, (head // 4 + 1) * D)
-            y = y_banks[i % 2]
+            y = y_banks[results[0] % 2]
+            results[0] += 1
             tiles = w // N
             for c in range(tiles):
                 nc.tensor.matmul_mx(
                     out=y[:, c, :],
-                    lhsT=w_codes[i][:, c * N : (c + 1) * N].bitcast(FP8X4),
-                    lhsT_scale=w_scales[i][:, c * N : (c + 1) * N],
+                    lhsT=w_codes[(i, c0)][:, c * N : (c + 1) * N].bitcast(FP8X4),
+                    lhsT_scale=w_scales[(i, c0)][:, c * N : (c + 1) * N],
                     rhs=v_codes[:, e_cols].bitcast(FP8X4),
                     rhs_scale=v_scales[:, e_cols],
                     start=True,
                     stop=True,
                 )
-            res = work.tile([P, tiles, D], F32, name="res")
-            if i >= n_units - SCALAR_EVAC:
+            res = work.tile([P, tiles, D], F32, name="res", bufs=4)
+            if i > last - SCALAR_EVAC:
                 nc.scalar.activation(out=res[:], in_=y[:, 0:tiles, :], func=ACT.Copy, scale=1.0 / 16.0)
             else:
                 nc.vector.tensor_scalar(out=res[:], in0=y[:, 0:tiles, :], scalar1=1.0 / 16.0, scalar2=None, op0=ALU.mult)
             nc.sync.dma_start(out=out[head, q0 : q0 + w, :].rearrange("(c p) e -> p c e", p=P), in_=res[:])
 
-        scores(*order[0])
-        scores(*order[1])
-        for n, (i, r) in enumerate(order):
-            cap(i, r)
-            if n + 2 < len(order):
-                scores(*order[n + 2])
-            if r >= 2:
-                silu(i, r - 2)
-            if r == 3:
-                weights(i)
-                for extra in extras_after_weights.get(i, []):
-                    extra()
-                if i > 0:
-                    finish(i - 1)
-                w_quant(i)
-        finish(n_units - 1)
+        def complete(i):
+            silu(i, 1)
+            weights(i)
+            if i in after_weights:
+                after_weights[i]()
+            lag = 2 if i < EARLY_UNITS else 1
+            while results[0] <= i - lag:
+                finish(results[0])
+            w_quant(i)
+            if i in after_quant:
+                after_quant[i]()
+
+        scores((0, 0))
+        scores((1, 0), (0, 1))
+        cap(0, 0)
+        cap(0, 1)
+        for i in range(1, last):
+            cap(i, 0)
+            cap(i, 1)
+            scores((i + 1, 0), (i, 1))
+            if i == 1:
+                silu(0, 0)
+            if i == last - 1:
+                scores((last, 1))
+            cap(i - 1, 2)
+            cap(i - 1, 3)
+            silu(i, 0)
+            complete(i - 1)
+        cap(last, 0)
+        cap(last, 1)
+        cap(last - 1, 2)
+        cap(last - 1, 3)
+        cap(last, 2)
+        complete(last - 1)
+        cap(last, 3)
+        silu(last, 0)
+        for c0 in (0, N):
+            silu(last, 1, c0, N)
+            weights(last, c0, N)
+        for c0 in (0, N):
+            w_quant(last, c0, N)
+        finish(last - 1)
+        for c0 in (0, N):
+            finish(last, c0, N)

@@ -26,8 +26,8 @@ UNITS = (
     (0, 1, 0), (1, 1, 0), (3, 1, 0), (2, 1, 0), (1, 1, 1), (3, 1, 1), (0, 1, 1), (2, 1, 1),
 )
 BANKS = (2, 1, 2, 1)
-SCALAR_EVAC = 2
-EARLY_UNITS = 8
+SCALAR_EVAC = 3
+LAG = 2
 
 
 def tile_rows_a_silu_kb_mask_cap_kernel(tc, qT, kT, t, v, kb, mask, out):
@@ -125,11 +125,11 @@ def tile_rows_a_silu_kb_mask_cap_kernel(tc, qT, kT, t, v, kb, mask, out):
         nc.vector.tensor_copy(out=dst, in_=src)
         dst, src = k_cast_views(1)
         nc.scalar.copy(out=dst, in_=src)
-        nc.vector.tensor_scalar(out=kb_half[:], in0=kb_sb[:], scalar1=0.5, scalar2=None, op0=ALU.mult)
         k_quant(0)
         k_quant(1)
         interleave(q_bf[:, 0:N, :], q_raw[0][:, :, 0:N])
         interleave(q_bf[:, N:HALF, :], q_raw[0][:, :, N:HALF])
+        nc.vector.tensor_scalar(out=kb_half[:], in0=kb_sb[:], scalar1=0.5, scalar2=None, op0=ALU.mult)
         q_quant(0, N)
         q_quant(N, N)
         k_quant(2)
@@ -209,6 +209,14 @@ def tile_rows_a_silu_kb_mask_cap_kernel(tc, qT, kT, t, v, kb, mask, out):
                 scale=2.0,
             )
 
+        def silu_all(i, c0, w):
+            nc.scalar.activation(
+                out=gated[i][:, :, c0 : c0 + w, :],
+                in_=capped[i][:, :, c0 : c0 + w].rearrange("p (a e) n -> p a n e", e=2),
+                func=ACT.Silu,
+                scale=2.0,
+            )
+
         def weights(i, c0=0, w=HALF):
             q0 = UNITS[i][2] * HALF + c0
             w_bf[(i, c0)] = work.tile([P, w, PACK], BF16, name="w_bf", align_bytes=64)
@@ -260,9 +268,8 @@ def tile_rows_a_silu_kb_mask_cap_kernel(tc, qT, kT, t, v, kb, mask, out):
             weights(i)
             if i in after_weights:
                 after_weights[i]()
-            lag = 2 if i < EARLY_UNITS else 1
-            while results[0] <= i - lag:
-                finish(results[0])
+            if i >= LAG:
+                finish(i - LAG)
             w_quant(i)
             if i in after_quant:
                 after_quant[i]()
@@ -283,19 +290,18 @@ def tile_rows_a_silu_kb_mask_cap_kernel(tc, qT, kT, t, v, kb, mask, out):
             cap(i - 1, 3)
             silu(i, 0)
             complete(i - 1)
-        cap(last, 0)
-        cap(last, 1)
         cap(last - 1, 2)
         cap(last - 1, 3)
-        cap(last, 2)
+        cap(last, 0)
         complete(last - 1)
-        cap(last, 3)
-        silu(last, 0)
+        for r in range(1, PACK):
+            cap(last, r)
         for c0 in (0, N):
-            silu(last, 1, c0, N)
+            silu_all(last, c0, N)
             weights(last, c0, N)
         for c0 in (0, N):
             w_quant(last, c0, N)
+        finish(last - 2)
         finish(last - 1)
         for c0 in (0, N):
             finish(last, c0, N)

@@ -140,8 +140,8 @@ def tile_rows_a_silu_kb_mask_cap_kernel(tc, qT, kT, t, v, kb, mask, out):
         nc.sync.dma_start(out=q_raw[2][0 : 2 * ROWS], in_=features(qT[0:2]))
         nc.sync.dma_start(out=q_raw[2][2 * ROWS : P], in_=features(qT[6:8]))
         interleave(q_bf[:, HALF:NQ, :], q_raw[1][:])
-        mask_times_t(0)
         q_quant(HALF, HALF)
+        mask_times_t(0)
         mask_pairs(0)
         for g in range(KV):
             interleave(v_bf[:, g], v_raw[:, g])
@@ -274,8 +274,8 @@ def tile_rows_a_silu_kb_mask_cap_kernel(tc, qT, kT, t, v, kb, mask, out):
             if i in after_quant:
                 after_quant[i]()
 
-        scores((0, 0))
-        scores((1, 0), (0, 1))
+        scores((0, 0), (1, 0))
+        scores((0, 1))
         cap(0, 0)
         cap(0, 1)
         for i in range(1, last):

@@ -21,12 +21,7 @@ N = 128
 HALF = 256
 
 HEADS = ((2, 3, 4, 5), (0, 1, 6, 7))
-UNITS = (
-    (0, 0, 0), (2, 0, 0), (0, 0, 1), (1, 0, 0), (3, 0, 0), (2, 0, 1), (1, 0, 1), (3, 0, 1),
-    (0, 1, 0), (1, 1, 0), (3, 1, 0), (2, 1, 0), (1, 1, 1), (3, 1, 1), (0, 1, 1), (2, 1, 1),
-)
 BANKS = (2, 1, 2, 1)
-SCALAR_EVAC = 3
 LAG = 2
 
 
@@ -43,7 +38,7 @@ def tile_rows_a_silu_kb_mask_cap_kernel(tc, qT, kT, t, v, kb, mask, out):
         k_mx = keep.tile([P, NT + NT // 4], U32, name="k_mx", align_bytes=64)
         k_codes = k_mx[:, 0:NT]
         k_scales = k_mx[:, NT : NT + NT // 4].bitcast(U8)
-        q_raw = [keep.tile([P, PACK, w], F32, name="q_raw%d" % i) for i, w in enumerate((HALF, HALF, NQ))]
+        q_raw = [keep.tile([P, PACK, w], F32, name="q_raw%d" % i) for i, w in enumerate((N, N, HALF, NQ))]
         q_bf = keep.tile([P, 2 * NQ, PACK], BF16, name="q_bf", align_bytes=64)
         q_codes = keep.tile([P, 2 * NQ], U32, name="q_codes", align_bytes=64)
         q_scales = keep.tile([P, 2 * NQ], U8, name="q_scales", align_bytes=64)
@@ -51,14 +46,13 @@ def tile_rows_a_silu_kb_mask_cap_kernel(tc, qT, kT, t, v, kb, mask, out):
         v_bf = keep.tile([P, KV, D, PACK], BF16, name="v_bf", align_bytes=64)
         v_codes = keep.tile([P, KV * D], U32, name="v_codes", align_bytes=64)
         v_scales = keep.tile([P, KV * D], U8, name="v_scales", align_bytes=64)
-        m_raw = [keep.tile([P, PACK, HALF], F32, name="m_raw%d" % i) for i in range(2)]
-        mt = keep.tile([P, 2, NQ, 2], F32, name="mt")
+        mt = keep.tile([P, PACK, NQ], F32, name="mt")
         kb_sb = keep.tile([P, PACK], F32, name="kb_sb")
         kb_half = keep.tile([P, PACK], F32, name="kb_half")
         t_sb = keep.tile([P, PACK], F32, name="t_sb")
         warm = keep.tile([P, 2], F32, name="warm")
         score_banks = [
-            [psum.tile([P, 2, HALF], F32, name="sc%d_%d" % (g, b)) for b in range(BANKS[g])] for g in range(4)
+            [psum.tile([P, NQ], F32, name="sc%d_%d" % (g, b)) for b in range(BANKS[g])] for g in range(4)
         ]
         y_banks = [psum.tile([P, PACK, D], F32, name="y%d" % b) for b in range(2)]
 
@@ -70,11 +64,12 @@ def tile_rows_a_silu_kb_mask_cap_kernel(tc, qT, kT, t, v, kb, mask, out):
 
         nc.sync.dma_start(out=k_raw[0:ROWS], in_=features(kT[0:1]))
         nc.scalar.dma_start(out=k_raw[2 * ROWS : 3 * ROWS], in_=features(kT[1:2]))
-        nc.sync.dma_start(out=q_raw[0][:], in_=features(qT[2:6, :, 0:HALF]))
+        nc.sync.dma_start(out=q_raw[0][:], in_=features(qT[2:6, :, 0:N]))
         nc.scalar.dma_start(out=kb_sb[:], in_=kb.rearrange("(p j) o -> p (j o)", j=PACK))
-        nc.sync.dma_start(out=q_raw[1][:], in_=features(qT[2:6, :, HALF:NQ]))
+        nc.sync.dma_start(out=q_raw[1][:], in_=features(qT[2:6, :, N:HALF]))
+        nc.sync.dma_start(out=q_raw[2][:], in_=features(qT[2:6, :, HALF:NQ]))
         nc.sync.dma_start(out=t_sb[:], in_=t.rearrange("(p j) o -> p (j o)", j=PACK))
-        nc.sync.dma_start(out=m_raw[0][:], in_=tokens(mask[:, 0:HALF]))
+        nc.sync.dma_start(out=mt[:], in_=tokens(mask))
         nc.sync.dma_start(out=v_raw[:], in_=v.rearrange("g (p j) e -> p g j e", j=PACK))
 
         nc.vector.memset(warm[:, 0:1], 0.0)
@@ -109,40 +104,32 @@ def tile_rows_a_silu_kb_mask_cap_kernel(tc, qT, kT, t, v, kb, mask, out):
                 in_=q_bf[:, c0 : c0 + w, :].rearrange("p n j -> p (n j)"),
             )
 
-        def mask_times_t(i):
+        def mask_times_t():
             for r in range(PACK):
                 nc.vector.tensor_scalar(
-                    out=m_raw[i][:, r, :], in0=m_raw[i][:, r, :], scalar1=t_sb[:, r : r + 1], scalar2=None, op0=ALU.mult
+                    out=mt[:, r, :], in0=mt[:, r, :], scalar1=t_sb[:, r : r + 1], scalar2=None, op0=ALU.mult
                 )
-
-        def mask_pairs(i):
-            nc.vector.tensor_copy(
-                out=mt[:, :, i * HALF : (i + 1) * HALF, :],
-                in_=m_raw[i][:].rearrange("p (a e) n -> p a n e", e=2),
-            )
 
         dst, src = k_cast_views(0)
         nc.vector.tensor_copy(out=dst, in_=src)
         dst, src = k_cast_views(1)
         nc.scalar.copy(out=dst, in_=src)
+        nc.scalar.activation(out=kb_half[:], in_=kb_sb[:], func=ACT.Copy, scale=0.5)
+        interleave(q_bf[:, 0:N, :], q_raw[0][:])
         k_quant(0)
         k_quant(1)
-        interleave(q_bf[:, 0:N, :], q_raw[0][:, :, 0:N])
-        interleave(q_bf[:, N:HALF, :], q_raw[0][:, :, N:HALF])
-        nc.vector.tensor_scalar(out=kb_half[:], in0=kb_sb[:], scalar1=0.5, scalar2=None, op0=ALU.mult)
         q_quant(0, N)
-        q_quant(N, N)
+        interleave(q_bf[:, N:HALF, :], q_raw[1][:])
         k_quant(2)
+        q_quant(N, N)
         k_quant(3)
         nc.sync.dma_start(out=k_mx[ROWS : 2 * ROWS].bitcast(I32), in_=k_mx[0:ROWS].bitcast(I32))
         nc.sync.dma_start(out=k_mx[3 * ROWS : P].bitcast(I32), in_=k_mx[2 * ROWS : 3 * ROWS].bitcast(I32))
-        nc.sync.dma_start(out=m_raw[1][:], in_=tokens(mask[:, HALF:NQ]))
-        nc.sync.dma_start(out=q_raw[2][0 : 2 * ROWS], in_=features(qT[0:2]))
-        nc.sync.dma_start(out=q_raw[2][2 * ROWS : P], in_=features(qT[6:8]))
-        interleave(q_bf[:, HALF:NQ, :], q_raw[1][:])
+        nc.sync.dma_start(out=q_raw[3][0 : 2 * ROWS], in_=features(qT[0:2]))
+        nc.sync.dma_start(out=q_raw[3][2 * ROWS : P], in_=features(qT[6:8]))
+        interleave(q_bf[:, HALF:NQ, :], q_raw[2][:])
         q_quant(HALF, HALF)
-        mask_times_t(0)
-        mask_pairs(0)
+        mask_times_t()
         for g in range(KV):
             interleave(v_bf[:, g], v_raw[:, g])
 
@@ -152,156 +139,194 @@ def tile_rows_a_silu_kb_mask_cap_kernel(tc, qT, kT, t, v, kb, mask, out):
             )
 
         def late_q_cast(half):
-            interleave(q_bf[:, NQ + half * HALF : NQ + (half + 1) * HALF, :], q_raw[2][:, :, half * HALF : (half + 1) * HALF])
+            interleave(q_bf[:, NQ + half * HALF : NQ + (half + 1) * HALF, :], q_raw[3][:, :, half * HALF : (half + 1) * HALF])
 
-        def late_mask():
+        def late_q():
             v_quant()
-            mask_times_t(1)
+            late_q_cast(0)
+            late_q_cast(1)
+            q_quant(NQ, HALF)
+            q_quant(NQ + HALF, HALF)
 
-        after_weights = {0: late_mask, 1: lambda: mask_pairs(1), 4: lambda: late_q_cast(0), 7: lambda: late_q_cast(1)}
-        after_quant = {4: lambda: q_quant(NQ, HALF), 7: lambda: q_quant(NQ + HALF, HALF)}
+        p0, p1, q0, q1 = (0, 0, 0, HALF), (0, 0, HALF, HALF), (2, 0, 0, HALF), (2, 0, HALF, HALF)
+        a, b0, b1 = (0, 1, 0, NQ), (2, 1, 0, HALF), (2, 1, HALF, HALF)
 
-        last = len(UNITS) - 1
-        visits = [(0, 0)]
-        for i in range(1, last + 1):
-            visits += [(i, 0), (i - 1, 1)]
-        visits.append((last, 1))
+        def caps(unit, slots, c0=0, w=None):
+            return [("cap", (unit, slots, c0, w or unit[3]), r) for r in slots]
+
+        def gate(unit, c0=0, w=HALF):
+            return [("silu", unit, c0, w)]
+
+        low, high = (0, 1), (2, 3)
+        order = caps(p0, low, 0, N) + caps(q0, low, 0, N) + caps(p0, low, N, N) + caps(q0, low, N, N)
+        order = order + caps(p0, high) + caps(q0, high) + gate(p0)
+        order = order + caps(p1, low) + caps(p1, high) + caps(q1, low) + caps(q1, high)
+        waiting = gate(q0) + gate(p1) + gate(q1)
+        for s in range(2):
+            x, y = (1, s, 0, NQ), (3, s, 0, NQ)
+            for r in range(PACK):
+                order = order + caps(x, (r,)) + caps(y, (r,))
+                if r == PACK - 1:
+                    waiting = gate(x) + gate(x, HALF) + gate(y) + gate(y, HALF)
+                order = order + waiting[:1]
+                waiting = waiting[1:]
+        for r in range(PACK):
+            order = order + caps(a, (r,)) + waiting[:1]
+            waiting = waiting[1:]
+        order = order + caps(b0, low) + gate(a) + caps(b0, high) + gate(a, HALF)
+        closing = caps(b1, low) + caps(b1, high)
+        order = order + closing[:1] + gate(b0) + closing[1:] + gate(b1, 0, N) + gate(b1, N, N)
+
+        fills, last_use, bank_of = [], {}, {}
         uses = [0, 0, 0, 0]
-        bank_of = {}
-        for i, a in visits:
-            g = UNITS[i][0]
-            bank_of[(i, a)] = score_banks[g][uses[g] % BANKS[g]]
-            uses[g] += 1
+        for n, step in enumerate(order):
+            if step[0] == "cap":
+                fill = step[1]
+                g = fill[0][0]
+                if fill not in bank_of:
+                    fills.append(fill)
+                    bank_of[fill] = (g, uses[g] % BANKS[g])
+                    uses[g] += 1
+                last_use[fill] = n
 
         capped, gated, w_bf, w_codes, w_scales = {}, {}, {}, {}, {}
 
-        def scores(*pairs):
-            for e in range(2):
-                for c in range(0, HALF, N):
-                    for i, a in pairs:
-                        g, s, half = UNITS[i]
-                        r = 2 * a + e
-                        rows = slice(g * ROWS, (g + 1) * ROWS)
-                        cols = slice(s * NQ + half * HALF + c, s * NQ + half * HALF + c + N)
-                        nc.tensor.matmul_mx(
-                            out=bank_of[(i, a)][:, e, c : c + N],
-                            lhsT=k_codes[rows, r * N : (r + 1) * N].bitcast(FP8X4),
-                            lhsT_scale=k_scales[rows, r * N : (r + 1) * N],
-                            rhs=q_codes[rows, cols].bitcast(FP8X4),
-                            rhs_scale=q_scales[rows, cols],
-                            start=True,
-                            stop=True,
-                        )
+        def scores(fill):
+            unit, slots, c0, w = fill
+            g, s = unit[0], unit[1]
+            bank = score_banks[g][bank_of[fill][1]]
+            rows = slice(g * ROWS, (g + 1) * ROWS)
+            first = s * NQ + unit[2] + c0
+            for e, r in enumerate(slots):
+                for c in range(0, w, N):
+                    cols = slice(first + c, first + c + N)
+                    nc.tensor.matmul_mx(
+                        out=bank[:, e * w + c : e * w + c + N],
+                        lhsT=k_codes[rows, r * N : (r + 1) * N].bitcast(FP8X4),
+                        lhsT_scale=k_scales[rows, r * N : (r + 1) * N],
+                        rhs=q_codes[rows, cols].bitcast(FP8X4),
+                        rhs_scale=q_scales[rows, cols],
+                        start=True,
+                        stop=True,
+                    )
 
-        def cap(i, r):
-            if r == 0:
-                capped[i] = work.tile([P, PACK, HALF], F32, name="capped")
-                gated[i] = work.tile([P, 2, HALF, 2], F32, name="gated")
+        def cap(fill, r):
+            unit, slots, c0, w = fill
+            if unit not in capped:
+                capped[unit] = keep.tile([P, PACK, unit[3]], F32, name="capped%d_%d_%d" % unit[0:3])
+            bank = score_banks[unit[0]][bank_of[fill][1]]
+            e = slots.index(r)
             nc.scalar.activation(
-                out=capped[i][:, r, :], in_=bank_of[(i, r // 2)][:, r % 2, :], func=ACT.Tanh, scale=0.5, bias=kb_half[:, r : r + 1]
+                out=capped[unit][:, r, c0 : c0 + w],
+                in_=bank[:, e * w : (e + 1) * w],
+                func=ACT.Tanh,
+                scale=0.5,
+                bias=kb_half[:, r : r + 1],
             )
 
-        def silu(i, a, c0=0, w=HALF):
-            nc.scalar.activation(
-                out=gated[i][:, a, c0 : c0 + w, :],
-                in_=capped[i][:, 2 * a : 2 * a + 2, c0 : c0 + w].rearrange("p e n -> p n e"),
-                func=ACT.Silu,
-                scale=2.0,
-            )
+        pieces = [step[1:] for step in order if step[0] == "silu"]
+        last = len(pieces) - 1
 
-        def silu_all(i, c0, w):
-            nc.scalar.activation(
-                out=gated[i][:, :, c0 : c0 + w, :],
-                in_=capped[i][:, :, c0 : c0 + w].rearrange("p (a e) n -> p a n e", e=2),
-                func=ACT.Silu,
-                scale=2.0,
-            )
+        def silu(n):
+            unit, c0, w = pieces[n]
+            gated[n] = work.tile([P, PACK, w], F32, name="gated", bufs=4)
+            nc.scalar.activation(out=gated[n][:], in_=capped[unit][:, :, c0 : c0 + w], func=ACT.Silu, scale=2.0)
 
-        def weights(i, c0=0, w=HALF):
-            q0 = UNITS[i][2] * HALF + c0
-            w_bf[(i, c0)] = work.tile([P, w, PACK], BF16, name="w_bf", align_bytes=64)
+        def weights(n):
+            unit, c0, w = pieces[n]
+            first = unit[2] + c0
+            w_bf[n] = work.tile([P, w, PACK], BF16, name="w_bf", align_bytes=64)
             nc.vector.tensor_tensor(
-                out=w_bf[(i, c0)][:].rearrange("p n (a e) -> p n a e", e=2),
-                in0=gated[i][:, :, c0 : c0 + w, :].rearrange("p a n e -> p n a e"),
-                in1=mt[:, :, q0 : q0 + w, :].rearrange("p a n e -> p n a e"),
+                out=w_bf[n][:].rearrange("p (c i) r -> p c r i", i=4),
+                in0=gated[n][:].rearrange("p r (c i) -> p c r i", i=4),
+                in1=mt[:, :, first : first + w].rearrange("p r (c i) -> p c r i", i=4),
                 op=ALU.mult,
             )
 
-        def w_quant(i, c0=0, w=HALF):
-            w_codes[(i, c0)] = work.tile([P, w], U32, name="w_codes", align_bytes=64, bufs=4)
-            w_scales[(i, c0)] = work.tile([P, w], U8, name="w_scales", align_bytes=64, bufs=4)
+        def w_quant(n):
+            w = pieces[n][2]
+            w_codes[n] = work.tile([P, w], U32, name="w_codes", align_bytes=64, bufs=4)
+            w_scales[n] = work.tile([P, w], U8, name="w_scales", align_bytes=64, bufs=4)
             nc.vector.quantize_mx(
-                out=w_codes[(i, c0)][:].bitcast(FP8X4),
-                scales=w_scales[(i, c0)][:],
-                in_=w_bf[(i, c0)][:].rearrange("p n j -> p (n j)"),
+                out=w_codes[n][:].bitcast(FP8X4),
+                scales=w_scales[n][:],
+                in_=w_bf[n][:].rearrange("p n j -> p (n j)"),
             )
 
-        results = [0]
+        groups = [(n, n + 1) for n in range(0, last - 3, 2)] + [(n,) for n in range(last - 2, last + 1)]
+        place = {}
+        for i, group in enumerate(groups):
+            tile0 = 0
+            for n in group:
+                place[n] = (i, tile0)
+                tile0 += pieces[n][2] // N
 
-        def finish(i, c0=0, w=HALF):
-            g, s, half = UNITS[i]
-            head = HEADS[s][g]
-            q0 = half * HALF + c0
+        def second_product(n):
+            unit, c0, w = pieces[n]
+            head = HEADS[unit[1]][unit[0]]
             e_cols = slice(head // 4 * D, (head // 4 + 1) * D)
-            y = y_banks[results[0] % 2]
-            results[0] += 1
-            tiles = w // N
-            for c in range(tiles):
+            i, tile0 = place[n]
+            for c in range(w // N):
                 nc.tensor.matmul_mx(
-                    out=y[:, c, :],
-                    lhsT=w_codes[(i, c0)][:, c * N : (c + 1) * N].bitcast(FP8X4),
-                    lhsT_scale=w_scales[(i, c0)][:, c * N : (c + 1) * N],
+                    out=y_banks[i % 2][:, tile0 + c, :],
+                    lhsT=w_codes[n][:, c * N : (c + 1) * N].bitcast(FP8X4),
+                    lhsT_scale=w_scales[n][:, c * N : (c + 1) * N],
                     rhs=v_codes[:, e_cols].bitcast(FP8X4),
                     rhs_scale=v_scales[:, e_cols],
                     start=True,
                     stop=True,
                 )
+
+        def store(i, on_scalar):
+            tiles = sum(pieces[n][2] // N for n in groups[i])
+            y = y_banks[i % 2]
             res = work.tile([P, tiles, D], F32, name="res", bufs=4)
-            if i > last - SCALAR_EVAC:
+            if on_scalar:
                 nc.scalar.activation(out=res[:], in_=y[:, 0:tiles, :], func=ACT.Copy, scale=1.0 / 16.0)
             else:
                 nc.vector.tensor_scalar(out=res[:], in0=y[:, 0:tiles, :], scalar1=1.0 / 16.0, scalar2=None, op0=ALU.mult)
-            nc.sync.dma_start(out=out[head, q0 : q0 + w, :].rearrange("(c p) e -> p c e", p=P), in_=res[:])
+            for n in groups[i]:
+                unit, c0, w = pieces[n]
+                first = unit[2] + c0
+                tile0 = place[n][1]
+                nc.sync.dma_start(
+                    out=out[HEADS[unit[1]][unit[0]], first : first + w, :].rearrange("(c p) e -> p c e", p=P),
+                    in_=res[:, tile0 : tile0 + w // N, :],
+                )
 
-        def complete(i):
-            silu(i, 1)
-            weights(i)
-            if i in after_weights:
-                after_weights[i]()
-            if i >= LAG:
-                finish(i - LAG)
-            w_quant(i)
-            if i in after_quant:
-                after_quant[i]()
+        filled = []
 
-        scores((0, 0), (1, 0))
-        scores((0, 1))
-        cap(0, 0)
-        cap(0, 1)
-        for i in range(1, last):
-            cap(i, 0)
-            cap(i, 1)
-            scores((i + 1, 0), (i, 1))
-            if i == 1:
-                silu(0, 0)
-            if i == last - 1:
-                scores((last, 1))
-            cap(i - 1, 2)
-            cap(i - 1, 3)
-            silu(i, 0)
-            complete(i - 1)
-        cap(last - 1, 2)
-        cap(last - 1, 3)
-        cap(last, 0)
-        complete(last - 1)
-        for r in range(1, PACK):
-            cap(last, r)
-        for c0 in (0, N):
-            silu_all(last, c0, N)
-            weights(last, c0, N)
-        for c0 in (0, N):
-            w_quant(last, c0, N)
-        finish(last - 2)
-        finish(last - 1)
-        for c0 in (0, N):
-            finish(last, c0, N)
+        def refill(done):
+            while len(filled) < len(fills):
+                fill = fills[len(filled)]
+                if any(bank_of[f] == bank_of[fill] and last_use[f] > done for f in filled):
+                    break
+                scores(fill)
+                filled.append(fill)
+
+        refill(-1)
+        n = 0
+        for done, step in enumerate(order):
+            if step[0] == "cap":
+                cap(step[1], step[2])
+            else:
+                silu(n)
+                if n >= LAG:
+                    second_product(n - LAG)
+                weights(n)
+                if n == 0:
+                    late_q()
+                if n >= LAG and n < last - 1 and groups[place[n - LAG][0]][-1] == n - LAG:
+                    store(place[n - LAG][0], False)
+                if n < last - 1:
+                    w_quant(n)
+                n += 1
+            refill(done)
+        w_quant(last - 1)
+        w_quant(last)
+        store(len(groups) - 4, True)
+        second_product(last - 1)
+        store(len(groups) - 3, True)
+        second_product(last)
+        store(len(groups) - 2, True)
+        store(len(groups) - 1, False)

@@ -141,15 +141,11 @@ def tile_rows_a_silu_kb_mask_cap_kernel(tc, qT, kT, t, v, kb, mask, out):
         def late_q_cast(half):
             interleave(q_bf[:, NQ + half * HALF : NQ + (half + 1) * HALF, :], q_raw[3][:, :, half * HALF : (half + 1) * HALF])
 
-        def late_q():
-            v_quant()
-            late_q_cast(0)
-            late_q_cast(1)
-            q_quant(NQ, HALF)
-            q_quant(NQ + HALF, HALF)
+        after_weights = {0: v_quant, 2: lambda: late_q_cast(0), 4: lambda: late_q_cast(1)}
+        after_quant = {2: lambda: q_quant(NQ, HALF), 4: lambda: q_quant(NQ + HALF, HALF)}
 
         p0, p1, q0, q1 = (0, 0, 0, HALF), (0, 0, HALF, HALF), (2, 0, 0, HALF), (2, 0, HALF, HALF)
-        a, b0, b1 = (0, 1, 0, NQ), (2, 1, 0, HALF), (2, 1, HALF, HALF)
+        a0, a1, b0, b1 = (0, 1, 0, HALF), (0, 1, HALF, HALF), (2, 1, 0, HALF), (2, 1, HALF, HALF)
 
         def caps(unit, slots, c0=0, w=None):
             return [("cap", (unit, slots, c0, w or unit[3]), r) for r in slots]
@@ -162,18 +158,19 @@ def tile_rows_a_silu_kb_mask_cap_kernel(tc, qT, kT, t, v, kb, mask, out):
         order = order + caps(p0, high) + caps(q0, high) + gate(p0)
         order = order + caps(p1, low) + caps(p1, high) + caps(q1, low) + caps(q1, high)
         waiting = gate(q0) + gate(p1) + gate(q1)
-        for s in range(2):
-            x, y = (1, s, 0, NQ), (3, s, 0, NQ)
-            for r in range(PACK):
-                order = order + caps(x, (r,)) + caps(y, (r,))
-                if r == PACK - 1:
-                    waiting = gate(x) + gate(x, HALF) + gate(y) + gate(y, HALF)
-                order = order + waiting[:1]
-                waiting = waiting[1:]
+        x, y = (1, 0, 0, NQ), (3, 0, 0, NQ)
         for r in range(PACK):
-            order = order + caps(a, (r,)) + waiting[:1]
+            order = order + caps(x, (r,)) + caps(y, (r,))
+            if r == PACK - 1:
+                waiting = gate(x) + gate(x, HALF) + gate(y) + gate(y, HALF)
+            order = order + waiting[:1]
             waiting = waiting[1:]
-        order = order + caps(b0, low) + gate(a) + caps(b0, high) + gate(a, HALF)
+        for c0 in (0, HALF):
+            x, y = (1, 1, c0, HALF), (3, 1, c0, HALF)
+            order = order + caps(x, low) + caps(y, low) + waiting[:2] + caps(x, high) + caps(y, high) + waiting[2:] + gate(x)
+            waiting = gate(y)
+        order = order + caps(a0, low) + caps(a0, high) + waiting + caps(a1, low) + gate(a0) + caps(a1, high)
+        order = order + caps(b0, low) + gate(a1) + caps(b0, high)
         closing = caps(b1, low) + caps(b1, high)
         order = order + closing[:1] + gate(b0) + closing[1:] + gate(b1, 0, N) + gate(b1, N, N)
 
@@ -314,12 +311,14 @@ def tile_rows_a_silu_kb_mask_cap_kernel(tc, qT, kT, t, v, kb, mask, out):
                 if n >= LAG:
                     second_product(n - LAG)
                 weights(n)
-                if n == 0:
-                    late_q()
+                if n in after_weights:
+                    after_weights[n]()
                 if n >= LAG and n < last - 1 and groups[place[n - LAG][0]][-1] == n - LAG:
                     store(place[n - LAG][0], False)
                 if n < last - 1:
                     w_quant(n)
+                if n in after_quant:
+                    after_quant[n]()
                 n += 1
             refill(done)
         w_quant(last - 1)

@@ -20,33 +20,33 @@ ROWS = 32
 N = 128
 HALF = 256
 
-HEADS = ((2, 3, 4, 5), (0, 1, 6, 7))
+HEADS = {(0, 0): 0, (0, 1): 1, (1, 1): 2, (1, 2): 3, (2, 0): 4, (2, 1): 5, (3, 1): 6, (3, 2): 7}
 BANKS = (2, 1, 2, 1)
-LAG = 2
+LAG = 3
+FIRST_PRODUCT = 6
 
 
 def tile_rows_a_silu_kb_mask_cap_kernel(tc, qT, kT, t, v, kb, mask, out):
     nc = tc.nc
     with ExitStack() as ctx:
         keep = ctx.enter_context(tc.tile_pool(name="keep", bufs=1))
-        work = ctx.enter_context(tc.tile_pool(name="work", bufs=3))
         psum = ctx.enter_context(tc.psum_pool(name="psum", bufs=1))
         ctx.enter_context(tc.manual_schedule())
 
-        k_raw = keep.tile([P, PACK, NT], F32, name="k_raw")
+        k_raw = [keep.tile([P, PACK, HALF], F32, name="k_raw%d" % i) for i in range(2)]
         k_bf = keep.tile([P, PACK, N, PACK], BF16, name="k_bf", align_bytes=64)
         k_mx = keep.tile([P, NT + NT // 4], U32, name="k_mx", align_bytes=64)
         k_codes = k_mx[:, 0:NT]
         k_scales = k_mx[:, NT : NT + NT // 4].bitcast(U8)
-        q_raw = [keep.tile([P, PACK, w], F32, name="q_raw%d" % i) for i, w in enumerate((N, N, HALF, NQ))]
-        q_bf = keep.tile([P, 2 * NQ, PACK], BF16, name="q_bf", align_bytes=64)
-        q_codes = keep.tile([P, 2 * NQ], U32, name="q_codes", align_bytes=64)
-        q_scales = keep.tile([P, 2 * NQ], U8, name="q_scales", align_bytes=64)
+        q_raw = [keep.tile([P, PACK, NQ], F32, name="q_raw%d" % i) for i in range(2)]
+        q_bf = keep.tile([P, 3 * NQ, PACK], BF16, name="q_bf", align_bytes=64)
+        q_codes = keep.tile([P, 3 * NQ], U32, name="q_codes", align_bytes=64)
+        q_scales = keep.tile([P, 3 * NQ], U8, name="q_scales", align_bytes=64)
         v_raw = keep.tile([P, KV, PACK, D], F32, name="v_raw")
         v_bf = keep.tile([P, KV, D, PACK], BF16, name="v_bf", align_bytes=64)
         v_codes = keep.tile([P, KV * D], U32, name="v_codes", align_bytes=64)
         v_scales = keep.tile([P, KV * D], U8, name="v_scales", align_bytes=64)
-        mt = keep.tile([P, PACK, NQ], F32, name="mt")
+        mt = [keep.tile([P, PACK, HALF], F32, name="mt%d" % i) for i in range(2)]
         kb_sb = keep.tile([P, PACK], F32, name="kb_sb")
         kb_half = keep.tile([P, PACK], F32, name="kb_half")
         t_sb = keep.tile([P, PACK], F32, name="t_sb")
@@ -62,26 +62,14 @@ def tile_rows_a_silu_kb_mask_cap_kernel(tc, qT, kT, t, v, kb, mask, out):
         def tokens(ap):
             return ap.rearrange("(p j) n -> p j n", j=PACK)
 
-        nc.sync.dma_start(out=k_raw[0:ROWS], in_=features(kT[0:1]))
-        nc.scalar.dma_start(out=k_raw[2 * ROWS : 3 * ROWS], in_=features(kT[1:2]))
-        nc.sync.dma_start(out=q_raw[0][:], in_=features(qT[2:6, :, 0:N]))
-        nc.scalar.dma_start(out=kb_sb[:], in_=kb.rearrange("(p j) o -> p (j o)", j=PACK))
-        nc.sync.dma_start(out=q_raw[1][:], in_=features(qT[2:6, :, N:HALF]))
-        nc.sync.dma_start(out=q_raw[2][:], in_=features(qT[2:6, :, HALF:NQ]))
-        nc.sync.dma_start(out=t_sb[:], in_=t.rearrange("(p j) o -> p (j o)", j=PACK))
-        nc.sync.dma_start(out=mt[:], in_=tokens(mask))
-        nc.sync.dma_start(out=v_raw[:], in_=v.rearrange("g (p j) e -> p g j e", j=PACK))
-
-        nc.vector.memset(warm[:, 0:1], 0.0)
-        nc.scalar.activation(out=warm[:, 1:2], in_=warm[:, 0:1], func=ACT.Silu)
-        nc.vector.memset(k_mx[:, NT : NT + NT // 4], 0)
-        nc.vector.memset(k_raw[ROWS : 2 * ROWS], 0.0)
+        def rows_of(g, count=1):
+            return slice(g * ROWS, (g + count) * ROWS)
 
         kp = 3 * ROWS
 
-        def k_cast_views(a):
-            dst = k_bf[0:kp, 2 * a : 2 * a + 2].rearrange("p r s j -> p s r j")
-            src = k_raw[0:kp].rearrange("p j (s r) -> p s r j", r=PACK)[:, :, 2 * a : 2 * a + 2, :]
+        def k_cast_views(a, half):
+            dst = k_bf[0:kp, 2 * a : 2 * a + 2, half * N // 2 : (half + 1) * N // 2].rearrange("p r s j -> p s r j")
+            src = k_raw[half][0:kp].rearrange("p j (s r) -> p s r j", r=PACK)[:, :, 2 * a : 2 * a + 2, :]
             return dst, src
 
         def k_quant(r):
@@ -97,54 +85,92 @@ def tile_rows_a_silu_kb_mask_cap_kernel(tc, qT, kT, t, v, kb, mask, out):
                 in_=src.rearrange("p j (c i) -> p c j i", i=4),
             )
 
-        def q_quant(c0, w):
+        def q_cast(s, c0, w, parts=P):
+            interleave(q_bf[0:parts, s * NQ + c0 : s * NQ + c0 + w, :], q_raw[s % 2][0:parts, :, c0 : c0 + w])
+
+        def q_quant(s, c0, w, parts=P):
+            cols = slice(s * NQ + c0, s * NQ + c0 + w)
             nc.vector.quantize_mx(
-                out=q_codes[:, c0 : c0 + w].bitcast(FP8X4),
-                scales=q_scales[:, c0 : c0 + w],
-                in_=q_bf[:, c0 : c0 + w, :].rearrange("p n j -> p (n j)"),
+                out=q_codes[0:parts, cols].bitcast(FP8X4),
+                scales=q_scales[0:parts, cols],
+                in_=q_bf[0:parts, cols, :].rearrange("p n j -> p (n j)"),
             )
 
-        def mask_times_t():
+        def mask_times_t(half):
             for r in range(PACK):
                 nc.vector.tensor_scalar(
-                    out=mt[:, r, :], in0=mt[:, r, :], scalar1=t_sb[:, r : r + 1], scalar2=None, op0=ALU.mult
+                    out=mt[half][:, r, :], in0=mt[half][:, r, :], scalar1=t_sb[:, r : r + 1], scalar2=None, op0=ALU.mult
                 )
 
-        dst, src = k_cast_views(0)
-        nc.vector.tensor_copy(out=dst, in_=src)
-        dst, src = k_cast_views(1)
-        nc.scalar.copy(out=dst, in_=src)
+        for half in range(2):
+            cols = slice(half * HALF, (half + 1) * HALF)
+            nc.sync.dma_start(out=k_raw[half][rows_of(0)], in_=features(kT[0:1, :, cols]))
+            nc.scalar.dma_start(out=k_raw[half][rows_of(2)], in_=features(kT[1:2, :, cols]))
+        nc.sync.dma_start(out=q_raw[0][rows_of(0), :, 0:N], in_=features(qT[0:1, :, 0:N]))
+        nc.scalar.dma_start(out=q_raw[0][rows_of(2), :, 0:N], in_=features(qT[4:5, :, 0:N]))
+        nc.scalar.dma_start(out=kb_sb[:], in_=kb.rearrange("(p j) o -> p (j o)", j=PACK))
+        nc.sync.dma_start(out=q_raw[0][rows_of(0), :, N:NQ], in_=features(qT[0:1, :, N:NQ]))
+
+        nc.vector.memset(warm[:, 0:1], 0.0)
+        nc.scalar.activation(out=warm[:, 1:2], in_=warm[:, 0:1], func=ACT.Silu)
+        for half in range(2):
+            nc.vector.memset(k_raw[half][rows_of(1)], 0.0)
+        nc.gpsimd.memset(q_raw[0][rows_of(1)], 0.0)
+        nc.vector.memset(k_mx[:, NT : NT + NT // 4], 0)
+
+        nc.scalar.dma_start(out=q_raw[0][rows_of(2), :, N:NQ], in_=features(qT[4:5, :, N:NQ]))
+        nc.sync.dma_start(out=t_sb[:], in_=t.rearrange("(p j) o -> p (j o)", j=PACK))
+        nc.sync.dma_start(out=q_raw[1][rows_of(0, 2)], in_=features(qT[1:3]))
+        for half in range(2):
+            dst, src = k_cast_views(0, half)
+            nc.vector.tensor_copy(out=dst, in_=src)
+            dst, src = k_cast_views(1, half)
+            nc.scalar.copy(out=dst, in_=src)
+            if half == 0:
+                nc.scalar.dma_start(out=q_raw[1][rows_of(2, 2)], in_=features(qT[5:7]))
         nc.scalar.activation(out=kb_half[:], in_=kb_sb[:], func=ACT.Copy, scale=0.5)
-        interleave(q_bf[:, 0:N, :], q_raw[0][:])
+        q_cast(0, 0, N, kp)
         k_quant(0)
         k_quant(1)
-        q_quant(0, N)
-        interleave(q_bf[:, N:HALF, :], q_raw[1][:])
+        q_quant(0, 0, N, kp)
         k_quant(2)
-        q_quant(N, N)
         k_quant(3)
-        nc.sync.dma_start(out=k_mx[ROWS : 2 * ROWS].bitcast(I32), in_=k_mx[0:ROWS].bitcast(I32))
-        nc.sync.dma_start(out=k_mx[3 * ROWS : P].bitcast(I32), in_=k_mx[2 * ROWS : 3 * ROWS].bitcast(I32))
-        nc.sync.dma_start(out=q_raw[3][0 : 2 * ROWS], in_=features(qT[0:2]))
-        nc.sync.dma_start(out=q_raw[3][2 * ROWS : P], in_=features(qT[6:8]))
-        interleave(q_bf[:, HALF:NQ, :], q_raw[2][:])
-        q_quant(HALF, HALF)
-        mask_times_t()
-        for g in range(KV):
-            interleave(v_bf[:, g], v_raw[:, g])
+        nc.sync.dma_start(out=k_mx[rows_of(1)].bitcast(I32), in_=k_mx[rows_of(0)].bitcast(I32))
+        nc.sync.dma_start(out=k_mx[rows_of(3)].bitcast(I32), in_=k_mx[rows_of(2)].bitcast(I32))
+        nc.sync.dma_start(out=mt[0][:], in_=tokens(mask[:, 0:HALF]))
+        nc.sync.dma_start(out=mt[1][:], in_=tokens(mask[:, HALF:NQ]))
+        nc.sync.dma_start(out=v_raw[:], in_=v.rearrange("g (p j) e -> p g j e", j=PACK))
+        q_cast(0, N, N, kp)
+        q_cast(0, 2 * N, N, kp)
+        q_quant(0, N, N, kp)
+        q_cast(0, 3 * N, N, kp)
+        q_quant(0, 2 * N, N, kp)
+        q_quant(0, 3 * N, N, kp)
+        nc.sync.dma_start(out=q_raw[0][rows_of(1)], in_=features(qT[3:4]))
+        nc.sync.dma_start(out=q_raw[0][rows_of(3)], in_=features(qT[7:8]))
+        q_cast(1, 0, HALF)
+        q_cast(1, HALF, HALF)
+        q_quant(1, 0, HALF)
+        q_quant(1, HALF, HALF)
+        mask_times_t(0)
 
-        def v_quant():
+        def v_prepare():
+            for g in range(KV):
+                interleave(v_bf[:, g], v_raw[:, g])
+            mask_times_t(1)
             nc.vector.quantize_mx(
                 out=v_codes[:].bitcast(FP8X4), scales=v_scales[:], in_=v_bf[:].rearrange("p g e j -> p (g e j)")
             )
 
-        def late_q_cast(half):
-            interleave(q_bf[:, NQ + half * HALF : NQ + (half + 1) * HALF, :], q_raw[3][:, :, half * HALF : (half + 1) * HALF])
+        def last_q():
+            q_cast(2, 0, HALF)
+            q_cast(2, HALF, HALF)
+            q_quant(2, 0, HALF)
+            q_quant(2, HALF, HALF)
 
-        after_weights = {0: v_quant, 2: lambda: late_q_cast(0), 4: lambda: late_q_cast(1)}
-        after_quant = {2: lambda: q_quant(NQ, HALF), 4: lambda: q_quant(NQ + HALF, HALF)}
+        after_weights = {1: v_prepare, 3: last_q}
 
-        p0, p1, q0, q1 = (0, 0, 0, HALF), (0, 0, HALF, HALF), (2, 0, 0, HALF), (2, 0, HALF, HALF)
+        p, q, x, y, x2, y2 = [(g, s, 0, NQ) for g, s in ((0, 0), (2, 0), (1, 1), (3, 1), (1, 2), (3, 2))]
         a0, a1, b0, b1 = (0, 1, 0, HALF), (0, 1, HALF, HALF), (2, 1, 0, HALF), (2, 1, HALF, HALF)
 
         def caps(unit, slots, c0=0, w=None):
@@ -154,22 +180,16 @@ def tile_rows_a_silu_kb_mask_cap_kernel(tc, qT, kT, t, v, kb, mask, out):
             return [("silu", unit, c0, w)]
 
         low, high = (0, 1), (2, 3)
-        order = caps(p0, low, 0, N) + caps(q0, low, 0, N) + caps(p0, low, N, N) + caps(q0, low, N, N)
-        order = order + caps(p0, high) + caps(q0, high) + gate(p0)
-        order = order + caps(p1, low) + caps(p1, high) + caps(q1, low) + caps(q1, high)
-        waiting = gate(q0) + gate(p1) + gate(q1)
-        x, y = (1, 0, 0, NQ), (3, 0, 0, NQ)
+        order = caps(p, low, 0, N) + caps(q, low, 0, N) + caps(p, high, 0, N) + caps(q, high, 0, N) + gate(p, 0, N) + gate(q, 0, N)
         for r in range(PACK):
-            order = order + caps(x, (r,)) + caps(y, (r,))
-            if r == PACK - 1:
-                waiting = gate(x) + gate(x, HALF) + gate(y) + gate(y, HALF)
-            order = order + waiting[:1]
-            waiting = waiting[1:]
-        for c0 in (0, HALF):
-            x, y = (1, 1, c0, HALF), (3, 1, c0, HALF)
-            order = order + caps(x, low) + caps(y, low) + waiting[:2] + caps(x, high) + caps(y, high) + waiting[2:] + gate(x)
-            waiting = gate(y)
-        order = order + caps(a0, low) + caps(a0, high) + waiting + caps(a1, low) + gate(a0) + caps(a1, high)
+            order = order + caps(p, (r,), N, NQ - N) + caps(q, (r,), N, NQ - N)
+        waiting = [gate(p, N, N) + gate(q, N, N), gate(p, HALF), gate(q, HALF), gate(x)]
+        for r in range(PACK):
+            order = order + caps(x, (r,)) + caps(y, (r,)) + waiting[r]
+        order = order + caps(x2, (0,))
+        order = order + gate(x, HALF) + caps(y2, (0,)) + caps(x2, (1,)) + gate(y) + caps(y2, (1,)) + caps(x2, (2,)) + gate(y, HALF)
+        order = order + caps(y2, (2,)) + caps(x2, (3,)) + caps(a0, low)[:1] + gate(x2) + caps(a0, low)[1:] + caps(y2, (3,)) + gate(x2, HALF)
+        order = order + caps(a0, high) + gate(y2) + caps(a1, low) + gate(y2, HALF) + caps(a1, high) + gate(a0)
         order = order + caps(b0, low) + gate(a1) + caps(b0, high)
         closing = caps(b1, low) + caps(b1, high)
         order = order + closing[:1] + gate(b0) + closing[1:] + gate(b1, 0, N) + gate(b1, N, N)
@@ -186,23 +206,26 @@ def tile_rows_a_silu_kb_mask_cap_kernel(tc, qT, kT, t, v, kb, mask, out):
                     uses[g] += 1
                 last_use[fill] = n
 
-        capped, gated, w_bf, w_codes, w_scales = {}, {}, {}, {}, {}
+        capped, gated, w_bf, w_codes, w_scales, quantised = {}, {}, {}, {}, {}, []
 
-        def scores(fill):
+        def score_calls(fill):
             unit, slots, c0, w = fill
             g, s = unit[0], unit[1]
             bank = score_banks[g][bank_of[fill][1]]
             rows = slice(g * ROWS, (g + 1) * ROWS)
             first = s * NQ + unit[2] + c0
-            for e, r in enumerate(slots):
-                for c in range(0, w, N):
-                    cols = slice(first + c, first + c + N)
+            return [(bank[:, e * w + c : e * w + c + N], rows, r, first + c) for e, r in enumerate(slots) for c in range(0, w, N)]
+
+        def scores(*together):
+            lists = [score_calls(fill) for fill in together]
+            for i in range(max(len(calls) for calls in lists)):
+                for dst, rows, r, col in [calls[i] for calls in lists if i < len(calls)]:
                     nc.tensor.matmul_mx(
-                        out=bank[:, e * w + c : e * w + c + N],
+                        out=dst,
                         lhsT=k_codes[rows, r * N : (r + 1) * N].bitcast(FP8X4),
                         lhsT_scale=k_scales[rows, r * N : (r + 1) * N],
-                        rhs=q_codes[rows, cols].bitcast(FP8X4),
-                        rhs_scale=q_scales[rows, cols],
+                        rhs=q_codes[rows, col : col + N].bitcast(FP8X4),
+                        rhs_scale=q_scales[rows, col : col + N],
                         start=True,
                         stop=True,
                     )
@@ -226,31 +249,32 @@ def tile_rows_a_silu_kb_mask_cap_kernel(tc, qT, kT, t, v, kb, mask, out):
 
         def silu(n):
             unit, c0, w = pieces[n]
-            gated[n] = work.tile([P, PACK, w], F32, name="gated", bufs=4)
-            nc.scalar.activation(out=gated[n][:], in_=capped[unit][:, :, c0 : c0 + w], func=ACT.Silu, scale=2.0)
+            gated[n] = capped[unit][:, :, c0 : c0 + w]
+            nc.scalar.activation(out=gated[n], in_=gated[n], func=ACT.Silu, scale=2.0)
 
         def weights(n):
             unit, c0, w = pieces[n]
             first = unit[2] + c0
-            w_bf[n] = work.tile([P, w, PACK], BF16, name="w_bf", align_bytes=64)
+            w_bf[n] = keep.tile([P, w, PACK], BF16, name="w_bf%d" % n, align_bytes=64)
             nc.vector.tensor_tensor(
                 out=w_bf[n][:].rearrange("p (c i) r -> p c r i", i=4),
-                in0=gated[n][:].rearrange("p r (c i) -> p c r i", i=4),
-                in1=mt[:, :, first : first + w].rearrange("p r (c i) -> p c r i", i=4),
+                in0=gated[n].rearrange("p r (c i) -> p c r i", i=4),
+                in1=mt[first // HALF][:, :, first % HALF : first % HALF + w].rearrange("p r (c i) -> p c r i", i=4),
                 op=ALU.mult,
             )
 
         def w_quant(n):
             w = pieces[n][2]
-            w_codes[n] = work.tile([P, w], U32, name="w_codes", align_bytes=64, bufs=4)
-            w_scales[n] = work.tile([P, w], U8, name="w_scales", align_bytes=64, bufs=4)
+            quantised.append(n)
+            w_codes[n] = keep.tile([P, w], U32, name="w_codes%d" % n, align_bytes=64)
+            w_scales[n] = keep.tile([P, w], U8, name="w_scales%d" % n, align_bytes=64)
             nc.vector.quantize_mx(
                 out=w_codes[n][:].bitcast(FP8X4),
                 scales=w_scales[n][:],
                 in_=w_bf[n][:].rearrange("p n j -> p (n j)"),
             )
 
-        groups = [(n, n + 1) for n in range(0, last - 3, 2)] + [(n,) for n in range(last - 2, last + 1)]
+        groups = [(0, 1, 2, 3)] + [(n, n + 1) for n in range(4, last - 4, 2)] + [(last - 4,), (last - 3, last - 2), (last - 1,), (last,)]
         place = {}
         for i, group in enumerate(groups):
             tile0 = 0
@@ -260,7 +284,7 @@ def tile_rows_a_silu_kb_mask_cap_kernel(tc, qT, kT, t, v, kb, mask, out):
 
         def second_product(n):
             unit, c0, w = pieces[n]
-            head = HEADS[unit[1]][unit[0]]
+            head = HEADS[unit[0:2]]
             e_cols = slice(head // 4 * D, (head // 4 + 1) * D)
             i, tile0 = place[n]
             for c in range(w // N):
@@ -274,58 +298,72 @@ def tile_rows_a_silu_kb_mask_cap_kernel(tc, qT, kT, t, v, kb, mask, out):
                     stop=True,
                 )
 
-        def store(i, on_scalar):
+        def store(i, on_scalar, queue=nc.sync):
             tiles = sum(pieces[n][2] // N for n in groups[i])
             y = y_banks[i % 2]
-            res = work.tile([P, tiles, D], F32, name="res", bufs=4)
+            res = keep.tile([P, tiles, D], F32, name="res%d" % i)
             if on_scalar:
                 nc.scalar.activation(out=res[:], in_=y[:, 0:tiles, :], func=ACT.Copy, scale=1.0 / 16.0)
             else:
                 nc.vector.tensor_scalar(out=res[:], in0=y[:, 0:tiles, :], scalar1=1.0 / 16.0, scalar2=None, op0=ALU.mult)
+            runs = []
             for n in groups[i]:
                 unit, c0, w = pieces[n]
-                first = unit[2] + c0
-                tile0 = place[n][1]
-                nc.sync.dma_start(
-                    out=out[HEADS[unit[1]][unit[0]], first : first + w, :].rearrange("(c p) e -> p c e", p=P),
-                    in_=res[:, tile0 : tile0 + w // N, :],
+                head, first = HEADS[unit[0:2]], unit[2] + c0
+                if runs and runs[-1][0] == head:
+                    runs[-1] = (head, runs[-1][1], runs[-1][2] + w, runs[-1][3])
+                else:
+                    runs.append((head, first, w, place[n][1]))
+            for head, first, w, tile0 in runs:
+                queue.dma_start(
+                    out=out[head, first : first + w, :].rearrange("(c p) e -> p c e", p=P), in_=res[:, tile0 : tile0 + w // N, :]
                 )
 
         filled = []
 
         def refill(done):
-            while len(filled) < len(fills):
-                fill = fills[len(filled)]
-                if any(bank_of[f] == bank_of[fill] and last_use[f] > done for f in filled):
-                    break
-                scores(fill)
-                filled.append(fill)
+            def free(i):
+                return i < len(fills) and not any(bank_of[f] == bank_of[fills[i]] and last_use[f] > done for f in filled)
+
+            while free(len(filled)):
+                i = len(filled)
+                both = free(i + 1) and bank_of[fills[i]][0] != bank_of[fills[i + 1]][0]
+                together = fills[i : i + 2] if both else fills[i : i + 1]
+                scores(*together)
+                filled.extend(together)
 
         refill(-1)
+        multiplied = []
         n = 0
         for done, step in enumerate(order):
             if step[0] == "cap":
                 cap(step[1], step[2])
             else:
+                if n == last - 1:
+                    store(len(groups) - 4, True)
                 silu(n)
-                if n >= LAG:
-                    second_product(n - LAG)
+                due = [m for m in quantised if m not in multiplied and n >= FIRST_PRODUCT and (m <= n - LAG or n >= 8)]
+                for m in due:
+                    second_product(m)
+                    multiplied.append(m)
+                if n == last - 1:
+                    w_quant(n - 1)
                 weights(n)
+                if n - 1 not in quantised and 1 <= n < last - 1:
+                    w_quant(n - 1)
                 if n in after_weights:
                     after_weights[n]()
-                if n >= LAG and n < last - 1 and groups[place[n - LAG][0]][-1] == n - LAG:
-                    store(place[n - LAG][0], False)
-                if n < last - 1:
+                for m in due:
+                    if n < last - 2 and groups[place[m][0]][-1] == m:
+                        store(place[m][0], False)
+                if n == last - 3:
                     w_quant(n)
-                if n in after_quant:
-                    after_quant[n]()
                 n += 1
             refill(done)
         w_quant(last - 1)
         w_quant(last)
-        store(len(groups) - 4, True)
-        second_product(last - 1)
         store(len(groups) - 3, True)
+        second_product(last - 1)
         second_product(last)
-        store(len(groups) - 2, True)
+        store(len(groups) - 2, True, nc.scalar)
         store(len(groups) - 1, False)

@@ -20,10 +20,11 @@ ROWS = 32
 N = 128
 HALF = 256
 
-HEADS = {(0, 0): 0, (0, 1): 1, (1, 1): 2, (1, 2): 3, (2, 0): 4, (2, 1): 5, (3, 1): 6, (3, 2): 7}
-BANKS = (2, 1, 2, 1)
+HEADS = {(0, 0): 2, (1, 0): 3, (2, 0): 4, (3, 0): 5, (0, 1): 0, (1, 1): 1, (2, 1): 6, (3, 1): 7}
+BANKS = (1, 2, 2, 1)
 LAG = 3
-FIRST_PRODUCT = 6
+Q_LOADS = ((0, N), (N, N), (HALF, HALF), (NQ, HALF), (NQ + HALF, HALF))
+CAUGHT_UP = 5
 
 
 def tile_rows_a_silu_kb_mask_cap_kernel(tc, qT, kT, t, v, kb, mask, out):
@@ -33,15 +34,15 @@ def tile_rows_a_silu_kb_mask_cap_kernel(tc, qT, kT, t, v, kb, mask, out):
         psum = ctx.enter_context(tc.psum_pool(name="psum", bufs=1))
         ctx.enter_context(tc.manual_schedule())
 
-        k_raw = [keep.tile([P, PACK, HALF], F32, name="k_raw%d" % i) for i in range(2)]
+        k_raw = keep.tile([P, PACK, NT], F32, name="k_raw")
         k_bf = keep.tile([P, PACK, N, PACK], BF16, name="k_bf", align_bytes=64)
         k_mx = keep.tile([P, NT + NT // 4], U32, name="k_mx", align_bytes=64)
         k_codes = k_mx[:, 0:NT]
         k_scales = k_mx[:, NT : NT + NT // 4].bitcast(U8)
-        q_raw = [keep.tile([P, PACK, NQ], F32, name="q_raw%d" % i) for i in range(2)]
-        q_bf = keep.tile([P, 3 * NQ, PACK], BF16, name="q_bf", align_bytes=64)
-        q_codes = keep.tile([P, 3 * NQ], U32, name="q_codes", align_bytes=64)
-        q_scales = keep.tile([P, 3 * NQ], U8, name="q_scales", align_bytes=64)
+        q_raw = {c0: keep.tile([P, PACK, w], F32, name="q_raw%d" % c0) for c0, w in Q_LOADS}
+        q_bf = keep.tile([P, 2 * NQ, PACK], BF16, name="q_bf", align_bytes=64)
+        q_codes = keep.tile([P, 2 * NQ], U32, name="q_codes", align_bytes=64)
+        q_scales = keep.tile([P, 2 * NQ], U8, name="q_scales", align_bytes=64)
         v_raw = keep.tile([P, KV, PACK, D], F32, name="v_raw")
         v_bf = keep.tile([P, KV, D, PACK], BF16, name="v_bf", align_bytes=64)
         v_codes = keep.tile([P, KV * D], U32, name="v_codes", align_bytes=64)
@@ -67,9 +68,9 @@ def tile_rows_a_silu_kb_mask_cap_kernel(tc, qT, kT, t, v, kb, mask, out):
 
         kp = 3 * ROWS
 
-        def k_cast_views(a, half):
-            dst = k_bf[0:kp, 2 * a : 2 * a + 2, half * N // 2 : (half + 1) * N // 2].rearrange("p r s j -> p s r j")
-            src = k_raw[half][0:kp].rearrange("p j (s r) -> p s r j", r=PACK)[:, :, 2 * a : 2 * a + 2, :]
+        def k_cast_views(a):
+            dst = k_bf[0:kp, 2 * a : 2 * a + 2].rearrange("p r s j -> p s r j")
+            src = k_raw[0:kp].rearrange("p j (s r) -> p s r j", r=PACK)[:, :, 2 * a : 2 * a + 2, :]
             return dst, src
 
         def k_quant(r):
@@ -85,15 +86,16 @@ def tile_rows_a_silu_kb_mask_cap_kernel(tc, qT, kT, t, v, kb, mask, out):
                 in_=src.rearrange("p j (c i) -> p c j i", i=4),
             )
 
-        def q_cast(s, c0, w, parts=P):
-            interleave(q_bf[0:parts, s * NQ + c0 : s * NQ + c0 + w, :], q_raw[s % 2][0:parts, :, c0 : c0 + w])
+        def q_cast(c0):
+            raw = q_raw[c0]
+            interleave(q_bf[:, c0 : c0 + raw.shape[2], :], raw[:])
 
-        def q_quant(s, c0, w, parts=P):
-            cols = slice(s * NQ + c0, s * NQ + c0 + w)
+        def q_quant(c0):
+            cols = slice(c0, c0 + q_raw[c0].shape[2])
             nc.vector.quantize_mx(
-                out=q_codes[0:parts, cols].bitcast(FP8X4),
-                scales=q_scales[0:parts, cols],
-                in_=q_bf[0:parts, cols, :].rearrange("p n j -> p (n j)"),
+                out=q_codes[:, cols].bitcast(FP8X4),
+                scales=q_scales[:, cols],
+                in_=q_bf[:, cols, :].rearrange("p n j -> p (n j)"),
             )
 
         def mask_times_t(half):
@@ -102,76 +104,64 @@ def tile_rows_a_silu_kb_mask_cap_kernel(tc, qT, kT, t, v, kb, mask, out):
                     out=mt[half][:, r, :], in0=mt[half][:, r, :], scalar1=t_sb[:, r : r + 1], scalar2=None, op0=ALU.mult
                 )
 
-        for half in range(2):
-            cols = slice(half * HALF, (half + 1) * HALF)
-            nc.sync.dma_start(out=k_raw[half][rows_of(0)], in_=features(kT[0:1, :, cols]))
-            nc.scalar.dma_start(out=k_raw[half][rows_of(2)], in_=features(kT[1:2, :, cols]))
-        nc.sync.dma_start(out=q_raw[0][rows_of(0), :, 0:N], in_=features(qT[0:1, :, 0:N]))
-        nc.scalar.dma_start(out=q_raw[0][rows_of(2), :, 0:N], in_=features(qT[4:5, :, 0:N]))
+        nc.sync.dma_start(out=k_raw[rows_of(1, 2)], in_=features(kT))
         nc.scalar.dma_start(out=kb_sb[:], in_=kb.rearrange("(p j) o -> p (j o)", j=PACK))
-        nc.sync.dma_start(out=q_raw[0][rows_of(0), :, N:NQ], in_=features(qT[0:1, :, N:NQ]))
+        nc.scalar.dma_start(out=t_sb[:], in_=t.rearrange("(p j) o -> p (j o)", j=PACK))
+        for c0, w in Q_LOADS[0:3]:
+            nc.sync.dma_start(out=q_raw[c0][:], in_=features(qT[2:6, :, c0 : c0 + w]))
+        nc.sync.dma_start(out=mt[0][:], in_=tokens(mask[:, 0:HALF]))
 
         nc.vector.memset(warm[:, 0:1], 0.0)
         nc.scalar.activation(out=warm[:, 1:2], in_=warm[:, 0:1], func=ACT.Silu)
-        for half in range(2):
-            nc.vector.memset(k_raw[half][rows_of(1)], 0.0)
-        nc.gpsimd.memset(q_raw[0][rows_of(1)], 0.0)
         nc.vector.memset(k_mx[:, NT : NT + NT // 4], 0)
+        nc.vector.memset(k_raw[rows_of(0)], 0.0)
 
-        nc.scalar.dma_start(out=q_raw[0][rows_of(2), :, N:NQ], in_=features(qT[4:5, :, N:NQ]))
-        nc.sync.dma_start(out=t_sb[:], in_=t.rearrange("(p j) o -> p (j o)", j=PACK))
-        nc.sync.dma_start(out=q_raw[1][rows_of(0, 2)], in_=features(qT[1:3]))
-        for half in range(2):
-            dst, src = k_cast_views(0, half)
-            nc.vector.tensor_copy(out=dst, in_=src)
-            dst, src = k_cast_views(1, half)
-            nc.scalar.copy(out=dst, in_=src)
-            if half == 0:
-                nc.scalar.dma_start(out=q_raw[1][rows_of(2, 2)], in_=features(qT[5:7]))
+        dst, src = k_cast_views(0)
+        nc.vector.tensor_copy(out=dst, in_=src)
+        dst, src = k_cast_views(1)
+        nc.scalar.copy(out=dst, in_=src)
         nc.scalar.activation(out=kb_half[:], in_=kb_sb[:], func=ACT.Copy, scale=0.5)
-        q_cast(0, 0, N, kp)
+        q_cast(0)
         k_quant(0)
         k_quant(1)
-        q_quant(0, 0, N, kp)
+        q_quant(0)
+        q_cast(N)
         k_quant(2)
+        q_quant(N)
         k_quant(3)
-        nc.sync.dma_start(out=k_mx[rows_of(1)].bitcast(I32), in_=k_mx[rows_of(0)].bitcast(I32))
+        nc.sync.dma_start(out=k_mx[rows_of(0)].bitcast(I32), in_=k_mx[rows_of(1)].bitcast(I32))
         nc.sync.dma_start(out=k_mx[rows_of(3)].bitcast(I32), in_=k_mx[rows_of(2)].bitcast(I32))
-        nc.sync.dma_start(out=mt[0][:], in_=tokens(mask[:, 0:HALF]))
         nc.sync.dma_start(out=mt[1][:], in_=tokens(mask[:, HALF:NQ]))
         nc.sync.dma_start(out=v_raw[:], in_=v.rearrange("g (p j) e -> p g j e", j=PACK))
-        q_cast(0, N, N, kp)
-        q_cast(0, 2 * N, N, kp)
-        q_quant(0, N, N, kp)
-        q_cast(0, 3 * N, N, kp)
-        q_quant(0, 2 * N, N, kp)
-        q_quant(0, 3 * N, N, kp)
-        nc.sync.dma_start(out=q_raw[0][rows_of(1)], in_=features(qT[3:4]))
-        nc.sync.dma_start(out=q_raw[0][rows_of(3)], in_=features(qT[7:8]))
-        q_cast(1, 0, HALF)
-        q_cast(1, HALF, HALF)
-        q_quant(1, 0, HALF)
-        q_quant(1, HALF, HALF)
+        for c0, w in Q_LOADS[3:]:
+            cols = slice(c0 - NQ, c0 - NQ + w)
+            nc.sync.dma_start(out=q_raw[c0][rows_of(0, 2)], in_=features(qT[0:2, :, cols]))
+            nc.sync.dma_start(out=q_raw[c0][rows_of(2, 2)], in_=features(qT[6:8, :, cols]))
+        q_cast(HALF)
+        q_quant(HALF)
         mask_times_t(0)
 
         def v_prepare():
+            mask_times_t(1)
             for g in range(KV):
                 interleave(v_bf[:, g], v_raw[:, g])
-            mask_times_t(1)
+
+        def v_quant_and_q():
+            q_cast(NQ)
             nc.vector.quantize_mx(
                 out=v_codes[:].bitcast(FP8X4), scales=v_scales[:], in_=v_bf[:].rearrange("p g e j -> p (g e j)")
             )
+            q_quant(NQ)
 
         def last_q():
-            q_cast(2, 0, HALF)
-            q_cast(2, HALF, HALF)
-            q_quant(2, 0, HALF)
-            q_quant(2, HALF, HALF)
+            q_cast(NQ + HALF)
+            q_quant(NQ + HALF)
 
-        after_weights = {1: v_prepare, 3: last_q}
+        after_weights = {0: v_prepare, 1: v_quant_and_q, 2: last_q}
 
-        p, q, x, y, x2, y2 = [(g, s, 0, NQ) for g, s in ((0, 0), (2, 0), (1, 1), (3, 1), (1, 2), (3, 2))]
-        a0, a1, b0, b1 = (0, 1, 0, HALF), (0, 1, HALF, HALF), (2, 1, 0, HALF), (2, 1, HALF, HALF)
+        x, y, x2, y2 = [(g, s, 0, NQ) for g, s in ((0, 0), (3, 0), (0, 1), (3, 1))]
+        p0, p1, q0, q1 = (1, 0, 0, HALF), (1, 0, HALF, HALF), (2, 0, 0, HALF), (2, 0, HALF, HALF)
+        a0, a1, b0, b1 = (1, 1, 0, HALF), (1, 1, HALF, HALF), (2, 1, 0, HALF), (2, 1, HALF, HALF)
 
         def caps(unit, slots, c0=0, w=None):
             return [("cap", (unit, slots, c0, w or unit[3]), r) for r in slots]
@@ -180,10 +170,10 @@ def tile_rows_a_silu_kb_mask_cap_kernel(tc, qT, kT, t, v, kb, mask, out):
             return [("silu", unit, c0, w)]
 
         low, high = (0, 1), (2, 3)
-        order = caps(p, low, 0, N) + caps(q, low, 0, N) + caps(p, high, 0, N) + caps(q, high, 0, N) + gate(p, 0, N) + gate(q, 0, N)
-        for r in range(PACK):
-            order = order + caps(p, (r,), N, NQ - N) + caps(q, (r,), N, NQ - N)
-        waiting = [gate(p, N, N) + gate(q, N, N), gate(p, HALF), gate(q, HALF), gate(x)]
+        order = caps(p0, low, 0, N) + caps(q0, low, 0, N) + caps(p0, low, N, N) + caps(q0, low, N, N)
+        order = order + caps(p0, high) + caps(q0, high) + gate(p0)
+        order = order + caps(p1, low) + caps(q1, low) + caps(p1, high) + caps(q1, high)
+        waiting = [gate(q0), gate(p1), gate(q1), gate(x)]
         for r in range(PACK):
             order = order + caps(x, (r,)) + caps(y, (r,)) + waiting[r]
         order = order + caps(x2, (0,))
@@ -274,7 +264,7 @@ def tile_rows_a_silu_kb_mask_cap_kernel(tc, qT, kT, t, v, kb, mask, out):
                 in_=w_bf[n][:].rearrange("p n j -> p (n j)"),
             )
 
-        groups = [(0, 1, 2, 3)] + [(n, n + 1) for n in range(4, last - 4, 2)] + [(last - 4,), (last - 3, last - 2), (last - 1,), (last,)]
+        groups = [(n, n + 1) for n in range(0, last - 4, 2)] + [(last - 4,), (last - 3, last - 2), (last - 1,), (last,)]
         place = {}
         for i, group in enumerate(groups):
             tile0 = 0
@@ -342,22 +332,20 @@ def tile_rows_a_silu_kb_mask_cap_kernel(tc, qT, kT, t, v, kb, mask, out):
                 if n == last - 1:
                     store(len(groups) - 4, True)
                 silu(n)
-                due = [m for m in quantised if m not in multiplied and n >= FIRST_PRODUCT and (m <= n - LAG or n >= 8)]
+                due = [m for m in quantised if m not in multiplied and (m <= n - LAG or n >= CAUGHT_UP)]
                 for m in due:
                     second_product(m)
                     multiplied.append(m)
                 if n == last - 1:
                     w_quant(n - 1)
                 weights(n)
-                if n - 1 not in quantised and 1 <= n < last - 1:
+                if 1 <= n < last - 1:
                     w_quant(n - 1)
                 if n in after_weights:
                     after_weights[n]()
                 for m in due:
                     if n < last - 2 and groups[place[m][0]][-1] == m:
                         store(place[m][0], False)
-                if n == last - 3:
-                    w_quant(n)
                 n += 1
             refill(done)
         w_quant(last - 1)

@@ -31,6 +31,7 @@ def tile_rows_a_silu_kb_mask_cap_kernel(tc, qT, kT, t, v, kb, mask, out):
     nc = tc.nc
     with ExitStack() as ctx:
         keep = ctx.enter_context(tc.tile_pool(name="keep", bufs=1))
+        work = ctx.enter_context(tc.tile_pool(name="work", bufs=4))
         psum = ctx.enter_context(tc.psum_pool(name="psum", bufs=1))
         ctx.enter_context(tc.manual_schedule())
 
@@ -48,9 +49,10 @@ def tile_rows_a_silu_kb_mask_cap_kernel(tc, qT, kT, t, v, kb, mask, out):
         v_codes = keep.tile([P, KV * D], U32, name="v_codes", align_bytes=64)
         v_scales = keep.tile([P, KV * D], U8, name="v_scales", align_bytes=64)
         mt = [keep.tile([P, PACK, HALF], F32, name="mt%d" % i) for i in range(2)]
-        kb_sb = keep.tile([P, PACK], F32, name="kb_sb")
+        rows_in = keep.tile([P, 2 * N], F32, name="rows_in")
+        rows_dealt = keep.tile([P, 2 * N], F32, name="rows_dealt", align_bytes=64)
+        per_token = keep.tile([P, 2 * N], F32, name="per_token", align_bytes=64)
         kb_half = keep.tile([P, PACK], F32, name="kb_half")
-        t_sb = keep.tile([P, PACK], F32, name="t_sb")
         warm = keep.tile([P, 2], F32, name="warm")
         score_banks = [
             [psum.tile([P, NQ], F32, name="sc%d_%d" % (g, b)) for b in range(BANKS[g])] for g in range(4)
@@ -72,6 +74,10 @@ def tile_rows_a_silu_kb_mask_cap_kernel(tc, qT, kT, t, v, kb, mask, out):
             dst = k_bf[0:kp, 2 * a : 2 * a + 2].rearrange("p r s j -> p s r j")
             src = k_raw[0:kp].rearrange("p j (s r) -> p s r j", r=PACK)[:, :, 2 * a : 2 * a + 2, :]
             return dst, src
+
+        def deal_views(a):
+            cols = slice(a * N, (a + 1) * N)
+            return rows_dealt[:, cols].rearrange("p (r i) -> p r i", r=PACK), rows_in[:, cols].rearrange("p (i r) -> p r i", r=PACK)
 
         def k_quant(r):
             nc.vector.quantize_mx(
@@ -101,14 +107,15 @@ def tile_rows_a_silu_kb_mask_cap_kernel(tc, qT, kT, t, v, kb, mask, out):
         def mask_times_t(half):
             for r in range(PACK):
                 nc.vector.tensor_scalar(
-                    out=mt[half][:, r, :], in0=mt[half][:, r, :], scalar1=t_sb[:, r : r + 1], scalar2=None, op0=ALU.mult
+                    out=mt[half][:, r, :], in0=mt[half][:, r, :], scalar1=per_token[:, N + r * ROWS : N + r * ROWS + 1], scalar2=None, op0=ALU.mult
                 )
 
         nc.sync.dma_start(out=k_raw[rows_of(1, 2)], in_=features(kT))
-        nc.scalar.dma_start(out=kb_sb[:], in_=kb.rearrange("(p j) o -> p (j o)", j=PACK))
-        nc.scalar.dma_start(out=t_sb[:], in_=t.rearrange("(p j) o -> p (j o)", j=PACK))
+        nc.vector.memset(rows_in[:], 0.0)
+        nc.sync.dma_start(out=rows_in[0:P:ROWS, 0:N], in_=kb.rearrange("(g n) o -> g (n o)", n=N))
         for c0, w in Q_LOADS[0:3]:
             nc.sync.dma_start(out=q_raw[c0][:], in_=features(qT[2:6, :, c0 : c0 + w]))
+        nc.sync.dma_start(out=rows_in[0:P:ROWS, N : 2 * N], in_=t.rearrange("(g n) o -> g (n o)", n=N))
         nc.sync.dma_start(out=mt[0][:], in_=tokens(mask[:, 0:HALF]))
 
         nc.vector.memset(warm[:, 0:1], 0.0)
@@ -118,13 +125,16 @@ def tile_rows_a_silu_kb_mask_cap_kernel(tc, qT, kT, t, v, kb, mask, out):
 
         dst, src = k_cast_views(0)
         nc.vector.tensor_copy(out=dst, in_=src)
+        dst, src = deal_views(0)
+        nc.scalar.copy(out=dst, in_=src)
         dst, src = k_cast_views(1)
         nc.scalar.copy(out=dst, in_=src)
-        nc.scalar.activation(out=kb_half[:], in_=kb_sb[:], func=ACT.Copy, scale=0.5)
+        nc.vector.transpose(out=per_token[:, 0:N], in_=rows_dealt[:, 0:N])
         q_cast(0)
         k_quant(0)
         k_quant(1)
         q_quant(0)
+        nc.vector.tensor_scalar(out=kb_half[:], in0=per_token[:, 0:N:ROWS], scalar1=0.5, scalar2=None, op0=ALU.mult)
         q_cast(N)
         k_quant(2)
         q_quant(N)
@@ -138,7 +148,10 @@ def tile_rows_a_silu_kb_mask_cap_kernel(tc, qT, kT, t, v, kb, mask, out):
             nc.sync.dma_start(out=q_raw[c0][rows_of(0, 2)], in_=features(qT[0:2, :, cols]))
             nc.sync.dma_start(out=q_raw[c0][rows_of(2, 2)], in_=features(qT[6:8, :, cols]))
         q_cast(HALF)
+        dst, src = deal_views(1)
+        nc.vector.tensor_copy(out=dst, in_=src)
         q_quant(HALF)
+        nc.vector.transpose(out=per_token[:, N : 2 * N], in_=rows_dealt[:, N : 2 * N])
         mask_times_t(0)
 
         def v_prepare():
@@ -239,16 +252,16 @@ def tile_rows_a_silu_kb_mask_cap_kernel(tc, qT, kT, t, v, kb, mask, out):
 
         def silu(n):
             unit, c0, w = pieces[n]
-            gated[n] = capped[unit][:, :, c0 : c0 + w]
-            nc.scalar.activation(out=gated[n], in_=gated[n], func=ACT.Silu, scale=2.0)
+            gated[n] = keep.tile([P, PACK, w], F32, name="gated%d" % n)
+            nc.scalar.activation(out=gated[n][:], in_=capped[unit][:, :, c0 : c0 + w], func=ACT.Silu, scale=2.0)
 
         def weights(n):
             unit, c0, w = pieces[n]
             first = unit[2] + c0
-            w_bf[n] = keep.tile([P, w, PACK], BF16, name="w_bf%d" % n, align_bytes=64)
+            w_bf[n] = work.tile([P, w, PACK], BF16, name="w_bf", align_bytes=64)
             nc.vector.tensor_tensor(
                 out=w_bf[n][:].rearrange("p (c i) r -> p c r i", i=4),
-                in0=gated[n].rearrange("p r (c i) -> p c r i", i=4),
+                in0=gated[n][:].rearrange("p r (c i) -> p c r i", i=4),
                 in1=mt[first // HALF][:, :, first % HALF : first % HALF + w].rearrange("p r (c i) -> p c r i", i=4),
                 op=ALU.mult,
             )

@@ -23,8 +23,8 @@ HALF = 256
 HEADS = {(0, 0): 2, (1, 0): 3, (2, 0): 4, (3, 0): 5, (0, 1): 0, (1, 1): 1, (2, 1): 6, (3, 1): 7}
 BANKS = (1, 2, 2, 1)
 LAG = 3
-Q_LOADS = ((0, N), (N, N), (HALF, HALF), (NQ, HALF), (NQ + HALF, HALF))
-CAUGHT_UP = 5
+Q_LOADS = ((0, N), (N, N), (HALF, HALF), (NQ, NQ))
+CAUGHT_UP = 11
 
 
 def tile_rows_a_silu_kb_mask_cap_kernel(tc, qT, kT, t, v, kb, mask, out):
@@ -48,12 +48,12 @@ def tile_rows_a_silu_kb_mask_cap_kernel(tc, qT, kT, t, v, kb, mask, out):
         v_bf = keep.tile([P, KV, D, PACK], BF16, name="v_bf", align_bytes=64)
         v_codes = keep.tile([P, KV * D], U32, name="v_codes", align_bytes=64)
         v_scales = keep.tile([P, KV * D], U8, name="v_scales", align_bytes=64)
-        mt = [keep.tile([P, PACK, HALF], F32, name="mt%d" % i) for i in range(2)]
+        mt = keep.tile([P, PACK, NQ], F32, name="mt")
         rows_in = keep.tile([P, 2 * N], F32, name="rows_in")
         rows_dealt = keep.tile([P, 2 * N], F32, name="rows_dealt", align_bytes=64)
         per_token = keep.tile([P, 2 * N], F32, name="per_token", align_bytes=64)
         kb_half = keep.tile([P, PACK], F32, name="kb_half")
-        warm = keep.tile([P, 2], F32, name="warm")
+        zero = keep.tile([P, 1], F32, name="zero")
         score_banks = [
             [psum.tile([P, NQ], F32, name="sc%d_%d" % (g, b)) for b in range(BANKS[g])] for g in range(4)
         ]
@@ -104,22 +104,22 @@ def tile_rows_a_silu_kb_mask_cap_kernel(tc, qT, kT, t, v, kb, mask, out):
                 in_=q_bf[:, cols, :].rearrange("p n j -> p (n j)"),
             )
 
-        def mask_times_t(half):
+        def mask_times_t():
             for r in range(PACK):
                 nc.vector.tensor_scalar(
-                    out=mt[half][:, r, :], in0=mt[half][:, r, :], scalar1=per_token[:, N + r * ROWS : N + r * ROWS + 1], scalar2=None, op0=ALU.mult
+                    out=mt[:, r, :], in0=mt[:, r, :], scalar1=per_token[:, N + r * ROWS : N + r * ROWS + 1], scalar2=None, op0=ALU.mult
                 )
 
         nc.sync.dma_start(out=k_raw[rows_of(1, 2)], in_=features(kT))
-        nc.vector.memset(rows_in[:], 0.0)
+        nc.vector.memset(rows_in[:, 0:N], 0.0)
+        nc.vector.memset(zero[:], 0.0)
+        nc.scalar.activation(out=rows_in[:, N : 2 * N], in_=zero[:].to_broadcast([P, N]), func=ACT.Silu)
         nc.sync.dma_start(out=rows_in[0:P:ROWS, 0:N], in_=kb.rearrange("(g n) o -> g (n o)", n=N))
         for c0, w in Q_LOADS[0:3]:
             nc.sync.dma_start(out=q_raw[c0][:], in_=features(qT[2:6, :, c0 : c0 + w]))
         nc.sync.dma_start(out=rows_in[0:P:ROWS, N : 2 * N], in_=t.rearrange("(g n) o -> g (n o)", n=N))
-        nc.sync.dma_start(out=mt[0][:], in_=tokens(mask[:, 0:HALF]))
+        nc.sync.dma_start(out=mt[:], in_=tokens(mask))
 
-        nc.vector.memset(warm[:, 0:1], 0.0)
-        nc.scalar.activation(out=warm[:, 1:2], in_=warm[:, 0:1], func=ACT.Silu)
         nc.vector.memset(k_mx[:, NT : NT + NT // 4], 0)
         nc.vector.memset(k_raw[rows_of(0)], 0.0)
 
@@ -141,38 +141,30 @@ def tile_rows_a_silu_kb_mask_cap_kernel(tc, qT, kT, t, v, kb, mask, out):
         k_quant(3)
         nc.sync.dma_start(out=k_mx[rows_of(0)].bitcast(I32), in_=k_mx[rows_of(1)].bitcast(I32))
         nc.sync.dma_start(out=k_mx[rows_of(3)].bitcast(I32), in_=k_mx[rows_of(2)].bitcast(I32))
-        nc.sync.dma_start(out=mt[1][:], in_=tokens(mask[:, HALF:NQ]))
         nc.sync.dma_start(out=v_raw[:], in_=v.rearrange("g (p j) e -> p g j e", j=PACK))
-        for c0, w in Q_LOADS[3:]:
-            cols = slice(c0 - NQ, c0 - NQ + w)
-            nc.sync.dma_start(out=q_raw[c0][rows_of(0, 2)], in_=features(qT[0:2, :, cols]))
-            nc.sync.dma_start(out=q_raw[c0][rows_of(2, 2)], in_=features(qT[6:8, :, cols]))
+        nc.sync.dma_start(out=q_raw[NQ][rows_of(0, 2)], in_=features(qT[0:2]))
+        nc.sync.dma_start(out=q_raw[NQ][rows_of(2, 2)], in_=features(qT[6:8]))
         q_cast(HALF)
         dst, src = deal_views(1)
         nc.vector.tensor_copy(out=dst, in_=src)
         q_quant(HALF)
         nc.vector.transpose(out=per_token[:, N : 2 * N], in_=rows_dealt[:, N : 2 * N])
-        mask_times_t(0)
+        mask_times_t()
 
         def v_prepare():
-            mask_times_t(1)
             for g in range(KV):
                 interleave(v_bf[:, g], v_raw[:, g])
 
         def v_quant_and_q():
-            q_cast(NQ)
             nc.vector.quantize_mx(
                 out=v_codes[:].bitcast(FP8X4), scales=v_scales[:], in_=v_bf[:].rearrange("p g e j -> p (g e j)")
             )
+            q_cast(NQ)
             q_quant(NQ)
 
-        def last_q():
-            q_cast(NQ + HALF)
-            q_quant(NQ + HALF)
+        after_weights = {0: v_prepare, 1: v_quant_and_q}
 
-        after_weights = {0: v_prepare, 1: v_quant_and_q, 2: last_q}
-
-        x, y, x2, y2 = [(g, s, 0, NQ) for g, s in ((0, 0), (3, 0), (0, 1), (3, 1))]
+        x, y = (0, 0, 0, NQ), (3, 0, 0, NQ)
         p0, p1, q0, q1 = (1, 0, 0, HALF), (1, 0, HALF, HALF), (2, 0, 0, HALF), (2, 0, HALF, HALF)
         a0, a1, b0, b1 = (1, 1, 0, HALF), (1, 1, HALF, HALF), (2, 1, 0, HALF), (2, 1, HALF, HALF)
 
@@ -185,14 +177,16 @@ def tile_rows_a_silu_kb_mask_cap_kernel(tc, qT, kT, t, v, kb, mask, out):
         low, high = (0, 1), (2, 3)
         order = caps(p0, low, 0, N) + caps(q0, low, 0, N) + caps(p0, low, N, N) + caps(q0, low, N, N)
         order = order + caps(p0, high) + caps(q0, high) + gate(p0)
-        order = order + caps(p1, low) + caps(q1, low) + caps(p1, high) + caps(q1, high)
-        waiting = [gate(q0), gate(p1), gate(q1), gate(x)]
+        order = order + caps(p1, low) + caps(p1, high) + gate(q0)
+        waiting = [caps(q1, low) + caps(q1, high), gate(p1), gate(q1), gate(x)]
         for r in range(PACK):
             order = order + caps(x, (r,)) + caps(y, (r,)) + waiting[r]
-        order = order + caps(x2, (0,))
-        order = order + gate(x, HALF) + caps(y2, (0,)) + caps(x2, (1,)) + gate(y) + caps(y2, (1,)) + caps(x2, (2,)) + gate(y, HALF)
-        order = order + caps(y2, (2,)) + caps(x2, (3,)) + caps(a0, low)[:1] + gate(x2) + caps(a0, low)[1:] + caps(y2, (3,)) + gate(x2, HALF)
-        order = order + caps(a0, high) + gate(y2) + caps(a1, low) + gate(y2, HALF) + caps(a1, high) + gate(a0)
+        waiting = gate(x, HALF) + gate(y) + gate(y, HALF)
+        for c0 in (0, HALF):
+            x2, y2 = (0, 1, c0, HALF), (3, 1, c0, HALF)
+            order = order + caps(x2, low) + caps(y2, low) + waiting[:2] + caps(x2, high) + caps(y2, high) + waiting[2:] + gate(x2)
+            waiting = gate(y2)
+        order = order + caps(a0, low) + caps(a0, high) + waiting + caps(a1, low) + gate(a0) + caps(a1, high)
         order = order + caps(b0, low) + gate(a1) + caps(b0, high)
         closing = caps(b1, low) + caps(b1, high)
         order = order + closing[:1] + gate(b0) + closing[1:] + gate(b1, 0, N) + gate(b1, N, N)
@@ -262,7 +256,7 @@ def tile_rows_a_silu_kb_mask_cap_kernel(tc, qT, kT, t, v, kb, mask, out):
             nc.vector.tensor_tensor(
                 out=w_bf[n][:].rearrange("p (c i) r -> p c r i", i=4),
                 in0=gated[n][:].rearrange("p r (c i) -> p c r i", i=4),
-                in1=mt[first // HALF][:, :, first % HALF : first % HALF + w].rearrange("p r (c i) -> p c r i", i=4),
+                in1=mt[:, :, first : first + w].rearrange("p r (c i) -> p c r i", i=4),
                 op=ALU.mult,
             )
 
@@ -301,7 +295,7 @@ def tile_rows_a_silu_kb_mask_cap_kernel(tc, qT, kT, t, v, kb, mask, out):
                     stop=True,
                 )
 
-        def store(i, on_scalar, queue=nc.sync):
+        def store(i, on_scalar):
             tiles = sum(pieces[n][2] // N for n in groups[i])
             y = y_banks[i % 2]
             res = keep.tile([P, tiles, D], F32, name="res%d" % i)
@@ -318,7 +312,7 @@ def tile_rows_a_silu_kb_mask_cap_kernel(tc, qT, kT, t, v, kb, mask, out):
                 else:
                     runs.append((head, first, w, place[n][1]))
             for head, first, w, tile0 in runs:
-                queue.dma_start(
+                nc.sync.dma_start(
                     out=out[head, first : first + w, :].rearrange("(c p) e -> p c e", p=P), in_=res[:, tile0 : tile0 + w // N, :]
                 )
 
@@ -330,7 +324,7 @@ def tile_rows_a_silu_kb_mask_cap_kernel(tc, qT, kT, t, v, kb, mask, out):
 
             while free(len(filled)):
                 i = len(filled)
-                both = free(i + 1) and bank_of[fills[i]][0] != bank_of[fills[i + 1]][0]
+                both = free(i + 1) and bank_of[fills[i]][0] + bank_of[fills[i + 1]][0] == 3
                 together = fills[i : i + 2] if both else fills[i : i + 1]
                 scores(*together)
                 filled.extend(together)
@@ -366,5 +360,5 @@ def tile_rows_a_silu_kb_mask_cap_kernel(tc, qT, kT, t, v, kb, mask, out):
         store(len(groups) - 3, True)
         second_product(last - 1)
         second_product(last)
-        store(len(groups) - 2, True, nc.scalar)
+        store(len(groups) - 2, True)
         store(len(groups) - 1, False)

@@ -24,7 +24,7 @@ HEADS = {(0, 0): 2, (1, 0): 3, (2, 0): 4, (3, 0): 5, (0, 1): 0, (1, 1): 1, (2, 1
 BANKS = (1, 2, 2, 1)
 LAG = 3
 Q_LOADS = ((0, N), (N, N), (HALF, HALF), (NQ, NQ))
-CAUGHT_UP = 11
+CAUGHT_UP = 7
 
 
 def tile_rows_a_silu_kb_mask_cap_kernel(tc, qT, kT, t, v, kb, mask, out):
@@ -164,7 +164,7 @@ def tile_rows_a_silu_kb_mask_cap_kernel(tc, qT, kT, t, v, kb, mask, out):
 
         after_weights = {0: v_prepare, 1: v_quant_and_q}
 
-        x, y = (0, 0, 0, NQ), (3, 0, 0, NQ)
+        x, y, x2, y2 = [(g, s, 0, NQ) for g, s in ((0, 0), (3, 0), (0, 1), (3, 1))]
         p0, p1, q0, q1 = (1, 0, 0, HALF), (1, 0, HALF, HALF), (2, 0, 0, HALF), (2, 0, HALF, HALF)
         a0, a1, b0, b1 = (1, 1, 0, HALF), (1, 1, HALF, HALF), (2, 1, 0, HALF), (2, 1, HALF, HALF)
 
@@ -181,12 +181,10 @@ def tile_rows_a_silu_kb_mask_cap_kernel(tc, qT, kT, t, v, kb, mask, out):
         waiting = [caps(q1, low) + caps(q1, high), gate(p1), gate(q1), gate(x)]
         for r in range(PACK):
             order = order + caps(x, (r,)) + caps(y, (r,)) + waiting[r]
-        waiting = gate(x, HALF) + gate(y) + gate(y, HALF)
-        for c0 in (0, HALF):
-            x2, y2 = (0, 1, c0, HALF), (3, 1, c0, HALF)
-            order = order + caps(x2, low) + caps(y2, low) + waiting[:2] + caps(x2, high) + caps(y2, high) + waiting[2:] + gate(x2)
-            waiting = gate(y2)
-        order = order + caps(a0, low) + caps(a0, high) + waiting + caps(a1, low) + gate(a0) + caps(a1, high)
+        order = order + caps(x2, (0,))
+        order = order + gate(x, HALF) + caps(y2, (0,)) + caps(x2, (1,)) + gate(y) + caps(y2, (1,)) + caps(x2, (2,)) + gate(y, HALF)
+        order = order + caps(y2, (2,)) + caps(x2, (3,)) + caps(a0, low)[:1] + gate(x2) + caps(a0, low)[1:] + caps(y2, (3,)) + gate(x2, HALF)
+        order = order + caps(a0, high) + gate(y2) + caps(a1, low) + gate(y2, HALF) + caps(a1, high) + gate(a0)
         order = order + caps(b0, low) + gate(a1) + caps(b0, high)
         closing = caps(b1, low) + caps(b1, high)
         order = order + closing[:1] + gate(b0) + closing[1:] + gate(b1, 0, N) + gate(b1, N, N)
@@ -271,7 +269,7 @@ def tile_rows_a_silu_kb_mask_cap_kernel(tc, qT, kT, t, v, kb, mask, out):
                 in_=w_bf[n][:].rearrange("p n j -> p (n j)"),
             )
 
-        groups = [(n, n + 1) for n in range(0, last - 4, 2)] + [(last - 4,), (last - 3, last - 2), (last - 1,), (last,)]
+        groups = [(0,)] + [(n, n + 1) for n in range(1, last - 5, 2)] + [(last - 5,), (last - 4, last - 3), (last - 2,), (last - 1,), (last,)]
         place = {}
         for i, group in enumerate(groups):
             tile0 = 0
@@ -337,9 +335,9 @@ def tile_rows_a_silu_kb_mask_cap_kernel(tc, qT, kT, t, v, kb, mask, out):
                 cap(step[1], step[2])
             else:
                 if n == last - 1:
-                    store(len(groups) - 4, True)
+                    store(len(groups) - 5, True)
                 silu(n)
-                due = [m for m in quantised if m not in multiplied and (m <= n - LAG or n >= CAUGHT_UP)]
+                due = [m for m in quantised if m not in multiplied and m < last - 2 and (m <= n - LAG or n >= CAUGHT_UP)]
                 for m in due:
                     second_product(m)
                     multiplied.append(m)
@@ -351,12 +349,14 @@ def tile_rows_a_silu_kb_mask_cap_kernel(tc, qT, kT, t, v, kb, mask, out):
                 if n in after_weights:
                     after_weights[n]()
                 for m in due:
-                    if n < last - 2 and groups[place[m][0]][-1] == m:
+                    if m < last - 5 and groups[place[m][0]][-1] == m:
                         store(place[m][0], False)
                 n += 1
             refill(done)
         w_quant(last - 1)
         w_quant(last)
+        store(len(groups) - 4, True)
+        second_product(last - 2)
         store(len(groups) - 3, True)
         second_product(last - 1)
         second_product(last)

@@ -17,14 +17,19 @@ ALU = mybir.AluOpType
 P = 128
 PACK = 4
 ROWS = 32
+TILES = 3
 N = 128
 HALF = 256
 
-HEADS = {(0, 0): 2, (1, 0): 3, (2, 0): 4, (3, 0): 5, (0, 1): 0, (1, 1): 1, (2, 1): 6, (3, 1): 7}
-BANKS = (1, 2, 2, 1)
+SETS = ((None, 3, 4), (0, 1, 2), (5, 6, 7))
+OPENING = ((0, N), (N, HALF), (N + HALF, N))
 LAG = 3
-Q_LOADS = ((0, N), (N, N), (HALF, HALF), (NQ, NQ))
-CAUGHT_UP = 7
+TIGHT = 8
+EARLY = 2
+QPLACE = 0
+LAST_SET = 5
+GROUPS = ((0, 1), (2, 3), (4, 5), (6, 7), (8,), (9,), (10,), (11,), (12,), (13,), (14,), (15,), (16, 17), (18,), (19,))
+ON_VECTOR = 11
 
 
 def tile_rows_a_silu_kb_mask_cap_kernel(tc, qT, kT, t, v, kb, mask, out):
@@ -35,28 +40,25 @@ def tile_rows_a_silu_kb_mask_cap_kernel(tc, qT, kT, t, v, kb, mask, out):
         psum = ctx.enter_context(tc.psum_pool(name="psum", bufs=1))
         ctx.enter_context(tc.manual_schedule())
 
+        used = slice(0, TILES * ROWS)
         k_raw = keep.tile([P, PACK, NT], F32, name="k_raw")
         k_bf = keep.tile([P, PACK, N, PACK], BF16, name="k_bf", align_bytes=64)
-        k_mx = keep.tile([P, NT + NT // 4], U32, name="k_mx", align_bytes=64)
-        k_codes = k_mx[:, 0:NT]
-        k_scales = k_mx[:, NT : NT + NT // 4].bitcast(U8)
-        q_raw = {c0: keep.tile([P, PACK, w], F32, name="q_raw%d" % c0) for c0, w in Q_LOADS}
+        k_mx = [keep.tile([P, NT + NT // 4], U32, name="k_mx%d" % a, align_bytes=64) for a in range(2)]
+        q_open = {c0: keep.tile([P, PACK, w], F32, name="q_open%d" % c0) for c0, w in OPENING}
+        q_raw = keep.tile([P, PACK, NQ], F32, name="q_raw")
         q_bf = keep.tile([P, 2 * NQ, PACK], BF16, name="q_bf", align_bytes=64)
-        q_codes = keep.tile([P, 2 * NQ], U32, name="q_codes", align_bytes=64)
-        q_scales = keep.tile([P, 2 * NQ], U8, name="q_scales", align_bytes=64)
+        q_codes = keep.tile([P, 3 * NQ], U32, name="q_codes", align_bytes=64)
+        q_scales = keep.tile([P, 3 * NQ], U8, name="q_scales", align_bytes=64)
         v_raw = keep.tile([P, KV, PACK, D], F32, name="v_raw")
         v_bf = keep.tile([P, KV, D, PACK], BF16, name="v_bf", align_bytes=64)
         v_codes = keep.tile([P, KV * D], U32, name="v_codes", align_bytes=64)
         v_scales = keep.tile([P, KV * D], U8, name="v_scales", align_bytes=64)
         mt = keep.tile([P, PACK, NQ], F32, name="mt")
-        rows_in = keep.tile([P, 2 * N], F32, name="rows_in")
-        rows_dealt = keep.tile([P, 2 * N], F32, name="rows_dealt", align_bytes=64)
-        per_token = keep.tile([P, 2 * N], F32, name="per_token", align_bytes=64)
+        kb_raw = keep.tile([P, PACK], F32, name="kb_raw")
         kb_half = keep.tile([P, PACK], F32, name="kb_half")
+        t_raw = keep.tile([P, PACK], F32, name="t_raw")
         zero = keep.tile([P, 1], F32, name="zero")
-        score_banks = [
-            [psum.tile([P, NQ], F32, name="sc%d_%d" % (g, b)) for b in range(BANKS[g])] for g in range(4)
-        ]
+        score_banks = [[psum.tile([P, NQ], F32, name="sc%d_%d" % (g, b)) for b in range(2)] for g in range(TILES)]
         y_banks = [psum.tile([P, PACK, D], F32, name="y%d" % b) for b in range(2)]
 
         def features(ap):
@@ -65,26 +67,29 @@ def tile_rows_a_silu_kb_mask_cap_kernel(tc, qT, kT, t, v, kb, mask, out):
         def tokens(ap):
             return ap.rearrange("(p j) n -> p j n", j=PACK)
 
+        def per_token(ap):
+            return ap.rearrange("(p j) o -> p (j o)", j=PACK)
+
         def rows_of(g, count=1):
             return slice(g * ROWS, (g + count) * ROWS)
 
-        kp = 3 * ROWS
+        def keys_of(g, head):
+            return k_mx[0 if head // 4 == g // 2 else 1]
 
         def k_cast_views(a):
-            dst = k_bf[0:kp, 2 * a : 2 * a + 2].rearrange("p r s j -> p s r j")
-            src = k_raw[0:kp].rearrange("p j (s r) -> p s r j", r=PACK)[:, :, 2 * a : 2 * a + 2, :]
+            dst = k_bf[used, 2 * a : 2 * a + 2].rearrange("p r s j -> p s r j")
+            src = k_raw[used].rearrange("p j (s r) -> p s r j", r=PACK)[:, :, 2 * a : 2 * a + 2, :]
             return dst, src
-
-        def deal_views(a):
-            cols = slice(a * N, (a + 1) * N)
-            return rows_dealt[:, cols].rearrange("p (r i) -> p r i", r=PACK), rows_in[:, cols].rearrange("p (i r) -> p r i", r=PACK)
 
         def k_quant(r):
             nc.vector.quantize_mx(
-                out=k_codes[0:kp, r * N : (r + 1) * N].bitcast(FP8X4),
-                scales=k_scales[0:kp, r * N : (r + 1) * N],
-                in_=k_bf[0:kp, r].rearrange("p s j -> p (s j)"),
+                out=k_mx[0][used, r * N : (r + 1) * N].bitcast(FP8X4),
+                scales=k_mx[0][used, NT : NT + NT // 4].bitcast(U8)[:, r * N : (r + 1) * N],
+                in_=k_bf[used, r].rearrange("p s j -> p (s j)"),
             )
+
+        def k_copy(g, kv):
+            nc.sync.dma_start(out=keys_of(g, 4 * kv)[rows_of(g)].bitcast(I32), in_=k_mx[0][rows_of(1 + kv)].bitcast(I32))
 
         def interleave(dst, src):
             nc.vector.tensor_copy(
@@ -92,151 +97,148 @@ def tile_rows_a_silu_kb_mask_cap_kernel(tc, qT, kT, t, v, kb, mask, out):
                 in_=src.rearrange("p j (c i) -> p c j i", i=4),
             )
 
-        def q_cast(c0):
-            raw = q_raw[c0]
-            interleave(q_bf[:, c0 : c0 + raw.shape[2], :], raw[:])
-
-        def q_quant(c0):
-            cols = slice(c0, c0 + q_raw[c0].shape[2])
+        def q_quant(bf0, code0, w):
             nc.vector.quantize_mx(
-                out=q_codes[:, cols].bitcast(FP8X4),
-                scales=q_scales[:, cols],
-                in_=q_bf[:, cols, :].rearrange("p n j -> p (n j)"),
+                out=q_codes[used, code0 : code0 + w].bitcast(FP8X4),
+                scales=q_scales[used, code0 : code0 + w],
+                in_=q_bf[used, bf0 : bf0 + w, :].rearrange("p n j -> p (n j)"),
             )
 
-        def mask_times_t():
-            for r in range(PACK):
-                nc.vector.tensor_scalar(
-                    out=mt[:, r, :], in0=mt[:, r, :], scalar1=per_token[:, N + r * ROWS : N + r * ROWS + 1], scalar2=None, op0=ALU.mult
-                )
+        def open_cast(c0):
+            raw = q_open[c0]
+            interleave(q_bf[used, c0 : c0 + raw.shape[2], :], raw[used])
+
+        def set_load(s):
+            heads = SETS[s]
+            nc.sync.dma_start(out=q_raw[rows_of(1, 2)], in_=features(qT[heads[1] : heads[2] + 1]))
+            nc.sync.dma_start(out=q_raw[rows_of(0)], in_=features(qT[heads[0] : heads[0] + 1]))
+
+        def set_cast():
+            interleave(q_bf[used, NQ : 2 * NQ, :], q_raw[used])
 
         nc.sync.dma_start(out=k_raw[rows_of(1, 2)], in_=features(kT))
-        nc.vector.memset(rows_in[:, 0:N], 0.0)
-        nc.vector.memset(zero[:], 0.0)
-        nc.scalar.activation(out=rows_in[:, N : 2 * N], in_=zero[:].to_broadcast([P, N]), func=ACT.Silu)
-        nc.sync.dma_start(out=rows_in[0:P:ROWS, 0:N], in_=kb.rearrange("(g n) o -> g (n o)", n=N))
-        for c0, w in Q_LOADS[0:3]:
-            nc.sync.dma_start(out=q_raw[c0][:], in_=features(qT[2:6, :, c0 : c0 + w]))
-        nc.sync.dma_start(out=rows_in[0:P:ROWS, N : 2 * N], in_=t.rearrange("(g n) o -> g (n o)", n=N))
-        nc.sync.dma_start(out=mt[:], in_=tokens(mask))
+        nc.sync.dma_start(out=q_open[0][rows_of(1, 2)], in_=features(qT[3:5, :, 0:N]))
+        nc.sync.dma_start(out=kb_raw[:], in_=per_token(kb))
+        for c0, w in OPENING[1:]:
+            nc.sync.dma_start(out=q_open[c0][rows_of(1, 2)], in_=features(qT[3:5, :, c0 : c0 + w]))
+        set_load(1)
+        nc.sync.dma_start(out=t_raw[:], in_=per_token(t))
+        for a in range(2):
+            nc.sync.dma_start(out=mt[:, 2 * a : 2 * a + 2, :], in_=tokens(mask)[:, 2 * a : 2 * a + 2, :])
 
-        nc.vector.memset(k_mx[:, NT : NT + NT // 4], 0)
+        nc.vector.memset(zero[:], 0.0)
+        for c0 in (0, N + HALF):
+            nc.scalar.activation(
+                out=q_open[c0][rows_of(0)].rearrange("p j n -> p (j n)"), in_=zero[rows_of(0)].to_broadcast([ROWS, PACK * N]), func=ACT.Silu
+            )
         nc.vector.memset(k_raw[rows_of(0)], 0.0)
+        nc.vector.memset(k_mx[0][:, NT : NT + NT // 4], 0)
+        nc.gpsimd.memset(q_open[N][rows_of(0)], 0.0)
 
         dst, src = k_cast_views(0)
         nc.vector.tensor_copy(out=dst, in_=src)
-        dst, src = deal_views(0)
-        nc.scalar.copy(out=dst, in_=src)
         dst, src = k_cast_views(1)
         nc.scalar.copy(out=dst, in_=src)
-        nc.vector.transpose(out=per_token[:, 0:N], in_=rows_dealt[:, 0:N])
-        q_cast(0)
+        nc.scalar.activation(out=kb_half[:], in_=kb_raw[:], func=ACT.Copy, scale=0.5)
+        open_cast(0)
         k_quant(0)
+        q_quant(0, 0, N)
         k_quant(1)
-        q_quant(0)
-        nc.vector.tensor_scalar(out=kb_half[:], in0=per_token[:, 0:N:ROWS], scalar1=0.5, scalar2=None, op0=ALU.mult)
-        q_cast(N)
         k_quant(2)
-        q_quant(N)
         k_quant(3)
-        nc.sync.dma_start(out=k_mx[rows_of(0)].bitcast(I32), in_=k_mx[rows_of(1)].bitcast(I32))
-        nc.sync.dma_start(out=k_mx[rows_of(3)].bitcast(I32), in_=k_mx[rows_of(2)].bitcast(I32))
+        k_copy(0, 0)
         nc.sync.dma_start(out=v_raw[:], in_=v.rearrange("g (p j) e -> p g j e", j=PACK))
-        nc.sync.dma_start(out=q_raw[NQ][rows_of(0, 2)], in_=features(qT[0:2]))
-        nc.sync.dma_start(out=q_raw[NQ][rows_of(2, 2)], in_=features(qT[6:8]))
-        q_cast(HALF)
-        dst, src = deal_views(1)
-        nc.vector.tensor_copy(out=dst, in_=src)
-        q_quant(HALF)
-        nc.vector.transpose(out=per_token[:, N : 2 * N], in_=rows_dealt[:, N : 2 * N])
-        mask_times_t()
+        k_copy(2, 0)
+        k_copy(0, 1)
+        k_copy(1, 1)
+        open_cast(N)
+        open_cast(N + HALF)
+        for c0 in range(N, NQ, N):
+            q_quant(c0, c0, N)
+        set_cast()
+        set_load(2)
+        for r in range(PACK):
+            nc.vector.tensor_scalar(out=mt[:, r, :], in0=mt[:, r, :], scalar1=t_raw[:, r : r + 1], scalar2=None, op0=ALU.mult)
+            if r == QPLACE:
+                q_quant(NQ, NQ, NQ)
 
-        def v_prepare():
+        def v_cast():
             for g in range(KV):
                 interleave(v_bf[:, g], v_raw[:, g])
 
-        def v_quant_and_q():
+        def v_quant():
             nc.vector.quantize_mx(
                 out=v_codes[:].bitcast(FP8X4), scales=v_scales[:], in_=v_bf[:].rearrange("p g e j -> p (g e j)")
             )
-            q_cast(NQ)
-            q_quant(NQ)
 
-        after_weights = {0: v_prepare, 1: v_quant_and_q}
+        before_weights = {2: v_cast, LAST_SET: set_cast}
+        after_weights = {2: v_quant, LAST_SET: lambda: q_quant(NQ, 2 * NQ, NQ)}
 
-        x, y, x2, y2 = [(g, s, 0, NQ) for g, s in ((0, 0), (3, 0), (0, 1), (3, 1))]
-        p0, p1, q0, q1 = (1, 0, 0, HALF), (1, 0, HALF, HALF), (2, 0, 0, HALF), (2, 0, HALF, HALF)
-        a0, a1, b0, b1 = (1, 1, 0, HALF), (1, 1, HALF, HALF), (2, 1, 0, HALF), (2, 1, HALF, HALF)
+        p0, q0, p, q = (1, 0, 0, N), (2, 0, 0, N), (1, 0, N, NQ - N), (2, 0, N, NQ - N)
+        whole = [(g, s, 0, NQ) for g, s in ((1, 1), (0, 1), (2, 1), (0, 2), (1, 2))]
+        b0, b1, b2 = (2, 2, 0, HALF), (2, 2, HALF, N), (2, 2, HALF + N, N)
 
-        def caps(unit, slots, c0=0, w=None):
-            return [("cap", (unit, slots, c0, w or unit[3]), r) for r in slots]
+        def caps(unit, *slots):
+            return [("cap", (unit, slots), r) for r in slots]
 
         def gate(unit, c0=0, w=HALF):
             return [("silu", unit, c0, w)]
 
-        low, high = (0, 1), (2, 3)
-        order = caps(p0, low, 0, N) + caps(q0, low, 0, N) + caps(p0, low, N, N) + caps(q0, low, N, N)
-        order = order + caps(p0, high) + caps(q0, high) + gate(p0)
-        order = order + caps(p1, low) + caps(p1, high) + gate(q0)
-        waiting = [caps(q1, low) + caps(q1, high), gate(p1), gate(q1), gate(x)]
+        order = caps(p0, 0) + caps(q0, 0) + caps(p0, 1, 2) + caps(q0, 1, 2)[:1] + caps(p0, 3) + caps(q0, 1, 2)[1:] + caps(q0, 3)
+        order = order + gate(p0, 0, N) + gate(q0, 0, N)
         for r in range(PACK):
-            order = order + caps(x, (r,)) + caps(y, (r,)) + waiting[r]
-        order = order + caps(x2, (0,))
-        order = order + gate(x, HALF) + caps(y2, (0,)) + caps(x2, (1,)) + gate(y) + caps(y2, (1,)) + caps(x2, (2,)) + gate(y, HALF)
-        order = order + caps(y2, (2,)) + caps(x2, (3,)) + caps(a0, low)[:1] + gate(x2) + caps(a0, low)[1:] + caps(y2, (3,)) + gate(x2, HALF)
-        order = order + caps(a0, high) + gate(y2) + caps(a1, low) + gate(y2, HALF) + caps(a1, high) + gate(a0)
-        order = order + caps(b0, low) + gate(a1) + caps(b0, high)
-        closing = caps(b1, low) + caps(b1, high)
-        order = order + closing[:1] + gate(b0) + closing[1:] + gate(b1, 0, N) + gate(b1, N, N)
+            order = order + caps(p, r) + caps(q, r)
+        order = order + gate(p) + caps(whole[0], 0) + gate(q)
+        waiting = gate(p, HALF, N) + gate(q, HALF, N)
+        for i, unit in enumerate(whole):
+            ahead = caps(whole[i + 1], 0) if i + 1 < len(whole) else caps(b0, 0, 1)[:1]
+            order = order + caps(unit, 1) + caps(unit, 2) + waiting + caps(unit, 3) + ahead + gate(unit)
+            waiting = gate(unit, HALF)
+        order = order + caps(b0, 0, 1)[1:] + caps(b0, 2, 3)[:1] + waiting + caps(b0, 2, 3)[1:]
+        order = order + caps(b1, 0, 1, 2, 3)[:EARLY] + gate(b0, 0, N) + caps(b1, 0, 1, 2, 3)[EARLY:] + gate(b0, N, N)
+        order = order + caps(b2, 0, 1, 2, 3) + gate(b1, 0, N) + gate(b2, 0, N)
 
         fills, last_use, bank_of = [], {}, {}
-        uses = [0, 0, 0, 0]
+        uses = [0] * TILES
         for n, step in enumerate(order):
             if step[0] == "cap":
                 fill = step[1]
                 g = fill[0][0]
                 if fill not in bank_of:
                     fills.append(fill)
-                    bank_of[fill] = (g, uses[g] % BANKS[g])
+                    bank_of[fill] = (g, uses[g] % 2)
                     uses[g] += 1
                 last_use[fill] = n
 
         capped, gated, w_bf, w_codes, w_scales, quantised = {}, {}, {}, {}, {}, []
 
-        def score_calls(fill):
-            unit, slots, c0, w = fill
-            g, s = unit[0], unit[1]
+        def scores(fill):
+            unit, slots = fill
+            g, s, first, w = unit
             bank = score_banks[g][bank_of[fill][1]]
-            rows = slice(g * ROWS, (g + 1) * ROWS)
-            first = s * NQ + unit[2] + c0
-            return [(bank[:, e * w + c : e * w + c + N], rows, r, first + c) for e, r in enumerate(slots) for c in range(0, w, N)]
-
-        def scores(*together):
-            lists = [score_calls(fill) for fill in together]
-            for i in range(max(len(calls) for calls in lists)):
-                for dst, rows, r, col in [calls[i] for calls in lists if i < len(calls)]:
+            keys = keys_of(g, SETS[s][g])
+            for e, r in enumerate(slots):
+                for c in range(0, w, N):
+                    col = s * NQ + first + c
                     nc.tensor.matmul_mx(
-                        out=dst,
-                        lhsT=k_codes[rows, r * N : (r + 1) * N].bitcast(FP8X4),
-                        lhsT_scale=k_scales[rows, r * N : (r + 1) * N],
-                        rhs=q_codes[rows, col : col + N].bitcast(FP8X4),
-                        rhs_scale=q_scales[rows, col : col + N],
+                        out=bank[:, e * w + c : e * w + c + N],
+                        lhsT=keys[rows_of(g), r * N : (r + 1) * N].bitcast(FP8X4),
+                        lhsT_scale=keys[rows_of(g), NT : NT + NT // 4].bitcast(U8)[:, r * N : (r + 1) * N],
+                        rhs=q_codes[rows_of(g), col : col + N].bitcast(FP8X4),
+                        rhs_scale=q_scales[rows_of(g), col : col + N],
                         start=True,
                         stop=True,
                     )
 
         def cap(fill, r):
-            unit, slots, c0, w = fill
+            unit, slots = fill
+            w = unit[3]
             if unit not in capped:
-                capped[unit] = keep.tile([P, PACK, unit[3]], F32, name="capped%d_%d_%d" % unit[0:3])
+                capped[unit] = keep.tile([P, PACK, w], F32, name="capped%d_%d_%d" % unit[0:3])
             bank = score_banks[unit[0]][bank_of[fill][1]]
             e = slots.index(r)
             nc.scalar.activation(
-                out=capped[unit][:, r, c0 : c0 + w],
-                in_=bank[:, e * w : (e + 1) * w],
-                func=ACT.Tanh,
-                scale=0.5,
-                bias=kb_half[:, r : r + 1],
+                out=capped[unit][:, r, :], in_=bank[:, e * w : (e + 1) * w], func=ACT.Tanh, scale=0.5, bias=kb_half[:, r : r + 1]
             )
 
         pieces = [step[1:] for step in order if step[0] == "silu"]
@@ -269,7 +271,7 @@ def tile_rows_a_silu_kb_mask_cap_kernel(tc, qT, kT, t, v, kb, mask, out):
                 in_=w_bf[n][:].rearrange("p n j -> p (n j)"),
             )
 
-        groups = [(0,)] + [(n, n + 1) for n in range(1, last - 5, 2)] + [(last - 5,), (last - 4, last - 3), (last - 2,), (last - 1,), (last,)]
+        groups = GROUPS
         place = {}
         for i, group in enumerate(groups):
             tile0 = 0
@@ -279,7 +281,7 @@ def tile_rows_a_silu_kb_mask_cap_kernel(tc, qT, kT, t, v, kb, mask, out):
 
         def second_product(n):
             unit, c0, w = pieces[n]
-            head = HEADS[unit[0:2]]
+            head = SETS[unit[1]][unit[0]]
             e_cols = slice(head // 4 * D, (head // 4 + 1) * D)
             i, tile0 = place[n]
             for c in range(w // N):
@@ -304,8 +306,8 @@ def tile_rows_a_silu_kb_mask_cap_kernel(tc, qT, kT, t, v, kb, mask, out):
             runs = []
             for n in groups[i]:
                 unit, c0, w = pieces[n]
-                head, first = HEADS[unit[0:2]], unit[2] + c0
-                if runs and runs[-1][0] == head:
+                head, first = SETS[unit[1]][unit[0]], unit[2] + c0
+                if runs and runs[-1][0] == head and runs[-1][1] + runs[-1][2] == first:
                     runs[-1] = (head, runs[-1][1], runs[-1][2] + w, runs[-1][3])
                 else:
                     runs.append((head, first, w, place[n][1]))
@@ -317,48 +319,44 @@ def tile_rows_a_silu_kb_mask_cap_kernel(tc, qT, kT, t, v, kb, mask, out):
         filled = []
 
         def refill(done):
-            def free(i):
-                return i < len(fills) and not any(bank_of[f] == bank_of[fills[i]] and last_use[f] > done for f in filled)
-
-            while free(len(filled)):
-                i = len(filled)
-                both = free(i + 1) and bank_of[fills[i]][0] + bank_of[fills[i + 1]][0] == 3
-                together = fills[i : i + 2] if both else fills[i : i + 1]
-                scores(*together)
-                filled.extend(together)
+            while len(filled) < len(fills):
+                fill = fills[len(filled)]
+                if any(bank_of[f] == bank_of[fill] and last_use[f] > done for f in filled):
+                    return
+                scores(fill)
+                filled.append(fill)
 
         refill(-1)
-        multiplied = []
+        multiplied, stored = [], []
         n = 0
         for done, step in enumerate(order):
             if step[0] == "cap":
                 cap(step[1], step[2])
             else:
-                if n == last - 1:
-                    store(len(groups) - 5, True)
                 silu(n)
-                due = [m for m in quantised if m not in multiplied and m < last - 2 and (m <= n - LAG or n >= CAUGHT_UP)]
+                due = [m for m in quantised if m not in multiplied and (m <= n - LAG or m >= TIGHT) and n > 2 and place[m][0] < len(stored) + 2]
                 for m in due:
                     second_product(m)
                     multiplied.append(m)
-                if n == last - 1:
-                    w_quant(n - 1)
+                if n in before_weights:
+                    before_weights[n]()
                 weights(n)
-                if 1 <= n < last - 1:
+                if 1 <= n <= TIGHT:
                     w_quant(n - 1)
                 if n in after_weights:
                     after_weights[n]()
-                for m in due:
-                    if m < last - 5 and groups[place[m][0]][-1] == m:
-                        store(place[m][0], False)
+                while len(stored) < ON_VECTOR and groups[len(stored)][-1] in multiplied:
+                    store(len(stored), False)
+                    stored.append(len(stored))
+                if TIGHT <= n < last - 3:
+                    w_quant(n)
+                if n in (last - 2, last):
+                    w_quant(n - 1)
+                    w_quant(n)
                 n += 1
             refill(done)
-        w_quant(last - 1)
-        w_quant(last)
-        store(len(groups) - 4, True)
-        second_product(last - 2)
-        store(len(groups) - 3, True)
-        second_product(last - 1)
-        second_product(last)
-        store(len(groups) - 2, True)
-        store(len(groups) - 1, False)
+        for i in range(len(stored), len(groups)):
+            for m in [m for g in groups[i : i + 2] for m in g if m not in multiplied]:
+                second_product(m)
+                multiplied.append(m)
+            store(i, i < len(groups) - 1)

@@ -23,6 +23,7 @@ HALF = 256
 
 SETS = ((None, 3, 4), (0, 1, 2), (5, 6, 7))
 OPENING = ((0, N), (N, HALF), (N + HALF, N))
+AHEAD = 6
 LAG = 3
 TIGHT = 8
 EARLY = 2
@@ -188,17 +189,20 @@ def tile_rows_a_silu_kb_mask_cap_kernel(tc, qT, kT, t, v, kb, mask, out):
         order = order + gate(p0, 0, N) + gate(q0, 0, N)
         for r in range(PACK):
             order = order + caps(p, r) + caps(q, r)
-        order = order + gate(p) + caps(whole[0], 0) + gate(q)
+        order = order + gate(p) + caps(whole[0], 0) + caps(whole[0], 1) + gate(q)
+        lanes_from = len(order)
         waiting = gate(p, HALF, N) + gate(q, HALF, N)
-        for i, unit in enumerate(whole):
-            ahead = caps(whole[i + 1], 0) if i + 1 < len(whole) else caps(b0, 0, 1)[:1]
-            order = order + caps(unit, 1) + caps(unit, 2) + waiting + caps(unit, 3) + ahead + gate(unit)
+        for unit, ahead in zip(whole, whole[1:]):
+            order = order + caps(ahead, 0) + caps(unit, 2) + waiting + caps(unit, 3) + caps(ahead, 1) + gate(unit)
             waiting = gate(unit, HALF)
+        lanes_to = len(order)
+        order = order + caps(whole[-1], 2) + waiting + caps(whole[-1], 3) + caps(b0, 0, 1)[:1] + gate(whole[-1])
+        waiting = gate(whole[-1], HALF)
         order = order + caps(b0, 0, 1)[1:] + caps(b0, 2, 3)[:1] + waiting + caps(b0, 2, 3)[1:]
         order = order + caps(b1, 0, 1, 2, 3)[:EARLY] + gate(b0, 0, N) + caps(b1, 0, 1, 2, 3)[EARLY:] + gate(b0, N, N)
         order = order + caps(b2, 0, 1, 2, 3) + gate(b1, 0, N) + gate(b2, 0, N)
 
-        fills, last_use, bank_of = [], {}, {}
+        fills, first_use, last_use, bank_of = [], {}, {}, {}
         uses = [0] * TILES
         for n, step in enumerate(order):
             if step[0] == "cap":
@@ -206,29 +210,33 @@ def tile_rows_a_silu_kb_mask_cap_kernel(tc, qT, kT, t, v, kb, mask, out):
                 g = fill[0][0]
                 if fill not in bank_of:
                     fills.append(fill)
+                    first_use[fill] = n
                     bank_of[fill] = (g, uses[g] % 2)
                     uses[g] += 1
                 last_use[fill] = n
 
         capped, gated, w_bf, w_codes, w_scales, quantised = {}, {}, {}, {}, {}, []
 
-        def scores(fill):
+        def score_calls(fill):
             unit, slots = fill
             g, s, first, w = unit
             bank = score_banks[g][bank_of[fill][1]]
-            keys = keys_of(g, SETS[s][g])
-            for e, r in enumerate(slots):
-                for c in range(0, w, N):
-                    col = s * NQ + first + c
-                    nc.tensor.matmul_mx(
-                        out=bank[:, e * w + c : e * w + c + N],
-                        lhsT=keys[rows_of(g), r * N : (r + 1) * N].bitcast(FP8X4),
-                        lhsT_scale=keys[rows_of(g), NT : NT + NT // 4].bitcast(U8)[:, r * N : (r + 1) * N],
-                        rhs=q_codes[rows_of(g), col : col + N].bitcast(FP8X4),
-                        rhs_scale=q_scales[rows_of(g), col : col + N],
-                        start=True,
-                        stop=True,
-                    )
+            return [(bank[:, e * w + c : e * w + c + N], g, s, r, s * NQ + first + c) for e, r in enumerate(slots) for c in range(0, w, N)]
+
+        def scores(together):
+            lanes = [[call for fill in together if fill[0][0] == g for call in score_calls(fill)] for g in range(TILES)]
+            calls = [lane[i] for i in range(max(len(lane) for lane in lanes)) for lane in lanes if i < len(lane)]
+            for dst, g, s, r, col in calls:
+                keys = keys_of(g, SETS[s][g])
+                nc.tensor.matmul_mx(
+                    out=dst,
+                    lhsT=keys[rows_of(g), r * N : (r + 1) * N].bitcast(FP8X4),
+                    lhsT_scale=keys[rows_of(g), NT : NT + NT // 4].bitcast(U8)[:, r * N : (r + 1) * N],
+                    rhs=q_codes[rows_of(g), col : col + N].bitcast(FP8X4),
+                    rhs_scale=q_scales[rows_of(g), col : col + N],
+                    start=True,
+                    stop=True,
+                )
 
         def cap(fill, r):
             unit, slots = fill
@@ -319,12 +327,15 @@ def tile_rows_a_silu_kb_mask_cap_kernel(tc, qT, kT, t, v, kb, mask, out):
         filled = []
 
         def refill(done):
-            while len(filled) < len(fills):
-                fill = fills[len(filled)]
-                if any(bank_of[f] == bank_of[fill] and last_use[f] > done for f in filled):
-                    return
-                scores(fill)
-                filled.append(fill)
+            taken = [bank_of[f] for f in filled if last_use[f] > done]
+            together = []
+            for fill in fills:
+                if fill not in filled and first_use[fill] <= done + AHEAD:
+                    if bank_of[fill] not in taken:
+                        together.append(fill)
+                    taken.append(bank_of[fill])
+            scores(together)
+            filled.extend(together)
 
         refill(-1)
         multiplied, stored = [], []
@@ -354,7 +365,8 @@ def tile_rows_a_silu_kb_mask_cap_kernel(tc, qT, kT, t, v, kb, mask, out):
                     w_quant(n - 1)
                     w_quant(n)
                 n += 1
-            refill(done)
+            if not lanes_from <= done < lanes_to or order[done + 1][0] == "silu" and step[0] == "cap":
+                refill(done)
         for i in range(len(stored), len(groups)):
             for m in [m for g in groups[i : i + 2] for m in g if m not in multiplied]:
                 second_product(m)

@@ -24,13 +24,15 @@ HALF = 256
 SETS = ((None, 3, 4), (0, 1, 2), (5, 6, 7))
 OPENING = ((0, N), (N, HALF), (N + HALF, N))
 AHEAD = 6
-LAG = 3
-TIGHT = 8
+ENDQ = {4: (5,), 3: (4,), 0: (3, 2, 1, 0)}
+WIDE = 2
+LAG = 1
+TIGHT = 4
 EARLY = 2
 QPLACE = 0
-LAST_SET = 5
-GROUPS = ((0, 1), (2, 3), (4, 5), (6, 7), (8,), (9,), (10,), (11,), (12,), (13,), (14,), (15,), (16, 17), (18,), (19,))
-ON_VECTOR = 11
+LAST_SET = 6
+GROUPS = ((0, 1), (2, 3), (4, 5), (6, 7), (8, 9), (10,), (11,), (12,), (13,), (14,), (15,), (16, 17), (18, 19), (20, 21))
+ON_VECTOR = 10
 
 
 def tile_rows_a_silu_kb_mask_cap_kernel(tc, qT, kT, t, v, kb, mask, out):
@@ -78,8 +80,8 @@ def tile_rows_a_silu_kb_mask_cap_kernel(tc, qT, kT, t, v, kb, mask, out):
             return k_mx[0 if head // 4 == g // 2 else 1]
 
         def k_cast_views(a):
-            dst = k_bf[used, 2 * a : 2 * a + 2].rearrange("p r s j -> p s r j")
-            src = k_raw[used].rearrange("p j (s r) -> p s r j", r=PACK)[:, :, 2 * a : 2 * a + 2, :]
+            dst = k_bf[used, 2 * a : 2 * a + 2].rearrange("p r s j -> p s j r")
+            src = k_raw[used].rearrange("p j (s r) -> p s j r", r=PACK)[:, :, :, 2 * a : 2 * a + 2]
             return dst, src
 
         def k_quant(r):
@@ -189,18 +191,20 @@ def tile_rows_a_silu_kb_mask_cap_kernel(tc, qT, kT, t, v, kb, mask, out):
         order = order + gate(p0, 0, N) + gate(q0, 0, N)
         for r in range(PACK):
             order = order + caps(p, r) + caps(q, r)
-        order = order + gate(p) + caps(whole[0], 0) + caps(whole[0], 1) + gate(q)
-        lanes_from = len(order)
-        waiting = gate(p, HALF, N) + gate(q, HALF, N)
+        order = order + gate(p, 0, NQ - N) + caps(whole[0], 0) + caps(whole[0], 1) + gate(q, 0, NQ - N)
+        waiting = []
         for unit, ahead in zip(whole, whole[1:]):
-            order = order + caps(ahead, 0) + caps(unit, 2) + waiting + caps(unit, 3) + caps(ahead, 1) + gate(unit)
-            waiting = gate(unit, HALF)
-        lanes_to = len(order)
+            order = order + caps(ahead, 0) + caps(unit, 2) + waiting + caps(unit, 3) + caps(ahead, 1)
+            if unit in whole[:WIDE]:
+                order, waiting = order + gate(unit, 0, NQ), []
+            else:
+                order, waiting = order + gate(unit), gate(unit, HALF)
         order = order + caps(whole[-1], 2) + waiting + caps(whole[-1], 3) + caps(b0, 0, 1)[:1] + gate(whole[-1])
         waiting = gate(whole[-1], HALF)
         order = order + caps(b0, 0, 1)[1:] + caps(b0, 2, 3)[:1] + waiting + caps(b0, 2, 3)[1:]
         order = order + caps(b1, 0, 1, 2, 3)[:EARLY] + gate(b0, 0, N) + caps(b1, 0, 1, 2, 3)[EARLY:] + gate(b0, N, N)
-        order = order + caps(b2, 0, 1, 2, 3) + gate(b1, 0, N) + gate(b2, 0, N)
+        order = order + caps(b2, 0, 1, 2, 3)[:2] + gate(b1, 0, N // 2) + caps(b2, 0, 1, 2, 3)[2:] + gate(b1, N // 2, N // 2)
+        order = order + gate(b2, 0, N // 2) + gate(b2, N // 2, N // 2)
 
         fills, first_use, last_use, bank_of = [], {}, {}, {}
         uses = [0] * TILES
@@ -249,13 +253,19 @@ def tile_rows_a_silu_kb_mask_cap_kernel(tc, qT, kT, t, v, kb, mask, out):
                 out=capped[unit][:, r, :], in_=bank[:, e * w : (e + 1) * w], func=ACT.Tanh, scale=0.5, bias=kb_half[:, r : r + 1]
             )
 
-        pieces = [step[1:] for step in order if step[0] == "silu"]
+        def split(step):
+            unit, c0, w = step[1:]
+            return [(unit, c0 + c, min(HALF, w - c)) for c in range(0, w, HALF)]
+
+        pieces = [piece for step in order if step[0] == "silu" for piece in split(step)]
         last = len(pieces) - 1
 
-        def silu(n):
-            unit, c0, w = pieces[n]
-            gated[n] = keep.tile([P, PACK, w], F32, name="gated%d" % n)
-            nc.scalar.activation(out=gated[n][:], in_=capped[unit][:, :, c0 : c0 + w], func=ACT.Silu, scale=2.0)
+        def silu(step, n):
+            unit, c0, w = step[1:]
+            result = keep.tile([P, PACK, w], F32, name="gated%d" % n)
+            nc.scalar.activation(out=result[:], in_=capped[unit][:, :, c0 : c0 + w], func=ACT.Silu, scale=2.0)
+            for i, piece in enumerate(split(step)):
+                gated[n + i] = result[:, :, piece[1] - c0 : piece[1] - c0 + piece[2]]
 
         def weights(n):
             unit, c0, w = pieces[n]
@@ -263,19 +273,23 @@ def tile_rows_a_silu_kb_mask_cap_kernel(tc, qT, kT, t, v, kb, mask, out):
             w_bf[n] = work.tile([P, w, PACK], BF16, name="w_bf", align_bytes=64)
             nc.vector.tensor_tensor(
                 out=w_bf[n][:].rearrange("p (c i) r -> p c r i", i=4),
-                in0=gated[n][:].rearrange("p r (c i) -> p c r i", i=4),
+                in0=gated[n].rearrange("p r (c i) -> p c r i", i=4),
                 in1=mt[:, :, first : first + w].rearrange("p r (c i) -> p c r i", i=4),
                 op=ALU.mult,
             )
 
         def w_quant(n):
-            w = pieces[n][2]
+            c0, w = pieces[n][1:]
             quantised.append(n)
-            w_codes[n] = keep.tile([P, w], U32, name="w_codes%d" % n, align_bytes=64)
-            w_scales[n] = keep.tile([P, w], U8, name="w_scales%d" % n, align_bytes=64)
+            if c0 % N:
+                w_codes[n], w_scales[n] = w_codes[n - 1], w_scales[n - 1]
+            else:
+                w_codes[n] = keep.tile([P, max(w, N)], U32, name="w_codes%d" % n, align_bytes=64)
+                w_scales[n] = keep.tile([P, max(w, N)], U8, name="w_scales%d" % n, align_bytes=64)
+            cols = slice(c0 % N, c0 % N + w)
             nc.vector.quantize_mx(
-                out=w_codes[n][:].bitcast(FP8X4),
-                scales=w_scales[n][:],
+                out=w_codes[n][:, cols].bitcast(FP8X4),
+                scales=w_scales[n][:, cols],
                 in_=w_bf[n][:].rearrange("p n j -> p (n j)"),
             )
 
@@ -292,7 +306,7 @@ def tile_rows_a_silu_kb_mask_cap_kernel(tc, qT, kT, t, v, kb, mask, out):
             head = SETS[unit[1]][unit[0]]
             e_cols = slice(head // 4 * D, (head // 4 + 1) * D)
             i, tile0 = place[n]
-            for c in range(w // N):
+            for c in range((c0 % N + w) // N):
                 nc.tensor.matmul_mx(
                     out=y_banks[i % 2][:, tile0 + c, :],
                     lhsT=w_codes[n][:, c * N : (c + 1) * N].bitcast(FP8X4),
@@ -304,7 +318,7 @@ def tile_rows_a_silu_kb_mask_cap_kernel(tc, qT, kT, t, v, kb, mask, out):
                 )
 
         def store(i, on_scalar):
-            tiles = sum(pieces[n][2] // N for n in groups[i])
+            tiles = sum(pieces[n][2] for n in groups[i]) // N
             y = y_banks[i % 2]
             res = keep.tile([P, tiles, D], F32, name="res%d" % i)
             if on_scalar:
@@ -344,29 +358,28 @@ def tile_rows_a_silu_kb_mask_cap_kernel(tc, qT, kT, t, v, kb, mask, out):
             if step[0] == "cap":
                 cap(step[1], step[2])
             else:
-                silu(n)
+                silu(step, n)
                 due = [m for m in quantised if m not in multiplied and (m <= n - LAG or m >= TIGHT) and n > 2 and place[m][0] < len(stored) + 2]
                 for m in due:
                     second_product(m)
                     multiplied.append(m)
-                if n in before_weights:
-                    before_weights[n]()
-                weights(n)
-                if 1 <= n <= TIGHT:
-                    w_quant(n - 1)
-                if n in after_weights:
-                    after_weights[n]()
+                for piece in split(step):
+                    if n in before_weights:
+                        before_weights[n]()
+                    weights(n)
+                    if 1 <= n < last - 4 and n - 1 not in quantised:
+                        w_quant(n - 1)
+                    if n in after_weights:
+                        after_weights[n]()
+                    n += 1
                 while len(stored) < ON_VECTOR and groups[len(stored)][-1] in multiplied:
                     store(len(stored), False)
                     stored.append(len(stored))
-                if TIGHT <= n < last - 3:
-                    w_quant(n)
-                if n in (last - 2, last):
+                if TIGHT < n < last - 4:
                     w_quant(n - 1)
-                    w_quant(n)
-                n += 1
-            if not lanes_from <= done < lanes_to or order[done + 1][0] == "silu" and step[0] == "cap":
-                refill(done)
+                for m in ENDQ.get(last - n + 1, ()):
+                    w_quant(last - m)
+            refill(done)
         for i in range(len(stored), len(groups)):
             for m in [m for g in groups[i : i + 2] for m in g if m not in multiplied]:
                 second_product(m)

@@ -20,19 +20,14 @@ ROWS = 32
 TILES = 3
 N = 128
 HALF = 256
+GROUP = H // KV
 
 SETS = ((None, 3, 4), (0, 1, 2), (5, 6, 7))
 OPENING = ((0, N), (N, HALF), (N + HALF, N))
-AHEAD = 6
-ENDQ = {4: (5,), 3: (4,), 0: (3, 2, 1, 0)}
 WIDE = 2
-LAG = 1
-TIGHT = 4
-EARLY = 2
-QPLACE = 0
-LAST_SET = 6
-GROUPS = ((0, 1), (2, 3), (4, 5), (6, 7), (8, 9), (10,), (11,), (12,), (13,), (14,), (15,), (16, 17), (18, 19), (20, 21))
-ON_VECTOR = 10
+AHEAD = 6
+V_PIECE = 2
+LAST_SET_PIECE = 6
 
 
 def tile_rows_a_silu_kb_mask_cap_kernel(tc, qT, kT, t, v, kb, mask, out):
@@ -76,8 +71,11 @@ def tile_rows_a_silu_kb_mask_cap_kernel(tc, qT, kT, t, v, kb, mask, out):
         def rows_of(g, count=1):
             return slice(g * ROWS, (g + count) * ROWS)
 
-        def keys_of(g, head):
-            return k_mx[0 if head // 4 == g // 2 else 1]
+        def keys_of(g, kv):
+            return k_mx[0 if kv == g // 2 else 1]
+
+        def key_scales(keys, rows, r):
+            return keys[rows, NT : NT + NT // 4].bitcast(U8)[:, r * N : (r + 1) * N]
 
         def k_cast_views(a):
             dst = k_bf[used, 2 * a : 2 * a + 2].rearrange("p r s j -> p s j r")
@@ -87,12 +85,12 @@ def tile_rows_a_silu_kb_mask_cap_kernel(tc, qT, kT, t, v, kb, mask, out):
         def k_quant(r):
             nc.vector.quantize_mx(
                 out=k_mx[0][used, r * N : (r + 1) * N].bitcast(FP8X4),
-                scales=k_mx[0][used, NT : NT + NT // 4].bitcast(U8)[:, r * N : (r + 1) * N],
+                scales=key_scales(k_mx[0], used, r),
                 in_=k_bf[used, r].rearrange("p s j -> p (s j)"),
             )
 
         def k_copy(g, kv):
-            nc.sync.dma_start(out=keys_of(g, 4 * kv)[rows_of(g)].bitcast(I32), in_=k_mx[0][rows_of(1 + kv)].bitcast(I32))
+            nc.sync.dma_start(out=keys_of(g, kv)[rows_of(g)].bitcast(I32), in_=k_mx[0][rows_of(1 + kv)].bitcast(I32))
 
         def interleave(dst, src):
             nc.vector.tensor_copy(
@@ -107,6 +105,10 @@ def tile_rows_a_silu_kb_mask_cap_kernel(tc, qT, kT, t, v, kb, mask, out):
                 in_=q_bf[used, bf0 : bf0 + w, :].rearrange("p n j -> p (n j)"),
             )
 
+        def open_load(c0, w):
+            heads = slice(SETS[0][1], SETS[0][2] + 1)
+            nc.sync.dma_start(out=q_open[c0][rows_of(1, 2)], in_=features(qT[heads, :, c0 : c0 + w]))
+
         def open_cast(c0):
             raw = q_open[c0]
             interleave(q_bf[used, c0 : c0 + raw.shape[2], :], raw[used])
@@ -120,10 +122,10 @@ def tile_rows_a_silu_kb_mask_cap_kernel(tc, qT, kT, t, v, kb, mask, out):
             interleave(q_bf[used, NQ : 2 * NQ, :], q_raw[used])
 
         nc.sync.dma_start(out=k_raw[rows_of(1, 2)], in_=features(kT))
-        nc.sync.dma_start(out=q_open[0][rows_of(1, 2)], in_=features(qT[3:5, :, 0:N]))
+        open_load(*OPENING[0])
         nc.sync.dma_start(out=kb_raw[:], in_=per_token(kb))
         for c0, w in OPENING[1:]:
-            nc.sync.dma_start(out=q_open[c0][rows_of(1, 2)], in_=features(qT[3:5, :, c0 : c0 + w]))
+            open_load(c0, w)
         set_load(1)
         nc.sync.dma_start(out=t_raw[:], in_=per_token(t))
         for a in range(2):
@@ -132,7 +134,9 @@ def tile_rows_a_silu_kb_mask_cap_kernel(tc, qT, kT, t, v, kb, mask, out):
         nc.vector.memset(zero[:], 0.0)
         for c0 in (0, N + HALF):
             nc.scalar.activation(
-                out=q_open[c0][rows_of(0)].rearrange("p j n -> p (j n)"), in_=zero[rows_of(0)].to_broadcast([ROWS, PACK * N]), func=ACT.Silu
+                out=q_open[c0][rows_of(0)].rearrange("p j n -> p (j n)"),
+                in_=zero[rows_of(0)].to_broadcast([ROWS, PACK * N]),
+                func=ACT.Silu,
             )
         nc.vector.memset(k_raw[rows_of(0)], 0.0)
         nc.vector.memset(k_mx[0][:, NT : NT + NT // 4], 0)
@@ -146,23 +150,24 @@ def tile_rows_a_silu_kb_mask_cap_kernel(tc, qT, kT, t, v, kb, mask, out):
         open_cast(0)
         k_quant(0)
         q_quant(0, 0, N)
-        k_quant(1)
-        k_quant(2)
-        k_quant(3)
+        for r in range(1, PACK):
+            k_quant(r)
         k_copy(0, 0)
         nc.sync.dma_start(out=v_raw[:], in_=v.rearrange("g (p j) e -> p g j e", j=PACK))
         k_copy(2, 0)
         k_copy(0, 1)
         k_copy(1, 1)
-        open_cast(N)
-        open_cast(N + HALF)
+        for c0, w in OPENING[1:]:
+            open_cast(c0)
         for c0 in range(N, NQ, N):
             q_quant(c0, c0, N)
         set_cast()
         set_load(2)
         for r in range(PACK):
-            nc.vector.tensor_scalar(out=mt[:, r, :], in0=mt[:, r, :], scalar1=t_raw[:, r : r + 1], scalar2=None, op0=ALU.mult)
-            if r == QPLACE:
+            nc.vector.tensor_scalar(
+                out=mt[:, r, :], in0=mt[:, r, :], scalar1=t_raw[:, r : r + 1], scalar2=None, op0=ALU.mult
+            )
+            if r == 0:
                 q_quant(NQ, NQ, NQ)
 
         def v_cast():
@@ -174,73 +179,115 @@ def tile_rows_a_silu_kb_mask_cap_kernel(tc, qT, kT, t, v, kb, mask, out):
                 out=v_codes[:].bitcast(FP8X4), scales=v_scales[:], in_=v_bf[:].rearrange("p g e j -> p (g e j)")
             )
 
-        before_weights = {2: v_cast, LAST_SET: set_cast}
-        after_weights = {2: v_quant, LAST_SET: lambda: q_quant(NQ, 2 * NQ, NQ)}
+        before_weights = {V_PIECE: v_cast, LAST_SET_PIECE: set_cast}
+        after_weights = {V_PIECE: v_quant, LAST_SET_PIECE: lambda: q_quant(NQ, 2 * NQ, NQ)}
 
-        p0, q0, p, q = (1, 0, 0, N), (2, 0, 0, N), (1, 0, N, NQ - N), (2, 0, N, NQ - N)
+        first_1, first_2 = [(g, 0, 0, N) for g in (1, 2)]
+        rest_1, rest_2 = [(g, 0, N, NQ - N) for g in (1, 2)]
         whole = [(g, s, 0, NQ) for g, s in ((1, 1), (0, 1), (2, 1), (0, 2), (1, 2))]
-        b0, b1, b2 = (2, 2, 0, HALF), (2, 2, HALF, N), (2, 2, HALF + N, N)
+        end_a, end_b, end_c = (2, 2, 0, HALF), (2, 2, HALF, N), (2, 2, HALF + N, N)
 
         def caps(unit, *slots):
             return [("cap", (unit, slots), r) for r in slots]
 
-        def gate(unit, c0=0, w=HALF):
+        def gate(unit, c0, w):
             return [("silu", unit, c0, w)]
 
-        order = caps(p0, 0) + caps(q0, 0) + caps(p0, 1, 2) + caps(q0, 1, 2)[:1] + caps(p0, 3) + caps(q0, 1, 2)[1:] + caps(q0, 3)
-        order = order + gate(p0, 0, N) + gate(q0, 0, N)
+        order = caps(first_1, 0) + caps(first_2, 0) + caps(first_1, 1, 2) + caps(first_2, 1, 2)
+        order = order + caps(first_1, 3) + caps(first_2, 3) + [("silu", None, 0, PACK - 1), ("silu", None, PACK - 1, PACK)]
         for r in range(PACK):
-            order = order + caps(p, r) + caps(q, r)
-        order = order + gate(p, 0, NQ - N) + caps(whole[0], 0) + caps(whole[0], 1) + gate(q, 0, NQ - N)
+            order = order + caps(rest_1, r) + caps(rest_2, r)
+        order = order + gate(rest_1, 0, NQ - N) + caps(whole[0], 0) + caps(whole[0], 1) + gate(rest_2, 0, NQ - N)
         waiting = []
         for unit, ahead in zip(whole, whole[1:]):
             order = order + caps(ahead, 0) + caps(unit, 2) + waiting + caps(unit, 3) + caps(ahead, 1)
             if unit in whole[:WIDE]:
                 order, waiting = order + gate(unit, 0, NQ), []
             else:
-                order, waiting = order + gate(unit), gate(unit, HALF)
-        order = order + caps(whole[-1], 2) + waiting + caps(whole[-1], 3) + caps(b0, 0, 1)[:1] + gate(whole[-1])
-        waiting = gate(whole[-1], HALF)
-        order = order + caps(b0, 0, 1)[1:] + caps(b0, 2, 3)[:1] + waiting + caps(b0, 2, 3)[1:]
-        order = order + caps(b1, 0, 1, 2, 3)[:EARLY] + gate(b0, 0, N) + caps(b1, 0, 1, 2, 3)[EARLY:] + gate(b0, N, N)
-        order = order + caps(b2, 0, 1, 2, 3)[:2] + gate(b1, 0, N // 2) + caps(b2, 0, 1, 2, 3)[2:] + gate(b1, N // 2, N // 2)
-        order = order + gate(b2, 0, N // 2) + gate(b2, N // 2, N // 2)
+                order, waiting = order + gate(unit, 0, HALF), gate(unit, HALF, HALF)
+        tanh_a = caps(end_a, 0, 1) + caps(end_a, 2, 3)
+        tanh_b, tanh_c = caps(end_b, 0, 1, 2, 3), caps(end_c, 0, 1, 2, 3)
+        order = order + caps(whole[-1], 2) + waiting + caps(whole[-1], 3) + tanh_a[:1] + gate(whole[-1], 0, HALF)
+        order = order + tanh_a[1:3] + gate(whole[-1], HALF, HALF) + tanh_a[3:]
+        order = order + tanh_b[:2] + gate(end_a, 0, N) + tanh_b[2:] + gate(end_a, N, N)
+        order = order + tanh_c[:2] + gate(end_b, 0, N // 2) + tanh_c[2:] + gate(end_b, N // 2, N // 2)
+        order = order + gate(end_c, 0, N // 2) + gate(end_c, N // 2, N // 2)
 
         fills, first_use, last_use, bank_of = [], {}, {}, {}
         uses = [0] * TILES
-        for n, step in enumerate(order):
+        for position, step in enumerate(order):
             if step[0] == "cap":
                 fill = step[1]
                 g = fill[0][0]
                 if fill not in bank_of:
                     fills.append(fill)
-                    first_use[fill] = n
+                    first_use[fill] = position
                     bank_of[fill] = (g, uses[g] % 2)
                     uses[g] += 1
-                last_use[fill] = n
+                last_use[fill] = position
 
-        capped, gated, w_bf, w_codes, w_scales, quantised = {}, {}, {}, {}, {}, []
+        def split(step):
+            unit, c0, w = step[1:]
+            if unit is None:
+                return [(first_1, 0, N), (first_2, 0, N)] if w == PACK else []
+            return [(unit, c0 + c, min(HALF, w - c)) for c in range(0, w, HALF)]
+
+        pieces = [piece for step in order if step[0] == "silu" for piece in split(step)]
+        closing = [n for n, piece in enumerate(pieces) if piece[0] in (end_a, end_b, end_c)]
+        halves = [n for n, piece in enumerate(pieces) if piece[0] in whole[WIDE:]]
+        groups = [(n, n + 1) for n in range(0, halves[0], 2)] + [(n,) for n in halves]
+        groups = groups + [(n, n + 1) for n in closing[::2]]
+        on_vector = groups.index((halves[-1],))
+        place = {}
+        for i, group in enumerate(groups):
+            tile0 = 0
+            for n in group:
+                place[n] = (i, tile0)
+                tile0 += pieces[n][2] // N
+
+        capped, gated, w_bf, w_codes, w_scales = {}, {}, {}, {}, {}
+        filled, quantised, multiplied, stored = [], [], [], []
+        first_capped = keep.tile([P, PACK, 2 * N], F32, name="first_capped")
+        first_gated = keep.tile([P, PACK, 2 * N], F32, name="first_gated")
+        for i, unit in enumerate((first_1, first_2)):
+            capped[unit] = first_capped[:, :, i * N : (i + 1) * N]
+            gated[i] = first_gated[:, :, i * N : (i + 1) * N]
 
         def score_calls(fill):
             unit, slots = fill
             g, s, first, w = unit
             bank = score_banks[g][bank_of[fill][1]]
-            return [(bank[:, e * w + c : e * w + c + N], g, s, r, s * NQ + first + c) for e, r in enumerate(slots) for c in range(0, w, N)]
+            return [
+                (bank[:, e * w + c : e * w + c + N], g, s, r, s * NQ + first + c)
+                for e, r in enumerate(slots)
+                for c in range(0, w, N)
+            ]
 
         def scores(together):
             lanes = [[call for fill in together if fill[0][0] == g for call in score_calls(fill)] for g in range(TILES)]
             calls = [lane[i] for i in range(max(len(lane) for lane in lanes)) for lane in lanes if i < len(lane)]
             for dst, g, s, r, col in calls:
-                keys = keys_of(g, SETS[s][g])
+                keys = keys_of(g, SETS[s][g] // GROUP)
                 nc.tensor.matmul_mx(
                     out=dst,
                     lhsT=keys[rows_of(g), r * N : (r + 1) * N].bitcast(FP8X4),
-                    lhsT_scale=keys[rows_of(g), NT : NT + NT // 4].bitcast(U8)[:, r * N : (r + 1) * N],
+                    lhsT_scale=key_scales(keys, rows_of(g), r),
                     rhs=q_codes[rows_of(g), col : col + N].bitcast(FP8X4),
                     rhs_scale=q_scales[rows_of(g), col : col + N],
                     start=True,
                     stop=True,
                 )
+
+        def refill(done):
+            taken = [bank_of[f] for f in filled if last_use[f] > done]
+            together = []
+            for fill in fills:
+                if fill not in filled and first_use[fill] <= done + AHEAD:
+                    if bank_of[fill] not in taken:
+                        together.append(fill)
+                    taken.append(bank_of[fill])
+            scores(together)
+            filled.extend(together)
 
         def cap(fill, r):
             unit, slots = fill
@@ -250,18 +297,18 @@ def tile_rows_a_silu_kb_mask_cap_kernel(tc, qT, kT, t, v, kb, mask, out):
             bank = score_banks[unit[0]][bank_of[fill][1]]
             e = slots.index(r)
             nc.scalar.activation(
-                out=capped[unit][:, r, :], in_=bank[:, e * w : (e + 1) * w], func=ACT.Tanh, scale=0.5, bias=kb_half[:, r : r + 1]
+                out=capped[unit][:, r, :],
+                in_=bank[:, e * w : (e + 1) * w],
+                func=ACT.Tanh,
+                scale=0.5,
+                bias=kb_half[:, r : r + 1],
             )
-
-        def split(step):
-            unit, c0, w = step[1:]
-            return [(unit, c0 + c, min(HALF, w - c)) for c in range(0, w, HALF)]
-
-        pieces = [piece for step in order if step[0] == "silu" for piece in split(step)]
-        last = len(pieces) - 1
 
         def silu(step, n):
             unit, c0, w = step[1:]
+            if unit is None:
+                nc.scalar.activation(out=first_gated[:, c0:w, :], in_=first_capped[:, c0:w, :], func=ACT.Silu, scale=2.0)
+                return
             result = keep.tile([P, PACK, w], F32, name="gated%d" % n)
             nc.scalar.activation(out=result[:], in_=capped[unit][:, :, c0 : c0 + w], func=ACT.Silu, scale=2.0)
             for i, piece in enumerate(split(step)):
@@ -293,19 +340,12 @@ def tile_rows_a_silu_kb_mask_cap_kernel(tc, qT, kT, t, v, kb, mask, out):
                 in_=w_bf[n][:].rearrange("p n j -> p (n j)"),
             )
 
-        groups = GROUPS
-        place = {}
-        for i, group in enumerate(groups):
-            tile0 = 0
-            for n in group:
-                place[n] = (i, tile0)
-                tile0 += pieces[n][2] // N
-
         def second_product(n):
             unit, c0, w = pieces[n]
-            head = SETS[unit[1]][unit[0]]
-            e_cols = slice(head // 4 * D, (head // 4 + 1) * D)
+            kv = SETS[unit[1]][unit[0]] // GROUP
+            e_cols = slice(kv * D, (kv + 1) * D)
             i, tile0 = place[n]
+            multiplied.append(n)
             for c in range((c0 % N + w) // N):
                 nc.tensor.matmul_mx(
                     out=y_banks[i % 2][:, tile0 + c, :],
@@ -321,6 +361,7 @@ def tile_rows_a_silu_kb_mask_cap_kernel(tc, qT, kT, t, v, kb, mask, out):
             tiles = sum(pieces[n][2] for n in groups[i]) // N
             y = y_banks[i % 2]
             res = keep.tile([P, tiles, D], F32, name="res%d" % i)
+            stored.append(i)
             if on_scalar:
                 nc.scalar.activation(out=res[:], in_=y[:, 0:tiles, :], func=ACT.Copy, scale=1.0 / 16.0)
             else:
@@ -329,59 +370,45 @@ def tile_rows_a_silu_kb_mask_cap_kernel(tc, qT, kT, t, v, kb, mask, out):
             for n in groups[i]:
                 unit, c0, w = pieces[n]
                 head, first = SETS[unit[1]][unit[0]], unit[2] + c0
-                if runs and runs[-1][0] == head and runs[-1][1] + runs[-1][2] == first:
+                if runs and runs[-1][0] == head:
                     runs[-1] = (head, runs[-1][1], runs[-1][2] + w, runs[-1][3])
                 else:
                     runs.append((head, first, w, place[n][1]))
             for head, first, w, tile0 in runs:
                 nc.sync.dma_start(
-                    out=out[head, first : first + w, :].rearrange("(c p) e -> p c e", p=P), in_=res[:, tile0 : tile0 + w // N, :]
+                    out=out[head, first : first + w, :].rearrange("(c p) e -> p c e", p=P),
+                    in_=res[:, tile0 : tile0 + w // N, :],
                 )
 
-        filled = []
-
-        def refill(done):
-            taken = [bank_of[f] for f in filled if last_use[f] > done]
-            together = []
-            for fill in fills:
-                if fill not in filled and first_use[fill] <= done + AHEAD:
-                    if bank_of[fill] not in taken:
-                        together.append(fill)
-                    taken.append(bank_of[fill])
-            scores(together)
-            filled.extend(together)
+        late = {closing[1]: closing[0:1], closing[2]: closing[1:2], closing[-1]: closing[2:]}
 
         refill(-1)
-        multiplied, stored = [], []
         n = 0
         for done, step in enumerate(order):
             if step[0] == "cap":
                 cap(step[1], step[2])
             else:
                 silu(step, n)
-                due = [m for m in quantised if m not in multiplied and (m <= n - LAG or m >= TIGHT) and n > 2 and place[m][0] < len(stored) + 2]
-                for m in due:
-                    second_product(m)
-                    multiplied.append(m)
+                for m in list(quantised):
+                    if m not in multiplied and n > V_PIECE and place[m][0] < len(stored) + 2:
+                        second_product(m)
                 for piece in split(step):
                     if n in before_weights:
                         before_weights[n]()
                     weights(n)
-                    if 1 <= n < last - 4 and n - 1 not in quantised:
+                    if 1 <= n <= closing[0] and n - 1 not in quantised:
                         w_quant(n - 1)
                     if n in after_weights:
                         after_weights[n]()
                     n += 1
-                while len(stored) < ON_VECTOR and groups[len(stored)][-1] in multiplied:
+                while len(stored) < on_vector and groups[len(stored)][-1] in multiplied:
                     store(len(stored), False)
-                    stored.append(len(stored))
-                if TIGHT < n < last - 4:
+                if stored and n <= closing[0]:
                     w_quant(n - 1)
-                for m in ENDQ.get(last - n + 1, ()):
-                    w_quant(last - m)
+                for m in late.get(n - 1, ()):
+                    w_quant(m)
             refill(done)
         for i in range(len(stored), len(groups)):
-            for m in [m for g in groups[i : i + 2] for m in g if m not in multiplied]:
+            for m in [m for group in groups[i : i + 2] for m in group if m not in multiplied]:
                 second_product(m)
-                multiplied.append(m)
             store(i, i < len(groups) - 1)

@@ -1,3 +1,4 @@
+import math
 from contextlib import ExitStack
 
 import concourse.mybir as mybir
@@ -28,6 +29,39 @@ WIDE = 2
 AHEAD = 6
 V_PIECE = 2
 LAST_SET_PIECE = 6
+SHIFT = -5.5
+
+
+def tanh_factors():
+    nodes = [math.cos((2 * k + 1) * math.pi / 18) for k in range(9)]
+    zs = [(x - nodes[-1]) / (1 - nodes[-1]) for x in nodes[:-1]]
+    dd = [math.tanh(math.sqrt(z)) / math.sqrt(z) for z in zs]
+    for level in range(1, 8):
+        for i in range(7, level - 1, -1):
+            dd[i] = (dd[i] - dd[i - 1]) / (zs[i] - zs[i - level])
+    coef = [dd[7]]
+    for i in range(6, -1, -1):
+        coef = [a - zs[i] * b for a, b in zip(coef + [0.0], [0.0] + coef)]
+        coef[-1] = coef[-1] + dd[i]
+    lead = coef[0]
+
+    def divide(p, c):
+        p = list(p)
+        for i in range(len(p) - 2):
+            p[i + 1] = p[i + 1] - SHIFT * p[i]
+            p[i + 2] = p[i + 2] - c * p[i]
+        return p[:-2], p[-2], p[-1]
+
+    p, shifts, rests = [a / lead for a in coef], [], []
+    while len(p) > 2:
+        c = 0.0
+        for step in range(60):
+            r1 = divide(p, c)[1]
+            c = c - r1 * 1e-4 / (divide(p, c + 1e-4)[1] - r1)
+        p, r1, r0 = divide(p, c)
+        shifts.append(c)
+        rests.append(r0)
+    return p[1], shifts[::-1], rests[::-1], lead
 
 
 def tile_rows_a_silu_kb_mask_cap_kernel(tc, qT, kT, t, v, kb, mask, out):
@@ -159,20 +193,69 @@ def tile_rows_a_silu_kb_mask_cap_kernel(tc, qT, kT, t, v, kb, mask, out):
         k_copy(1, 1)
         for c0, w in OPENING[1:]:
             open_cast(c0)
-        for c0 in range(N, NQ, N):
-            q_quant(c0, c0, N)
-        set_cast()
-        set_load(2)
-        for r in range(PACK):
+
+        def mask_t(r):
             nc.vector.tensor_scalar(
                 out=mt[:, r, :], in0=mt[:, r, :], scalar1=t_raw[:, r : r + 1], scalar2=None, op0=ALU.mult
             )
-            if r == 0:
-                q_quant(NQ, NQ, NQ)
+
+        def poly_steps(u, p, room):
+            g0, a, g, lead = tanh_factors()
+            z, y, y1, y2, y3, r1, r2 = room
+
+            def fold(dst, src, c, other):
+                return lambda: nc.vector.scalar_tensor_tensor(
+                    out=dst, in0=src, scalar=c, in1=other, op0=ALU.add, op1=ALU.mult
+                )
+
+            def moved(dst, c, f):
+                return lambda: nc.vector.tensor_scalar(out=dst, in0=y, scalar1=c, scalar2=f, op0=ALU.add, op1=ALU.mult)
+
+            return [
+                fold(z, u, 0.0, u),
+                fold(y, z, SHIFT, z),
+                moved(y1, a[0], 1.0),
+                moved(y2, a[1], 1.0),
+                moved(y3, a[2], lead),
+                fold(r1, z, g0, y1),
+                fold(r2, r1, g[0], y2),
+                fold(r1, r2, g[1], y3),
+                fold(r2, r1, g[2] * lead, u),
+                fold(p, r2, 1.0, u),
+            ]
+
+        def after_opening():
+            room = [k_raw[:, e // 2, (e % 2) * HALF : (e % 2 + 1) * HALF] for e in range(7)]
+            steps = poly_steps(first_capped[:, 0, :], first_gated[:, 0, :], room)
+            q_quant(N, N, N)
+            q_quant(2 * N, 2 * N, N)
+            q_quant(3 * N, 3 * N, N)
+            lanes = [
+                poly_steps(first_capped[:, 0, c : c + N], first_gated[:, 0, c : c + N], [x[:, c : c + N] for x in room])
+                for c in (0, N)
+            ]
+            for e in range(7):
+                if e in (2, 3, 4):
+                    steps[e]()
+                else:
+                    lanes[0][e]()
+                    lanes[1][e]()
+            set_cast()
+            set_load(2)
+            steps[7]()
+            q_quant(NQ, NQ, NQ)
+            steps[8]()
+            mask_t(0)
+            steps[9]()
+            mask_t(1)
+            mask_t(2)
+            mask_t(3)
 
         def v_cast():
-            for g in range(KV):
-                interleave(v_bf[:, g], v_raw[:, g])
+            nc.vector.tensor_copy(
+                out=v_bf[:].rearrange("p g (c i) j -> p g c j i", i=4),
+                in_=v_raw[:].rearrange("p g j (c i) -> p g c j i", i=4),
+            )
 
         def v_quant():
             nc.vector.quantize_mx(
@@ -194,7 +277,7 @@ def tile_rows_a_silu_kb_mask_cap_kernel(tc, qT, kT, t, v, kb, mask, out):
             return [("silu", unit, c0, w)]
 
         order = caps(first_1, 0) + caps(first_2, 0) + caps(first_1, 1, 2) + caps(first_2, 1, 2)
-        order = order + caps(first_1, 3) + caps(first_2, 3) + [("silu", None, 0, PACK - 1), ("silu", None, PACK - 1, PACK)]
+        order = order + caps(first_1, 3) + caps(first_2, 3) + [("silu", None, 1, PACK - 1), ("silu", None, PACK - 1, PACK)]
         for r in range(PACK):
             order = order + caps(rest_1, r) + caps(rest_2, r)
         order = order + gate(rest_1, 0, NQ - N) + caps(whole[0], 0) + caps(whole[0], 1) + gate(rest_2, 0, NQ - N)
@@ -387,6 +470,8 @@ def tile_rows_a_silu_kb_mask_cap_kernel(tc, qT, kT, t, v, kb, mask, out):
         for done, step in enumerate(order):
             if step[0] == "cap":
                 cap(step[1], step[2])
+                if done == 1:
+                    after_opening()
             else:
                 silu(step, n)
                 for m in list(quantised):

@@ -27,8 +27,11 @@ SETS = ((None, 3, 4), (0, 1, 2), (5, 6, 7))
 OPENING = ((0, N), (N, HALF), (N + HALF, N))
 WIDE = 2
 AHEAD = 6
-V_PIECE = 2
+V_PIECE = 0
+PATIENT = 0
 LAST_SET_PIECE = 6
+POLY = 320
+LANES = 2
 SHIFT = -5.5
 
 
@@ -162,8 +165,7 @@ def tile_rows_a_silu_kb_mask_cap_kernel(tc, qT, kT, t, v, kb, mask, out):
             open_load(c0, w)
         set_load(1)
         nc.sync.dma_start(out=t_raw[:], in_=per_token(t))
-        for a in range(2):
-            nc.sync.dma_start(out=mt[:, 2 * a : 2 * a + 2, :], in_=tokens(mask)[:, 2 * a : 2 * a + 2, :])
+        nc.sync.dma_start(out=mt[:, 0:2, :], in_=tokens(mask)[:, 0:2, :])
 
         nc.vector.memset(zero[:], 0.0)
         for c0 in (0, N + HALF):
@@ -187,6 +189,7 @@ def tile_rows_a_silu_kb_mask_cap_kernel(tc, qT, kT, t, v, kb, mask, out):
         for r in range(1, PACK):
             k_quant(r)
         k_copy(0, 0)
+        nc.sync.dma_start(out=mt[:, 2:4, :], in_=tokens(mask)[:, 2:4, :])
         nc.sync.dma_start(out=v_raw[:], in_=v.rearrange("g (p j) e -> p g j e", j=PACK))
         k_copy(2, 0)
         k_copy(0, 1)
@@ -225,31 +228,33 @@ def tile_rows_a_silu_kb_mask_cap_kernel(tc, qT, kT, t, v, kb, mask, out):
             ]
 
         def after_opening():
-            room = [k_raw[:, e // 2, (e % 2) * HALF : (e % 2 + 1) * HALF] for e in range(7)]
-            steps = poly_steps(first_capped[:, 0, :], first_gated[:, 0, :], room)
+            u_all = first_capped[:].rearrange("p r n -> p (r n)")
+            p_all = first_gated[:].rearrange("p r n -> p (r n)")
+            room = [k_raw[:, e, 0:POLY] for e in range(PACK)] + [q_open[N][:, 2 * e : 2 * e + 2, :].rearrange("p j n -> p (j n)")[:, 0:POLY] for e in range(2)]
+            room = room + [room[0]]
+            steps = poly_steps(u_all[:, 0:POLY], p_all[:, 0:POLY], room)
+            lane = POLY // LANES
+            lanes = [
+                poly_steps(u_all[:, c : c + lane], p_all[:, c : c + lane], [x[:, c : c + lane] for x in room])
+                for c in range(0, POLY, lane)
+            ]
             q_quant(N, N, N)
             q_quant(2 * N, 2 * N, N)
             q_quant(3 * N, 3 * N, N)
-            lanes = [
-                poly_steps(first_capped[:, 0, c : c + N], first_gated[:, 0, c : c + N], [x[:, c : c + N] for x in room])
-                for c in (0, N)
-            ]
-            for e in range(7):
-                if e in (2, 3, 4):
+            for e in range(5):
+                if e in (3, 4):
                     steps[e]()
                 else:
-                    lanes[0][e]()
-                    lanes[1][e]()
+                    for each in lanes:
+                        each[e]()
             set_cast()
             set_load(2)
-            steps[7]()
-            q_quant(NQ, NQ, NQ)
-            steps[8]()
-            mask_t(0)
-            steps[9]()
-            mask_t(1)
-            mask_t(2)
-            mask_t(3)
+            rest = steps[5:]
+            fill = [lambda: q_quant(NQ, NQ, NQ)] + [lambda r=r: mask_t(r) for r in range(PACK)]
+            for e, other in enumerate(fill):
+                if e < len(rest):
+                    rest[e]()
+                other()
 
         def v_cast():
             nc.vector.tensor_copy(
@@ -276,8 +281,8 @@ def tile_rows_a_silu_kb_mask_cap_kernel(tc, qT, kT, t, v, kb, mask, out):
         def gate(unit, c0, w):
             return [("silu", unit, c0, w)]
 
-        order = caps(first_1, 0) + caps(first_2, 0) + caps(first_1, 1, 2) + caps(first_2, 1, 2)
-        order = order + caps(first_1, 3) + caps(first_2, 3) + [("silu", None, 1, PACK - 1), ("silu", None, PACK - 1, PACK)]
+        order = caps(first_1, 0) + caps(first_2, 0) + caps(first_1, 1, 2)[:1] + caps(first_2, 1, 2)[:1] + caps(first_1, 1, 2)[1:] + caps(first_2, 1, 2)[1:]
+        order = order + caps(first_1, 3) + caps(first_2, 3) + [("silu", None, POLY, 3 * HALF), ("silu", None, 3 * HALF, 4 * HALF)]
         for r in range(PACK):
             order = order + caps(rest_1, r) + caps(rest_2, r)
         order = order + gate(rest_1, 0, NQ - N) + caps(whole[0], 0) + caps(whole[0], 1) + gate(rest_2, 0, NQ - N)
@@ -312,7 +317,7 @@ def tile_rows_a_silu_kb_mask_cap_kernel(tc, qT, kT, t, v, kb, mask, out):
         def split(step):
             unit, c0, w = step[1:]
             if unit is None:
-                return [(first_1, 0, N), (first_2, 0, N)] if w == PACK else []
+                return [(first_1, 0, N), (first_2, 0, N)] if w == 4 * HALF else []
             return [(unit, c0 + c, min(HALF, w - c)) for c in range(0, w, HALF)]
 
         pieces = [piece for step in order if step[0] == "silu" for piece in split(step)]
@@ -390,7 +395,10 @@ def tile_rows_a_silu_kb_mask_cap_kernel(tc, qT, kT, t, v, kb, mask, out):
         def silu(step, n):
             unit, c0, w = step[1:]
             if unit is None:
-                nc.scalar.activation(out=first_gated[:, c0:w, :], in_=first_capped[:, c0:w, :], func=ACT.Silu, scale=2.0)
+                flat = "p r n -> p (r n)"
+                nc.scalar.activation(
+                    out=first_gated[:].rearrange(flat)[:, c0:w], in_=first_capped[:].rearrange(flat)[:, c0:w], func=ACT.Silu, scale=2.0
+                )
                 return
             result = keep.tile([P, PACK, w], F32, name="gated%d" % n)
             nc.scalar.activation(out=result[:], in_=capped[unit][:, :, c0 : c0 + w], func=ACT.Silu, scale=2.0)
@@ -465,17 +473,20 @@ def tile_rows_a_silu_kb_mask_cap_kernel(tc, qT, kT, t, v, kb, mask, out):
 
         late = {closing[1]: closing[0:1], closing[2]: closing[1:2], closing[-1]: closing[2:]}
 
+        ripe = []
         refill(-1)
         n = 0
         for done, step in enumerate(order):
             if step[0] == "cap":
                 cap(step[1], step[2])
-                if done == 1:
+                if done == 3:
                     after_opening()
             else:
                 silu(step, n)
-                for m in list(quantised):
-                    if m not in multiplied and n > V_PIECE and place[m][0] < len(stored) + 2:
+                ready = list(ripe) if n < PATIENT else list(quantised)
+                ripe = list(quantised)
+                for m in ready:
+                    if m not in multiplied and n > 2 and place[m][0] < len(stored) + 2:
                         second_product(m)
                 for piece in split(step):
                     if n in before_weights:

@@ -18,21 +18,19 @@ ALU = mybir.AluOpType
 P = 128
 PACK = 4
 ROWS = 32
-TILES = 3
 N = 128
 HALF = 256
-GROUP = H // KV
-
-SETS = ((None, 3, 4), (0, 1, 2), (5, 6, 7))
-OPENING = ((0, N), (N, HALF), (N + HALF, N))
-WIDE = 2
-AHEAD = 6
-V_PIECE = 0
-PATIENT = 0
-LAST_SET_PIECE = 6
-POLY = 320
-LANES = 2
+BANKS = 3
 SHIFT = -5.5
+POLY = 384
+WIDE = 2
+LATE_AT = 3
+LAST_AT = 5
+HELD = 4
+RES_AT = (4, 5, 7, 8, 11, 12, 15)
+PROMPT = (5, 7, 9, 11, 13)
+Y_AFTER = {1: (0,), 2: (1,), 3: (3,), 4: (4,)}
+Y_BETWEEN = {3: 2}
 
 
 def tanh_factors():
@@ -71,30 +69,47 @@ def tile_rows_a_silu_kb_mask_cap_kernel(tc, qT, kT, t, v, kb, mask, out):
     nc = tc.nc
     with ExitStack() as ctx:
         keep = ctx.enter_context(tc.tile_pool(name="keep", bufs=1))
-        work = ctx.enter_context(tc.tile_pool(name="work", bufs=4))
         psum = ctx.enter_context(tc.psum_pool(name="psum", bufs=1))
         ctx.enter_context(tc.manual_schedule())
 
-        used = slice(0, TILES * ROWS)
+        low = slice(0, 3 * ROWS)
+        both = slice(ROWS, 3 * ROWS)
+        MID = NQ - N
+
+        def rows_of(g):
+            return slice(g * ROWS, (g + 1) * ROWS)
+
+        def mx_tile(name, w):
+            return keep.tile([P, w + w // 4], U32, name=name, align_bytes=64), w
+
+        def words(mx, rows, c0, w):
+            return mx[0][rows, c0 : c0 + w].bitcast(FP8X4)
+
+        def scales(mx, rows, c0, w):
+            return mx[0][rows, mx[1] : mx[1] + mx[1] // 4].bitcast(U8)[:, c0 : c0 + w]
+
         k_raw = keep.tile([P, PACK, NT], F32, name="k_raw")
         k_bf = keep.tile([P, PACK, N, PACK], BF16, name="k_bf", align_bytes=64)
-        k_mx = [keep.tile([P, NT + NT // 4], U32, name="k_mx%d" % a, align_bytes=64) for a in range(2)]
-        q_open = {c0: keep.tile([P, PACK, w], F32, name="q_open%d" % c0) for c0, w in OPENING}
-        q_raw = keep.tile([P, PACK, NQ], F32, name="q_raw")
-        q_bf = keep.tile([P, 2 * NQ, PACK], BF16, name="q_bf", align_bytes=64)
-        q_codes = keep.tile([P, 3 * NQ], U32, name="q_codes", align_bytes=64)
-        q_scales = keep.tile([P, 3 * NQ], U8, name="q_scales", align_bytes=64)
+        k_mx = mx_tile("k_mx", NT)
+        edge_raw = keep.tile([P, PACK, N], F32, name="edge_raw")
+        mid_raw = [keep.tile([P, PACK, w], F32, name="mid_raw%d" % w) for w in (HALF, N)]
+        late_raw = keep.tile([P, PACK, NQ], F32, name="late_raw")
+        q_bf = keep.tile([P, NQ, PACK], BF16, name="q_bf", align_bytes=64)
+        q_mx = {name: mx_tile(name, w) for name, w in (("first", N), ("last", N), ("mid", MID), ("mid_moved", MID), ("late", NQ), ("late_moved", NQ))}
         v_raw = keep.tile([P, KV, PACK, D], F32, name="v_raw")
         v_bf = keep.tile([P, KV, D, PACK], BF16, name="v_bf", align_bytes=64)
-        v_codes = keep.tile([P, KV * D], U32, name="v_codes", align_bytes=64)
-        v_scales = keep.tile([P, KV * D], U8, name="v_scales", align_bytes=64)
+        v_mx = mx_tile("v_mx", KV * D)
         mt = keep.tile([P, PACK, NQ], F32, name="mt")
         kb_raw = keep.tile([P, PACK], F32, name="kb_raw")
         kb_half = keep.tile([P, PACK], F32, name="kb_half")
         t_raw = keep.tile([P, PACK], F32, name="t_raw")
         zero = keep.tile([P, 1], F32, name="zero")
-        score_banks = [[psum.tile([P, NQ], F32, name="sc%d_%d" % (g, b)) for b in range(2)] for g in range(TILES)]
+        w_ring = [keep.tile([P, NQ, PACK], BF16, name="w_bf%d" % i, align_bytes=64) for i in range(4)]
+        score_banks = [[psum.tile([P, NQ], F32, name="sc%d_%d" % (kv, b)) for b in range(BANKS)] for kv in range(KV)]
         y_banks = [psum.tile([P, PACK, D], F32, name="y%d" % b) for b in range(2)]
+        every = slice(0, P)
+
+        sync, scalar, vector, tensor = [], [], [], []
 
         def features(ap):
             return ap.rearrange("h (p j) n -> (h p) j n", j=PACK)
@@ -105,111 +120,291 @@ def tile_rows_a_silu_kb_mask_cap_kernel(tc, qT, kT, t, v, kb, mask, out):
         def per_token(ap):
             return ap.rearrange("(p j) o -> p (j o)", j=PACK)
 
-        def rows_of(g, count=1):
-            return slice(g * ROWS, (g + count) * ROWS)
+        def dma(name, needs, dst, src):
+            return (name, needs, lambda: nc.sync.dma_start(out=dst, in_=src))
 
-        def keys_of(g, kv):
-            return k_mx[0 if kv == g // 2 else 1]
+        def move(name, needs, source, g, target):
+            return dma(name, needs, q_mx[source + "_moved"][0][rows_of(target)].bitcast(I32), q_mx[source][0][rows_of(g)].bitcast(I32))
 
-        def key_scales(keys, rows, r):
-            return keys[rows, NT : NT + NT // 4].bitcast(U8)[:, r * N : (r + 1) * N]
+        def interleave(name, needs, dst, src):
+            return (
+                name,
+                needs,
+                lambda: nc.vector.tensor_copy(
+                    out=dst.rearrange("p (c i) j -> p c j i", i=4), in_=src.rearrange("p j (c i) -> p c j i", i=4)
+                ),
+            )
 
-        def k_cast_views(a):
-            dst = k_bf[used, 2 * a : 2 * a + 2].rearrange("p r s j -> p s j r")
-            src = k_raw[used].rearrange("p j (s r) -> p s j r", r=PACK)[:, :, :, 2 * a : 2 * a + 2]
-            return dst, src
+        def quantise(name, needs, mx, rows, c0, w, src):
+            return (name, needs, lambda: nc.vector.quantize_mx(out=words(mx, rows, c0, w), scales=scales(mx, rows, c0, w), in_=src))
+
+        def q_quant(name, needs, source, rows, c0, w, bf0):
+            return quantise(name, needs, q_mx[source], rows, c0, w, q_bf[rows, bf0 : bf0 + w, :].rearrange("p n j -> p (n j)"))
 
         def k_quant(r):
-            nc.vector.quantize_mx(
-                out=k_mx[0][used, r * N : (r + 1) * N].bitcast(FP8X4),
-                scales=key_scales(k_mx[0], used, r),
-                in_=k_bf[used, r].rearrange("p s j -> p (s j)"),
+            return quantise(("k", r), [("k_cast", r // 2)], k_mx, low, r * N, N, k_bf[low, r].rearrange("p s j -> p (s j)"))
+
+        def k_cast_views(a):
+            dst = k_bf[low, 2 * a : 2 * a + 2].rearrange("p r s j -> p s j r")
+            src = k_raw[low].rearrange("p j (s r) -> p s j r", r=PACK)[:, :, :, 2 * a : 2 * a + 2]
+            return dst, src
+
+        vector.append(("zero", ["first_raw"], lambda: nc.vector.memset(zero[:], 0.0)))
+        scalar.append(
+            (
+                "edge_zero",
+                ["zero"],
+                lambda: nc.scalar.activation(
+                    out=edge_raw[rows_of(0)].rearrange("p j n -> p (j n)"),
+                    in_=zero[rows_of(0)].to_broadcast([ROWS, PACK * N]),
+                    func=ACT.Silu,
+                ),
+            )
+        )
+        vector.append((("k_zero", 0), [], lambda: nc.vector.memset(k_raw[rows_of(0)], 0.0)))
+        for name in ("mid", "late"):
+            vector.append((("plane", name), [], lambda name=name: nc.vector.memset(q_mx[name][0][:, q_mx[name][1] :], 0)))
+
+        def blocks(head, q0, count, source, c0):
+            return tuple((head, q0 + i * N, source, c0 + i * N) for i in range(count))
+
+        near, far = (3, 4), (2, 5)
+        late_near, late_far = (1, 6), (0, 7)
+        first = [(kv, blocks(near[kv], 0, 1, "first", 0)) for kv in range(KV)]
+        second = [(kv, blocks(near[kv], N, 2, "mid", 0)) for kv in range(KV)]
+        whole = [(kv, blocks(far[kv], N, 3, "mid_moved", 0) + blocks(near[kv], 3 * N, 1, "mid", HALF)) for kv in range(KV)]
+        whole = whole + [(kv, blocks(late_near[kv], 0, 4, "late", 0)) for kv in range(KV)]
+        whole = whole + [(0, blocks(late_far[0], 0, 4, "late_moved", 0)), (1, blocks(late_far[1], 0, 3, "late_moved", 0))]
+        last = [(1, blocks(late_far[1], 3 * N, 1, "late_moved", 3 * N) + blocks(far[1], 0, 1, "last", 0)), (0, blocks(far[0], 0, 1, "last", 0))]
+
+        def operand_ready(kv, block):
+            source = block[2]
+            if source == "mid":
+                return ("mid", block[3] // HALF)
+            return (source, kv) if source in ("mid_moved", "late_moved") else source
+
+        sync.append(dma("k_raw", [], k_raw[both], features(kT)))
+        sync.append(dma("first_raw", [], edge_raw[both], features(qT[3:5, :, 0:N])))
+        sync.append(dma("kb_raw", [], kb_raw[:], per_token(kb)))
+        sync.append(dma(("mid_raw", 0), [], mid_raw[0][:], features(qT[2:6, :, N : N + HALF])))
+        sync.append(dma(("mid_raw", 1), [], mid_raw[1][:], features(qT[2:6, :, N + HALF : NQ])))
+        sync.append(dma("t_raw", [], t_raw[:], per_token(t)))
+        sync.append(dma(("mask", 0), [], mt[:, 0:2, :], tokens(mask)[:, 0:2, :]))
+        sync.append(dma(("mask", 1), [], mt[:, 2:4, :], tokens(mask)[:, 2:4, :]))
+        sync.append(move(("mid_moved", 0), [("mid", 1)], "mid", 0, 1))
+        sync.append(move(("mid_moved", 1), [("mid", 1)], "mid", 3, 2))
+        sync.append(dma(("late_raw", 0), [], late_raw[0:64], features(qT[0:2])))
+        sync.append(dma(("late_raw", 1), [], late_raw[64:128], features(qT[6:8])))
+        sync.append(dma("v_raw", [], v_raw[:], v.rearrange("g (p j) e -> p g j e", j=PACK)))
+        for kv in range(KV):
+            head = far[kv]
+            sync.append(dma(("last_raw", kv), ["first_cast"], edge_raw[rows_of(1 + kv)], features(qT[head : head + 1, :, 0:N])))
+        sync.append(move(("late_moved", 0), ["late"], "late", 0, 1))
+        sync.append(move(("late_moved", 1), ["late"], "late", 3, 2))
+
+        dst0, src0 = k_cast_views(0)
+        dst1, src1 = k_cast_views(1)
+        vector.append((("k_cast", 0), ["k_raw"], lambda: nc.vector.tensor_copy(out=dst0, in_=src0)))
+        scalar.append((("k_cast", 1), ["k_raw", ("k_zero", 0)], lambda: nc.scalar.copy(out=dst1, in_=src1)))
+        scalar.append(("kb_half", ["kb_raw"], lambda: nc.scalar.activation(out=kb_half[:], in_=kb_raw[:], func=ACT.Copy, scale=0.5)))
+        vector.append(interleave("first_cast", ["first_raw", "edge_zero"], q_bf[low, 0:N, :], edge_raw[low]))
+        vector.append(k_quant(0))
+        vector.append(q_quant("first", [], "first", low, 0, N, 0))
+        vector.extend(k_quant(r) for r in range(1, PACK))
+        vector.append(interleave(("mid_cast", 0), [("mid_raw", 0)], q_bf[:, N : N + HALF, :], mid_raw[0][:]))
+        vector.append(q_quant(("mid", 0), [], "mid", every, 0, HALF, N))
+        vector.append(interleave(("mid_cast", 1), [("mid_raw", 1)], q_bf[:, N + HALF : NQ, :], mid_raw[1][:]))
+
+        capped, own = {}, {}
+        first_capped = keep.tile([P, PACK, 2 * N], F32, name="first_capped")
+        first_gated = keep.tile([P, PACK, 2 * N], F32, name="first_gated")
+        second_capped = keep.tile([P, PACK, NQ], F32, name="second_capped")
+        second_gated = keep.tile([P, PACK, NQ], F32, name="second_gated")
+        for kv in range(KV):
+            capped[first[kv]] = first_capped[:, :, kv * N : (kv + 1) * N]
+            capped[second[kv]] = second_capped[:, :, kv * HALF : (kv + 1) * HALF]
+        shared = {"first": (first, first_capped, first_gated, ["poly"]), "second": (second, second_capped, second_gated, [])}
+        for i, unit in enumerate(whole + last):
+            tile = keep.tile([P, PACK, N * len(unit[1])], F32, name="capped%d" % i)
+            capped[unit] = tile[:]
+            own[unit] = tile
+
+        def caps(unit, *slots):
+            return [("cap", unit, r) for r in slots]
+
+        def gate(unit, c0, w):
+            return [("silu", unit, c0, w)]
+
+        order = []
+        for r in range(PACK):
+            order = order + caps(first[0], r) + caps(first[1], r)
+        order = order + [("silu", "first", POLY, 3 * HALF), ("silu", "first", 3 * HALF, 4 * HALF)]
+        for r in range(PACK):
+            order = order + caps(second[0], r) + caps(second[1], r)
+        order = order + gate("second", 0, 3 * NQ) + caps(whole[0], 0) + gate("second", 3 * NQ, 4 * NQ) + caps(whole[0], 1, 2, 3)
+        for i in range(1, len(whole)):
+            unit, before = whole[i], whole[i - 1]
+            if i <= WIDE:
+                order = order + caps(unit, 0, 1) + gate(before, 0, NQ) + caps(unit, 2, 3)
+            else:
+                order = order + caps(unit, 0) + gate(before, 0, HALF) + caps(unit, 1) + gate(before, HALF, HALF) + caps(unit, 2, 3)
+        order = order + caps(last[0], 0) + gate(whole[-1], 0, N) + caps(last[0], 1) + gate(whole[-1], N, N) + caps(last[0], 2, 3) + gate(whole[-1], HALF, N)
+        order = order + gate(last[0], 0, N) + caps(last[1], 0, 1) + gate(last[0], N, N // 2) + caps(last[1], 2, 3)
+        order = order + gate(last[0], N + N // 2, N // 2) + gate(last[1], 0, N // 2) + gate(last[1], N // 2, N // 2)
+
+        def fills_of(unit):
+            if unit in first + second:
+                return [(unit, (0,)), (unit, (1, 2)), (unit, (3,))]
+            per_bank = NQ // (N * len(unit[1]))
+            return [(unit, tuple(range(r, r + per_bank))) for r in range(0, PACK, per_bank)]
+
+        bank_of, before_in_bank = {}, {}
+        for kv in range(KV):
+            row = [fill for unit in first + second + whole + last if unit[0] == kv for fill in fills_of(unit)]
+            for i, fill in enumerate(row):
+                bank_of[fill] = score_banks[kv][i % BANKS]
+                before_in_bank[fill] = row[i - BANKS] if i >= BANKS else None
+
+        def passes(fill):
+            (kv, cols), slots = fill
+            rows = rows_of(1 + kv)
+            old = before_in_bank[fill]
+            free = [("cap", old[0], r) for r in old[1]] if old else []
+            result = []
+            for e, r in enumerate(slots):
+                for b, block in enumerate(cols):
+                    c = (e * len(cols) + b) * N
+
+                    def call(dst=bank_of[fill][:, c : c + N], r=r, block=block):
+                        nc.tensor.matmul_mx(
+                            out=dst,
+                            lhsT=words(k_mx, rows, r * N, N),
+                            lhsT_scale=scales(k_mx, rows, r * N, N),
+                            rhs=words(q_mx[block[2]], rows, block[3], N),
+                            rhs_scale=scales(q_mx[block[2]], rows, block[3], N),
+                            start=True,
+                            stop=True,
+                        )
+
+                    result.append((("pass", fill, r, b), free + [("k", r), operand_ready(kv, block)], call))
+            return result
+
+        def side_by_side(a, b):
+            result = []
+            for i in range(max(len(a), len(b))):
+                result = result + a[i : i + 1] + b[i : i + 1]
+            return result
+
+        def cap(unit, r):
+            fill = [f for f in fills_of(unit) if r in f[1]][0]
+            w = N * len(unit[1])
+            e = fill[1].index(r)
+            needs = ["kb_half"] + [("pass", fill, s, b) for s in fill[1] for b in range(len(unit[1]))]
+            return (
+                ("cap", unit, r),
+                needs,
+                lambda: nc.scalar.activation(
+                    out=capped[unit][:, r, :], in_=bank_of[fill][:, e * w : (e + 1) * w], func=ACT.Tanh, scale=0.5, bias=kb_half[:, r : r + 1]
+                ),
             )
 
-        def k_copy(g, kv):
-            nc.sync.dma_start(out=keys_of(g, kv)[rows_of(g)].bitcast(I32), in_=k_mx[0][rows_of(1 + kv)].bitcast(I32))
+        pieces = []
+        flat = "p r n -> p (r n)"
+        for step in order:
+            if step[0] == "cap":
+                scalar.append(cap(step[1], step[2]))
+                continue
+            unit, c0, w = step[1:]
+            if unit in shared:
+                pair, src, dst, also = shared[unit]
+                width = N * len(pair[0][1])
+                if w == 2 * PACK * width:
+                    pieces.extend((pair[kv], 0, width, dst[:, :, kv * width : (kv + 1) * width], [step] + also) for kv in range(KV))
+                dst, src = dst[:].rearrange(flat)[:, c0:w], src[:].rearrange(flat)[:, c0:w]
+            else:
+                result = keep.tile([P, PACK, w], F32, name="gated%d" % len(pieces))
+                dst, src = result[:], capped[unit][:, :, c0 : c0 + w]
+                c = c0
+                while c < c0 + w:
+                    head = unit[1][c // N][0]
+                    width = min(c0 + w, N * max(b + 1 for b, block in enumerate(unit[1]) if block[0] == head)) - c
+                    pieces.append((unit, c, width, result[:, :, c - c0 : c - c0 + width], [step]))
+                    c += width
+            scalar.append((step, [], lambda dst=dst, src=src: nc.scalar.activation(out=dst, in_=src, func=ACT.Silu, scale=2.0)))
 
-        def interleave(dst, src):
-            nc.vector.tensor_copy(
-                out=dst.rearrange("p (c i) j -> p c j i", i=4),
-                in_=src.rearrange("p j (c i) -> p c j i", i=4),
+        w_mx = {}
+        for i, unit in enumerate(first + second + whole + last):
+            w_mx[unit] = mx_tile("w_mx%d" % i, N * len(unit[1]))
+
+        def weights(n):
+            unit, c0, w, gated, needs = pieces[n]
+            q0 = unit[1][c0 // N][1] + c0 % N
+            return (
+                ("weights", n),
+                needs + [("mt", r) for r in range(PACK)],
+                lambda: nc.vector.tensor_tensor(
+                    out=w_ring[n % 4][:, 0:w, :].rearrange("p (c i) r -> p c r i", i=4),
+                    in0=gated.rearrange("p r (c i) -> p c r i", i=4),
+                    in1=mt[:, :, q0 : q0 + w].rearrange("p r (c i) -> p c r i", i=4),
+                    op=ALU.mult,
+                ),
             )
 
-        def q_quant(bf0, code0, w):
-            nc.vector.quantize_mx(
-                out=q_codes[used, code0 : code0 + w].bitcast(FP8X4),
-                scales=q_scales[used, code0 : code0 + w],
-                in_=q_bf[used, bf0 : bf0 + w, :].rearrange("p n j -> p (n j)"),
-            )
+        def w_quant(n):
+            unit, c0, w = pieces[n][0:3]
+            return quantise(("w", n), [], w_mx[unit], every, c0, w, w_ring[n % 4][:, 0:w, :].rearrange("p n j -> p (n j)"))
 
-        def open_load(c0, w):
-            heads = slice(SETS[0][1], SETS[0][2] + 1)
-            nc.sync.dma_start(out=q_open[c0][rows_of(1, 2)], in_=features(qT[heads, :, c0 : c0 + w]))
+        groups = [[(unit, 0, 1) for unit in first], [(unit, 0, 2) for unit in second]] + [[(unit, 0, len(unit[1]))] for unit in whole]
+        groups = groups + [[(last[0], 0, 1)], [(last[0], 1, 1)], [(last[1], 0, 1)]]
 
-        def open_cast(c0):
-            raw = q_open[c0]
-            interleave(q_bf[used, c0 : c0 + raw.shape[2], :], raw[used])
+        def products(i):
+            free = [("res", i - 2)] if i >= 2 else []
+            result = []
+            place = 0
+            for unit, b0, count in groups[i]:
+                for b in range(b0, b0 + count):
+                    made = [("w", n) for n, piece in enumerate(pieces) if piece[0] == unit and piece[1] < (b + 1) * N and piece[1] + piece[2] > b * N]
 
-        def set_load(s):
-            heads = SETS[s]
-            nc.sync.dma_start(out=q_raw[rows_of(1, 2)], in_=features(qT[heads[1] : heads[2] + 1]))
-            nc.sync.dma_start(out=q_raw[rows_of(0)], in_=features(qT[heads[0] : heads[0] + 1]))
+                    def call(dst=y_banks[i % 2][:, place, :], unit=unit, b=b):
+                        nc.tensor.matmul_mx(
+                            out=dst,
+                            lhsT=words(w_mx[unit], every, b * N, N),
+                            lhsT_scale=scales(w_mx[unit], every, b * N, N),
+                            rhs=words(v_mx, every, unit[0] * D, D),
+                            rhs_scale=scales(v_mx, every, unit[0] * D, D),
+                            start=True,
+                            stop=True,
+                        )
 
-        def set_cast():
-            interleave(q_bf[used, NQ : 2 * NQ, :], q_raw[used])
+                    result.append((("y", i, place), free + made + ["v"], call))
+                    place += 1
+            return result
 
-        nc.sync.dma_start(out=k_raw[rows_of(1, 2)], in_=features(kT))
-        open_load(*OPENING[0])
-        nc.sync.dma_start(out=kb_raw[:], in_=per_token(kb))
-        for c0, w in OPENING[1:]:
-            open_load(c0, w)
-        set_load(1)
-        nc.sync.dma_start(out=t_raw[:], in_=per_token(t))
-        nc.sync.dma_start(out=mt[:, 0:2, :], in_=tokens(mask)[:, 0:2, :])
+        def result_out(i, on_scalar):
+            cols = [unit[1][b] for unit, b0, count in groups[i] for b in range(b0, b0 + count)]
+            res = res_room[i][:].rearrange("p r n -> p (r n)")[:, 0 : len(cols) * D].rearrange("p (c e) -> p c e", e=D)
+            y = y_banks[i % 2][:, 0 : len(cols), :]
+            start = 0
+            for e in range(1, len(cols) + 1):
+                if e == len(cols) or cols[e][0] != cols[start][0]:
+                    head, q0 = cols[start][0:2]
+                    rows = out[head, q0 : q0 + (e - start) * N, :].rearrange("(c p) e -> p c e", p=P)
+                    stores.setdefault(i, []).append(dma(("out", i, start), [("res", i)], rows, res[:, start:e, :]))
+                    start = e
+            needs = [("y", i, e) for e in range(len(cols))]
+            if on_scalar:
+                return (("res", i), needs, lambda: nc.scalar.activation(out=res, in_=y, func=ACT.Copy, scale=1.0 / 16.0))
+            return (("res", i), needs, lambda: nc.vector.tensor_scalar(out=res, in0=y, scalar1=1.0 / 16.0, scalar2=None, op0=ALU.mult))
 
-        nc.vector.memset(zero[:], 0.0)
-        for c0 in (0, N + HALF):
-            nc.scalar.activation(
-                out=q_open[c0][rows_of(0)].rearrange("p j n -> p (j n)"),
-                in_=zero[rows_of(0)].to_broadcast([ROWS, PACK * N]),
-                func=ACT.Silu,
-            )
-        nc.vector.memset(k_raw[rows_of(0)], 0.0)
-        nc.vector.memset(k_mx[0][:, NT : NT + NT // 4], 0)
-        nc.gpsimd.memset(q_open[N][rows_of(0)], 0.0)
-
-        dst, src = k_cast_views(0)
-        nc.vector.tensor_copy(out=dst, in_=src)
-        dst, src = k_cast_views(1)
-        nc.scalar.copy(out=dst, in_=src)
-        nc.scalar.activation(out=kb_half[:], in_=kb_raw[:], func=ACT.Copy, scale=0.5)
-        open_cast(0)
-        k_quant(0)
-        q_quant(0, 0, N)
-        for r in range(1, PACK):
-            k_quant(r)
-        k_copy(0, 0)
-        nc.sync.dma_start(out=mt[:, 2:4, :], in_=tokens(mask)[:, 2:4, :])
-        nc.sync.dma_start(out=v_raw[:], in_=v.rearrange("g (p j) e -> p g j e", j=PACK))
-        k_copy(2, 0)
-        k_copy(0, 1)
-        k_copy(1, 1)
-        for c0, w in OPENING[1:]:
-            open_cast(c0)
-
-        def mask_t(r):
-            nc.vector.tensor_scalar(
-                out=mt[:, r, :], in0=mt[:, r, :], scalar1=t_raw[:, r : r + 1], scalar2=None, op0=ALU.mult
-            )
+        stores = {}
+        res_room = [first_capped, second_capped] + [own[unit] for unit in whole] + [own[last[0]], own[whole[0]], own[last[1]]]
 
         def poly_steps(u, p, room):
             g0, a, g, lead = tanh_factors()
             z, y, y1, y2, y3, r1, r2 = room
 
             def fold(dst, src, c, other):
-                return lambda: nc.vector.scalar_tensor_tensor(
-                    out=dst, in0=src, scalar=c, in1=other, op0=ALU.add, op1=ALU.mult
-                )
+                return lambda: nc.vector.scalar_tensor_tensor(out=dst, in0=src, scalar=c, in1=other, op0=ALU.add, op1=ALU.mult)
 
             def moved(dst, c, f):
                 return lambda: nc.vector.tensor_scalar(out=dst, in0=y, scalar1=c, scalar2=f, op0=ALU.add, op1=ALU.mult)
@@ -227,284 +422,92 @@ def tile_rows_a_silu_kb_mask_cap_kernel(tc, qT, kT, t, v, kb, mask, out):
                 fold(p, r2, 1.0, u),
             ]
 
-        def after_opening():
-            u_all = first_capped[:].rearrange("p r n -> p (r n)")
-            p_all = first_gated[:].rearrange("p r n -> p (r n)")
-            room = [k_raw[:, e, 0:POLY] for e in range(PACK)] + [q_open[N][:, 2 * e : 2 * e + 2, :].rearrange("p j n -> p (j n)")[:, 0:POLY] for e in range(2)]
-            room = room + [room[0]]
-            steps = poly_steps(u_all[:, 0:POLY], p_all[:, 0:POLY], room)
-            lane = POLY // LANES
-            lanes = [
-                poly_steps(u_all[:, c : c + lane], p_all[:, c : c + lane], [x[:, c : c + lane] for x in room])
-                for c in range(0, POLY, lane)
-            ]
-            q_quant(N, N, N)
-            q_quant(2 * N, 2 * N, N)
-            q_quant(3 * N, 3 * N, N)
-            for e in range(5):
-                if e in (3, 4):
-                    steps[e]()
-                else:
-                    for each in lanes:
-                        each[e]()
-            set_cast()
-            set_load(2)
-            rest = steps[5:]
-            fill = [lambda: q_quant(NQ, NQ, NQ)] + [lambda r=r: mask_t(r) for r in range(PACK)]
-            for e, other in enumerate(fill):
-                if e < len(rest):
-                    rest[e]()
-                other()
+        u_all, p_all = first_capped[:].rearrange(flat), first_gated[:].rearrange(flat)
+        spare = mid_raw[0][:].rearrange("p j n -> p (j n)")
+        room = [k_raw[:, e, 0:POLY] for e in range(PACK)] + [spare[:, e * NQ : e * NQ + POLY] for e in range(2)]
+        room = room + [room[0]]
+        lane = POLY // 2
+        lanes = [poly_steps(u_all[:, c : c + lane], p_all[:, c : c + lane], [x[:, c : c + lane] for x in room]) for c in (0, lane)]
+        ready = [("k_cast", 1)] + [("cap", unit, r) for unit in first for r in range((POLY + HALF - 1) // HALF)]
+        steps = poly_steps(u_all[:, 0:POLY], p_all[:, 0:POLY], room)
+        paired = [(("poly", e, i), ready, lanes[i][e]) for e in range(3) for i in range(2)]
+        single = [(("poly", e) if e < 9 else "poly", ready, steps[e]) for e in range(3, 10)]
 
-        def v_cast():
-            nc.vector.tensor_copy(
-                out=v_bf[:].rearrange("p g (c i) j -> p g c j i", i=4),
-                in_=v_raw[:].rearrange("p g j (c i) -> p g c j i", i=4),
+        def mask_t(r):
+            return (
+                ("mt", r),
+                [("mask", r // 2), "t_raw"],
+                lambda: nc.vector.tensor_scalar(out=mt[:, r, :], in0=mt[:, r, :], scalar1=t_raw[:, r : r + 1], scalar2=None, op0=ALU.mult),
             )
 
-        def v_quant():
-            nc.vector.quantize_mx(
-                out=v_codes[:].bitcast(FP8X4), scales=v_scales[:], in_=v_bf[:].rearrange("p g e j -> p (g e j)")
-            )
+        v_cast = (
+            "v_cast",
+            ["v_raw"],
+            lambda: nc.vector.tensor_copy(
+                out=v_bf[:].rearrange("p g (c i) j -> p g c j i", i=4), in_=v_raw[:].rearrange("p g j (c i) -> p g c j i", i=4)
+            ),
+        )
+        v_quant = quantise("v", [], v_mx, every, 0, KV * D, v_bf[:].rearrange("p g e j -> p (g e j)"))
+        late_cast = interleave("late_cast", [("late_raw", 0), ("late_raw", 1)], q_bf[:], late_raw[:])
+        late_quant = q_quant("late", [], "late", every, 0, NQ, 0)
+        last_cast = interleave("last_cast", [("last_raw", 0), ("last_raw", 1)], q_bf[low, 0:N, :], edge_raw[low])
+        last_quant = q_quant("last", [], "last", low, 0, N, 0)
 
-        before_weights = {V_PIECE: v_cast, LAST_SET_PIECE: set_cast}
-        after_weights = {V_PIECE: v_quant, LAST_SET_PIECE: lambda: q_quant(NQ, 2 * NQ, NQ)}
+        vector.extend(paired[0:1] + [q_quant(("mid", 1), [], "mid", every, HALF, N, N + HALF)] + paired[1:] + single[0:2])
+        vector.extend(side_by_side(single[2:], [mask_t(r) for r in range(PACK)]))
+        ahead = {LATE_AT: [late_cast, w_quant(LATE_AT - 2), late_quant, v_cast], LAST_AT: [last_cast]}
+        behind = {LATE_AT: [v_quant], LAST_AT: [last_quant]}
+        for i, n in enumerate(RES_AT):
+            behind.setdefault(n, []).append(result_out(i, False))
+        tail = len(pieces) - HELD
+        for n in range(len(pieces)):
+            vector.extend(ahead.get(n, []))
+            vector.append(weights(n))
+            if 1 <= n <= tail and n - 1 not in PROMPT and n != LATE_AT - 1:
+                vector.append(w_quant(n - 1))
+            vector.extend(behind.get(n, []))
+            if n in PROMPT:
+                vector.append(w_quant(n))
+        vector.extend(w_quant(n) for n in range(tail, len(pieces)))
+        for i in range(len(RES_AT), len(groups)):
+            on_scalar = i < len(groups) - 1
+            (scalar if on_scalar else vector).append(result_out(i, on_scalar))
+        for i in range(len(groups)):
+            sync.extend(stores[i])
 
-        first_1, first_2 = [(g, 0, 0, N) for g in (1, 2)]
-        rest_1, rest_2 = [(g, 0, N, NQ - N) for g in (1, 2)]
-        whole = [(g, s, 0, NQ) for g, s in ((1, 1), (0, 1), (2, 1), (0, 2), (1, 2))]
-        end_a, end_b, end_c = (2, 2, 0, HALF), (2, 2, HALF, N), (2, 2, HALF + N, N)
+        def lane_of(fills):
+            return [call for fill in fills for call in passes(fill)]
 
-        def caps(unit, *slots):
-            return [("cap", (unit, slots), r) for r in slots]
-
-        def gate(unit, c0, w):
-            return [("silu", unit, c0, w)]
-
-        order = caps(first_1, 0) + caps(first_2, 0) + caps(first_1, 1, 2)[:1] + caps(first_2, 1, 2)[:1] + caps(first_1, 1, 2)[1:] + caps(first_2, 1, 2)[1:]
-        order = order + caps(first_1, 3) + caps(first_2, 3) + [("silu", None, POLY, 3 * HALF), ("silu", None, 3 * HALF, 4 * HALF)]
-        for r in range(PACK):
-            order = order + caps(rest_1, r) + caps(rest_2, r)
-        order = order + gate(rest_1, 0, NQ - N) + caps(whole[0], 0) + caps(whole[0], 1) + gate(rest_2, 0, NQ - N)
-        waiting = []
-        for unit, ahead in zip(whole, whole[1:]):
-            order = order + caps(ahead, 0) + caps(unit, 2) + waiting + caps(unit, 3) + caps(ahead, 1)
-            if unit in whole[:WIDE]:
-                order, waiting = order + gate(unit, 0, NQ), []
+        for a, b in zip(fills_of(first[0]), fills_of(first[1])):
+            tensor.extend(side_by_side(passes(a), passes(b)))
+        for a, b in zip(fills_of(second[0]), fills_of(second[1])):
+            tensor.extend(side_by_side(passes(a), passes(b)))
+        tensor.extend(lane_of(fills_of(whole[0])[0:2]))
+        for i, unit in enumerate(whole[:-1]):
+            if i == 1:
+                tensor.extend(lane_of(fills_of(unit)[2:4] + fills_of(whole[i + 1])[0:2]))
             else:
-                order, waiting = order + gate(unit, 0, HALF), gate(unit, HALF, HALF)
-        tanh_a = caps(end_a, 0, 1) + caps(end_a, 2, 3)
-        tanh_b, tanh_c = caps(end_b, 0, 1, 2, 3), caps(end_c, 0, 1, 2, 3)
-        order = order + caps(whole[-1], 2) + waiting + caps(whole[-1], 3) + tanh_a[:1] + gate(whole[-1], 0, HALF)
-        order = order + tanh_a[1:3] + gate(whole[-1], HALF, HALF) + tanh_a[3:]
-        order = order + tanh_b[:2] + gate(end_a, 0, N) + tanh_b[2:] + gate(end_a, N, N)
-        order = order + tanh_c[:2] + gate(end_b, 0, N // 2) + tanh_c[2:] + gate(end_b, N // 2, N // 2)
-        order = order + gate(end_c, 0, N // 2) + gate(end_c, N // 2, N // 2)
+                for r in range(2):
+                    tensor.extend(side_by_side(passes(fills_of(whole[i + 1])[r]), passes(fills_of(unit)[2 + r])))
+                    if r == 0 and i in Y_BETWEEN:
+                        tensor.extend(products(Y_BETWEEN[i]))
+            for g in Y_AFTER.get(i, []):
+                tensor.extend(products(g))
+        tensor.extend(side_by_side(lane_of(fills_of(last[1])), passes(fills_of(whole[-1])[2])))
+        tensor.extend(passes(fills_of(whole[-1])[3]) + products(5) + lane_of(fills_of(last[0])))
+        for g in range(6, len(groups)):
+            tensor.extend(products(g))
 
-        fills, first_use, last_use, bank_of = [], {}, {}, {}
-        uses = [0] * TILES
-        for position, step in enumerate(order):
-            if step[0] == "cap":
-                fill = step[1]
-                g = fill[0][0]
-                if fill not in bank_of:
-                    fills.append(fill)
-                    first_use[fill] = position
-                    bank_of[fill] = (g, uses[g] % 2)
-                    uses[g] += 1
-                last_use[fill] = position
-
-        def split(step):
-            unit, c0, w = step[1:]
-            if unit is None:
-                return [(first_1, 0, N), (first_2, 0, N)] if w == 4 * HALF else []
-            return [(unit, c0 + c, min(HALF, w - c)) for c in range(0, w, HALF)]
-
-        pieces = [piece for step in order if step[0] == "silu" for piece in split(step)]
-        closing = [n for n, piece in enumerate(pieces) if piece[0] in (end_a, end_b, end_c)]
-        halves = [n for n, piece in enumerate(pieces) if piece[0] in whole[WIDE:]]
-        groups = [(n, n + 1) for n in range(0, halves[0], 2)] + [(n,) for n in halves]
-        groups = groups + [(n, n + 1) for n in closing[::2]]
-        on_vector = groups.index((halves[-1],))
-        place = {}
-        for i, group in enumerate(groups):
-            tile0 = 0
-            for n in group:
-                place[n] = (i, tile0)
-                tile0 += pieces[n][2] // N
-
-        capped, gated, w_bf, w_codes, w_scales = {}, {}, {}, {}, {}
-        filled, quantised, multiplied, stored = [], [], [], []
-        first_capped = keep.tile([P, PACK, 2 * N], F32, name="first_capped")
-        first_gated = keep.tile([P, PACK, 2 * N], F32, name="first_gated")
-        for i, unit in enumerate((first_1, first_2)):
-            capped[unit] = first_capped[:, :, i * N : (i + 1) * N]
-            gated[i] = first_gated[:, :, i * N : (i + 1) * N]
-
-        def score_calls(fill):
-            unit, slots = fill
-            g, s, first, w = unit
-            bank = score_banks[g][bank_of[fill][1]]
-            return [
-                (bank[:, e * w + c : e * w + c + N], g, s, r, s * NQ + first + c)
-                for e, r in enumerate(slots)
-                for c in range(0, w, N)
-            ]
-
-        def scores(together):
-            lanes = [[call for fill in together if fill[0][0] == g for call in score_calls(fill)] for g in range(TILES)]
-            calls = [lane[i] for i in range(max(len(lane) for lane in lanes)) for lane in lanes if i < len(lane)]
-            for dst, g, s, r, col in calls:
-                keys = keys_of(g, SETS[s][g] // GROUP)
-                nc.tensor.matmul_mx(
-                    out=dst,
-                    lhsT=keys[rows_of(g), r * N : (r + 1) * N].bitcast(FP8X4),
-                    lhsT_scale=key_scales(keys, rows_of(g), r),
-                    rhs=q_codes[rows_of(g), col : col + N].bitcast(FP8X4),
-                    rhs_scale=q_scales[rows_of(g), col : col + N],
-                    start=True,
-                    stop=True,
-                )
-
-        def refill(done):
-            taken = [bank_of[f] for f in filled if last_use[f] > done]
-            together = []
-            for fill in fills:
-                if fill not in filled and first_use[fill] <= done + AHEAD:
-                    if bank_of[fill] not in taken:
-                        together.append(fill)
-                    taken.append(bank_of[fill])
-            scores(together)
-            filled.extend(together)
-
-        def cap(fill, r):
-            unit, slots = fill
-            w = unit[3]
-            if unit not in capped:
-                capped[unit] = keep.tile([P, PACK, w], F32, name="capped%d_%d_%d" % unit[0:3])
-            bank = score_banks[unit[0]][bank_of[fill][1]]
-            e = slots.index(r)
-            nc.scalar.activation(
-                out=capped[unit][:, r, :],
-                in_=bank[:, e * w : (e + 1) * w],
-                func=ACT.Tanh,
-                scale=0.5,
-                bias=kb_half[:, r : r + 1],
-            )
-
-        def silu(step, n):
-            unit, c0, w = step[1:]
-            if unit is None:
-                flat = "p r n -> p (r n)"
-                nc.scalar.activation(
-                    out=first_gated[:].rearrange(flat)[:, c0:w], in_=first_capped[:].rearrange(flat)[:, c0:w], func=ACT.Silu, scale=2.0
-                )
-                return
-            result = keep.tile([P, PACK, w], F32, name="gated%d" % n)
-            nc.scalar.activation(out=result[:], in_=capped[unit][:, :, c0 : c0 + w], func=ACT.Silu, scale=2.0)
-            for i, piece in enumerate(split(step)):
-                gated[n + i] = result[:, :, piece[1] - c0 : piece[1] - c0 + piece[2]]
-
-        def weights(n):
-            unit, c0, w = pieces[n]
-            first = unit[2] + c0
-            w_bf[n] = work.tile([P, w, PACK], BF16, name="w_bf", align_bytes=64)
-            nc.vector.tensor_tensor(
-                out=w_bf[n][:].rearrange("p (c i) r -> p c r i", i=4),
-                in0=gated[n].rearrange("p r (c i) -> p c r i", i=4),
-                in1=mt[:, :, first : first + w].rearrange("p r (c i) -> p c r i", i=4),
-                op=ALU.mult,
-            )
-
-        def w_quant(n):
-            c0, w = pieces[n][1:]
-            quantised.append(n)
-            if c0 % N:
-                w_codes[n], w_scales[n] = w_codes[n - 1], w_scales[n - 1]
-            else:
-                w_codes[n] = keep.tile([P, max(w, N)], U32, name="w_codes%d" % n, align_bytes=64)
-                w_scales[n] = keep.tile([P, max(w, N)], U8, name="w_scales%d" % n, align_bytes=64)
-            cols = slice(c0 % N, c0 % N + w)
-            nc.vector.quantize_mx(
-                out=w_codes[n][:, cols].bitcast(FP8X4),
-                scales=w_scales[n][:, cols],
-                in_=w_bf[n][:].rearrange("p n j -> p (n j)"),
-            )
-
-        def second_product(n):
-            unit, c0, w = pieces[n]
-            kv = SETS[unit[1]][unit[0]] // GROUP
-            e_cols = slice(kv * D, (kv + 1) * D)
-            i, tile0 = place[n]
-            multiplied.append(n)
-            for c in range((c0 % N + w) // N):
-                nc.tensor.matmul_mx(
-                    out=y_banks[i % 2][:, tile0 + c, :],
-                    lhsT=w_codes[n][:, c * N : (c + 1) * N].bitcast(FP8X4),
-                    lhsT_scale=w_scales[n][:, c * N : (c + 1) * N],
-                    rhs=v_codes[:, e_cols].bitcast(FP8X4),
-                    rhs_scale=v_scales[:, e_cols],
-                    start=True,
-                    stop=True,
-                )
-
-        def store(i, on_scalar):
-            tiles = sum(pieces[n][2] for n in groups[i]) // N
-            y = y_banks[i % 2]
-            res = keep.tile([P, tiles, D], F32, name="res%d" % i)
-            stored.append(i)
-            if on_scalar:
-                nc.scalar.activation(out=res[:], in_=y[:, 0:tiles, :], func=ACT.Copy, scale=1.0 / 16.0)
-            else:
-                nc.vector.tensor_scalar(out=res[:], in0=y[:, 0:tiles, :], scalar1=1.0 / 16.0, scalar2=None, op0=ALU.mult)
-            runs = []
-            for n in groups[i]:
-                unit, c0, w = pieces[n]
-                head, first = SETS[unit[1]][unit[0]], unit[2] + c0
-                if runs and runs[-1][0] == head:
-                    runs[-1] = (head, runs[-1][1], runs[-1][2] + w, runs[-1][3])
-                else:
-                    runs.append((head, first, w, place[n][1]))
-            for head, first, w, tile0 in runs:
-                nc.sync.dma_start(
-                    out=out[head, first : first + w, :].rearrange("(c p) e -> p c e", p=P),
-                    in_=res[:, tile0 : tile0 + w // N, :],
-                )
-
-        late = {closing[1]: closing[0:1], closing[2]: closing[1:2], closing[-1]: closing[2:]}
-
-        ripe = []
-        refill(-1)
-        n = 0
-        for done, step in enumerate(order):
-            if step[0] == "cap":
-                cap(step[1], step[2])
-                if done == 3:
-                    after_opening()
-            else:
-                silu(step, n)
-                ready = list(ripe) if n < PATIENT else list(quantised)
-                ripe = list(quantised)
-                for m in ready:
-                    if m not in multiplied and n > 2 and place[m][0] < len(stored) + 2:
-                        second_product(m)
-                for piece in split(step):
-                    if n in before_weights:
-                        before_weights[n]()
-                    weights(n)
-                    if 1 <= n <= closing[0] and n - 1 not in quantised:
-                        w_quant(n - 1)
-                    if n in after_weights:
-                        after_weights[n]()
-                    n += 1
-                while len(stored) < on_vector and groups[len(stored)][-1] in multiplied:
-                    store(len(stored), False)
-                if stored and n <= closing[0]:
-                    w_quant(n - 1)
-                for m in late.get(n - 1, ()):
-                    w_quant(m)
-            refill(done)
-        for i in range(len(stored), len(groups)):
-            for m in [m for group in groups[i : i + 2] for m in group if m not in multiplied]:
-                second_product(m)
-            store(i, i < len(groups) - 1)
+        queues = [sync, vector, scalar, tensor]
+        heads = [0] * len(queues)
+        done = set()
+        while any(h < len(queue) for h, queue in zip(heads, queues)):
+            moved_on = False
+            for e, queue in enumerate(queues):
+                while heads[e] < len(queue) and all(need in done for need in queue[heads[e]][1]):
+                    name, needs, call = queue[heads[e]]
+                    call()
+                    done.add(name)
+                    heads[e] += 1
+                    moved_on = True
+            assert moved_on, [queue[h][0:2] for h, queue in zip(heads, queues) if h < len(queue)]

@@ -95,7 +95,7 @@ def tile_rows_a_silu_kb_mask_cap_kernel(tc, qT, kT, t, v, kb, mask, out):
         mid_raw = [keep.tile([P, PACK, w], F32, name="mid_raw%d" % w) for w in (HALF, N)]
         late_raw = keep.tile([P, PACK, NQ], F32, name="late_raw")
         q_bf = keep.tile([P, NQ, PACK], BF16, name="q_bf", align_bytes=64)
-        q_mx = {name: mx_tile(name, w) for name, w in (("first", N), ("last", N), ("mid", MID), ("mid_moved", MID), ("late", NQ), ("late_moved", NQ))}
+        q_mx = {name: mx_tile(name, w) for name, w in (("first", N), ("last", N), ("mid", MID), ("mid_moved", MID), ("late", NQ), ("late_moved", NQ), ("late_more", NQ))}
         v_raw = keep.tile([P, KV, PACK, D], F32, name="v_raw")
         v_bf = keep.tile([P, KV, D, PACK], BF16, name="v_bf", align_bytes=64)
         v_mx = mx_tile("v_mx", KV * D)
@@ -120,11 +120,11 @@ def tile_rows_a_silu_kb_mask_cap_kernel(tc, qT, kT, t, v, kb, mask, out):
         def per_token(ap):
             return ap.rearrange("(p j) o -> p (j o)", j=PACK)
 
-        def dma(name, needs, dst, src):
-            return (name, needs, lambda: nc.sync.dma_start(out=dst, in_=src))
+        def dma(name, needs, dst, src, queue=nc.sync):
+            return (name, needs, lambda: queue.dma_start(out=dst, in_=src))
 
-        def move(name, needs, source, g, target):
-            return dma(name, needs, q_mx[source + "_moved"][0][rows_of(target)].bitcast(I32), q_mx[source][0][rows_of(g)].bitcast(I32))
+        def move(name, needs, source, g, into, target):
+            return dma(name, needs, q_mx[into][0][rows_of(target)].bitcast(I32), q_mx[source][0][rows_of(g)].bitcast(I32))
 
         def interleave(name, needs, dst, src):
             return (
@@ -149,6 +149,8 @@ def tile_rows_a_silu_kb_mask_cap_kernel(tc, qT, kT, t, v, kb, mask, out):
             src = k_raw[low].rearrange("p j (s r) -> p s j r", r=PACK)[:, :, :, 2 * a : 2 * a + 2]
             return dst, src
 
+        scalar.append(dma("kb_raw", ["first_raw"], kb_raw[:], per_token(kb), nc.scalar))
+        scalar.append(dma("t_raw", [], t_raw[:], per_token(t), nc.scalar))
         vector.append(("zero", ["first_raw"], lambda: nc.vector.memset(zero[:], 0.0)))
         scalar.append(
             (
@@ -169,38 +171,37 @@ def tile_rows_a_silu_kb_mask_cap_kernel(tc, qT, kT, t, v, kb, mask, out):
             return tuple((head, q0 + i * N, source, c0 + i * N) for i in range(count))
 
         near, far = (3, 4), (2, 5)
-        late_near, late_far = (1, 6), (0, 7)
         first = [(kv, blocks(near[kv], 0, 1, "first", 0)) for kv in range(KV)]
         second = [(kv, blocks(near[kv], N, 2, "mid", 0)) for kv in range(KV)]
         whole = [(kv, blocks(far[kv], N, 3, "mid_moved", 0) + blocks(near[kv], 3 * N, 1, "mid", HALF)) for kv in range(KV)]
-        whole = whole + [(kv, blocks(late_near[kv], 0, 4, "late", 0)) for kv in range(KV)]
-        whole = whole + [(0, blocks(late_far[0], 0, 4, "late_moved", 0)), (1, blocks(late_far[1], 0, 3, "late_moved", 0))]
-        last = [(1, blocks(late_far[1], 3 * N, 1, "late_moved", 3 * N) + blocks(far[1], 0, 1, "last", 0)), (0, blocks(far[0], 0, 1, "last", 0))]
+        whole = whole + [(0, blocks(0, 0, 4, "late", 0)), (1, blocks(6, 0, 4, "late_moved", 0))]
+        whole = whole + [(0, blocks(1, 0, 4, "late_moved", 0)), (1, blocks(7, 0, 3, "late_more", 0))]
+        last = [(1, blocks(7, 3 * N, 1, "late_more", 3 * N) + blocks(far[1], 0, 1, "last", 0)), (0, blocks(far[0], 0, 1, "last", 0))]
 
         def operand_ready(kv, block):
             source = block[2]
             if source == "mid":
                 return ("mid", block[3] // HALF)
-            return (source, kv) if source in ("mid_moved", "late_moved") else source
+            return (source, block[0]) if source in ("mid_moved", "late_moved", "late_more") else source
 
         sync.append(dma("k_raw", [], k_raw[both], features(kT)))
         sync.append(dma("first_raw", [], edge_raw[both], features(qT[3:5, :, 0:N])))
-        sync.append(dma("kb_raw", [], kb_raw[:], per_token(kb)))
         sync.append(dma(("mid_raw", 0), [], mid_raw[0][:], features(qT[2:6, :, N : N + HALF])))
         sync.append(dma(("mid_raw", 1), [], mid_raw[1][:], features(qT[2:6, :, N + HALF : NQ])))
-        sync.append(dma("t_raw", [], t_raw[:], per_token(t)))
         sync.append(dma(("mask", 0), [], mt[:, 0:2, :], tokens(mask)[:, 0:2, :]))
         sync.append(dma(("mask", 1), [], mt[:, 2:4, :], tokens(mask)[:, 2:4, :]))
-        sync.append(move(("mid_moved", 0), [("mid", 1)], "mid", 0, 1))
-        sync.append(move(("mid_moved", 1), [("mid", 1)], "mid", 3, 2))
-        sync.append(dma(("late_raw", 0), [], late_raw[0:64], features(qT[0:2])))
-        sync.append(dma(("late_raw", 1), [], late_raw[64:128], features(qT[6:8])))
+        sync.append(move(("mid_moved", 2), [("mid", 1)], "mid", 0, "mid_moved", 1))
+        sync.append(move(("mid_moved", 5), [("mid", 1)], "mid", 3, "mid_moved", 2))
+        sync.append(dma(("late_raw", 0), [], late_raw[both], features(qT[0:2])))
+        sync.append(dma(("late_raw", 1), [], late_raw[rows_of(3)], features(qT[6:7])))
+        sync.append(dma(("late_raw", 2), [], late_raw[rows_of(0)], features(qT[7:8])))
         sync.append(dma("v_raw", [], v_raw[:], v.rearrange("g (p j) e -> p g j e", j=PACK)))
         for kv in range(KV):
             head = far[kv]
             sync.append(dma(("last_raw", kv), ["first_cast"], edge_raw[rows_of(1 + kv)], features(qT[head : head + 1, :, 0:N])))
-        sync.append(move(("late_moved", 0), ["late"], "late", 0, 1))
-        sync.append(move(("late_moved", 1), ["late"], "late", 3, 2))
+        sync.append(move(("late_moved", 6), ["late"], "late", 3, "late_moved", 2))
+        sync.append(move(("late_moved", 1), ["late"], "late", 2, "late_moved", 1))
+        sync.append(move(("late_more", 7), ["late"], "late", 0, "late_more", 2))
 
         dst0, src0 = k_cast_views(0)
         dst1, src1 = k_cast_views(1)
@@ -253,9 +254,7 @@ def tile_rows_a_silu_kb_mask_cap_kernel(tc, qT, kT, t, v, kb, mask, out):
         order = order + gate(last[0], N + N // 2, N // 2) + gate(last[1], 0, N // 2) + gate(last[1], N // 2, N // 2)
 
         def fills_of(unit):
-            if unit in first + second:
-                return [(unit, (0,)), (unit, (1, 2)), (unit, (3,))]
-            per_bank = NQ // (N * len(unit[1]))
+            per_bank = NQ // (N * len(unit[1])) if unit in last else 1
             return [(unit, tuple(range(r, r + per_bank))) for r in range(0, PACK, per_bank)]
 
         bank_of, before_in_bank = {}, {}
@@ -448,7 +447,7 @@ def tile_rows_a_silu_kb_mask_cap_kernel(tc, qT, kT, t, v, kb, mask, out):
             ),
         )
         v_quant = quantise("v", [], v_mx, every, 0, KV * D, v_bf[:].rearrange("p g e j -> p (g e j)"))
-        late_cast = interleave("late_cast", [("late_raw", 0), ("late_raw", 1)], q_bf[:], late_raw[:])
+        late_cast = interleave("late_cast", [("late_raw", e) for e in range(3)], q_bf[:], late_raw[:])
         late_quant = q_quant("late", [], "late", every, 0, NQ, 0)
         last_cast = interleave("last_cast", [("last_raw", 0), ("last_raw", 1)], q_bf[low, 0:N, :], edge_raw[low])
         last_quant = q_quant("last", [], "last", low, 0, N, 0)

@@ -22,15 +22,18 @@ N = 128
 HALF = 256
 BANKS = 3
 SHIFT = -5.5
-POLY = 384
+POLY = 320
 WIDE = 2
 LATE_AT = 3
 LAST_AT = 5
-HELD = 4
-RES_AT = (4, 5, 7, 8, 11, 12, 15)
+HELD = 5
+RES_AT = (4, 5, 7, 8, 11, 13, 14)
 PROMPT = (5, 7, 9, 11, 13)
 Y_AFTER = {1: (0,), 2: (1,), 3: (3,), 4: (4,)}
 Y_BETWEEN = {3: 2}
+SHARE = 96
+WINDOW = 64
+FIRST = (13,)
 
 
 def tanh_factors():
@@ -142,11 +145,11 @@ def tile_rows_a_silu_kb_mask_cap_kernel(tc, qT, kT, t, v, kb, mask, out):
             return quantise(name, needs, q_mx[source], rows, c0, w, q_bf[rows, bf0 : bf0 + w, :].rearrange("p n j -> p (n j)"))
 
         def k_quant(r):
-            return quantise(("k", r), [("k_cast", r // 2)], k_mx, low, r * N, N, k_bf[low, r].rearrange("p s j -> p (s j)"))
+            return quantise(("k", r), [("k_cast", r // 2), "k_rest"], k_mx, low, r * N, N, k_bf[low, r].rearrange("p s j -> p (s j)"))
 
-        def k_cast_views(a):
-            dst = k_bf[low, 2 * a : 2 * a + 2].rearrange("p r s j -> p s j r")
-            src = k_raw[low].rearrange("p j (s r) -> p s j r", r=PACK)[:, :, :, 2 * a : 2 * a + 2]
+        def k_cast_views(a, s0, s1):
+            dst = k_bf[low, 2 * a : 2 * a + 2, s0:s1].rearrange("p r s j -> p s j r")
+            src = k_raw[low].rearrange("p j (s r) -> p s j r", r=PACK)[:, s0:s1, :, 2 * a : 2 * a + 2]
             return dst, src
 
         scalar.append(dma("kb_raw", ["first_raw"], kb_raw[:], per_token(kb), nc.scalar))
@@ -181,8 +184,8 @@ def tile_rows_a_silu_kb_mask_cap_kernel(tc, qT, kT, t, v, kb, mask, out):
         def operand_ready(kv, block):
             source = block[2]
             if source == "mid":
-                return ("mid", block[3] // HALF)
-            return (source, block[0]) if source in ("mid_moved", "late_moved", "late_more") else source
+                return ("mid", block[3] // N)
+            return (source, block[0]) if source == "mid_moved" else source
 
         sync.append(dma("k_raw", [], k_raw[both], features(kT)))
         sync.append(dma("first_raw", [], edge_raw[both], features(qT[3:5, :, 0:N])))
@@ -190,8 +193,8 @@ def tile_rows_a_silu_kb_mask_cap_kernel(tc, qT, kT, t, v, kb, mask, out):
         sync.append(dma(("mid_raw", 1), [], mid_raw[1][:], features(qT[2:6, :, N + HALF : NQ])))
         sync.append(dma(("mask", 0), [], mt[:, 0:2, :], tokens(mask)[:, 0:2, :]))
         sync.append(dma(("mask", 1), [], mt[:, 2:4, :], tokens(mask)[:, 2:4, :]))
-        sync.append(move(("mid_moved", 2), [("mid", 1)], "mid", 0, "mid_moved", 1))
-        sync.append(move(("mid_moved", 5), [("mid", 1)], "mid", 3, "mid_moved", 2))
+        sync.append(move(("mid_moved", 2), [("mid", 2)], "mid", 0, "mid_moved", 1))
+        sync.append(move(("mid_moved", 5), [("mid", 2)], "mid", 3, "mid_moved", 2))
         sync.append(dma(("late_raw", 0), [], late_raw[both], features(qT[0:2])))
         sync.append(dma(("late_raw", 1), [], late_raw[rows_of(3)], features(qT[6:7])))
         sync.append(dma(("late_raw", 2), [], late_raw[rows_of(0)], features(qT[7:8])))
@@ -199,12 +202,13 @@ def tile_rows_a_silu_kb_mask_cap_kernel(tc, qT, kT, t, v, kb, mask, out):
         for kv in range(KV):
             head = far[kv]
             sync.append(dma(("last_raw", kv), ["first_cast"], edge_raw[rows_of(1 + kv)], features(qT[head : head + 1, :, 0:N])))
-        sync.append(move(("late_moved", 6), ["late"], "late", 3, "late_moved", 2))
-        sync.append(move(("late_moved", 1), ["late"], "late", 2, "late_moved", 1))
-        sync.append(move(("late_more", 7), ["late"], "late", 0, "late_more", 2))
+        sync.append(dma("late_moved", ["late"], q_mx["late_moved"][0][both].bitcast(I32), q_mx["late"][0][2 * ROWS : P].bitcast(I32)))
+        sync.append(move("late_more", ["late"], "late", 0, "late_more", 2))
 
-        dst0, src0 = k_cast_views(0)
-        dst1, src1 = k_cast_views(1)
+        dst0, src0 = k_cast_views(0, 0, SHARE)
+        dst1, src1 = k_cast_views(1, 0, N)
+        dst2, src2 = k_cast_views(0, SHARE, N)
+        scalar.append(("k_rest", ["k_raw", ("k_zero", 0)], lambda: nc.scalar.copy(out=dst2, in_=src2)))
         vector.append((("k_cast", 0), ["k_raw"], lambda: nc.vector.tensor_copy(out=dst0, in_=src0)))
         scalar.append((("k_cast", 1), ["k_raw", ("k_zero", 0)], lambda: nc.scalar.copy(out=dst1, in_=src1)))
         scalar.append(("kb_half", ["kb_raw"], lambda: nc.scalar.activation(out=kb_half[:], in_=kb_raw[:], func=ACT.Copy, scale=0.5)))
@@ -212,8 +216,9 @@ def tile_rows_a_silu_kb_mask_cap_kernel(tc, qT, kT, t, v, kb, mask, out):
         vector.append(k_quant(0))
         vector.append(q_quant("first", [], "first", low, 0, N, 0))
         vector.extend(k_quant(r) for r in range(1, PACK))
-        vector.append(interleave(("mid_cast", 0), [("mid_raw", 0)], q_bf[:, N : N + HALF, :], mid_raw[0][:]))
-        vector.append(q_quant(("mid", 0), [], "mid", every, 0, HALF, N))
+        for b in range(2):
+            vector.append(interleave(("mid_cast", 0, b), [("mid_raw", 0)], q_bf[:, (1 + b) * N : (2 + b) * N, :], mid_raw[0][:, :, b * N : (b + 1) * N]))
+        vector.extend(q_quant(("mid", b), [], "mid", every, b * N, N, (1 + b) * N) for b in range(2))
         vector.append(interleave(("mid_cast", 1), [("mid_raw", 1)], q_bf[:, N + HALF : NQ, :], mid_raw[1][:]))
 
         capped, own = {}, {}
@@ -248,13 +253,13 @@ def tile_rows_a_silu_kb_mask_cap_kernel(tc, qT, kT, t, v, kb, mask, out):
             if i <= WIDE:
                 order = order + caps(unit, 0, 1) + gate(before, 0, NQ) + caps(unit, 2, 3)
             else:
-                order = order + caps(unit, 0) + gate(before, 0, HALF) + caps(unit, 1) + gate(before, HALF, HALF) + caps(unit, 2, 3)
+                order = order + caps(unit, 0) + gate(before, 0, HALF) + gate(before, HALF, HALF) + caps(unit, 1, 2, 3)
         order = order + caps(last[0], 0) + gate(whole[-1], 0, N) + caps(last[0], 1) + gate(whole[-1], N, N) + caps(last[0], 2, 3) + gate(whole[-1], HALF, N)
         order = order + gate(last[0], 0, N) + caps(last[1], 0, 1) + gate(last[0], N, N // 2) + caps(last[1], 2, 3)
-        order = order + gate(last[0], N + N // 2, N // 2) + gate(last[1], 0, N // 2) + gate(last[1], N // 2, N // 2)
+        order = order + gate(last[0], N + N // 2, N // 2) + gate(last[1], 0, N // 2) + gate(last[1], N // 2, N // 4) + gate(last[1], 3 * N // 4, N // 4)
 
         def fills_of(unit):
-            per_bank = NQ // (N * len(unit[1])) if unit in last else 1
+            per_bank = NQ // (N * len(unit[1])) if unit == last[1] else 1
             return [(unit, tuple(range(r, r + per_bank))) for r in range(0, PACK, per_bank)]
 
         bank_of, before_in_bank = {}, {}
@@ -335,6 +340,9 @@ def tile_rows_a_silu_kb_mask_cap_kernel(tc, qT, kT, t, v, kb, mask, out):
         for i, unit in enumerate(first + second + whole + last):
             w_mx[unit] = mx_tile("w_mx%d" % i, N * len(unit[1]))
 
+        closes = [(piece[1] + piece[2]) % WINDOW == 0 for piece in pieces]
+        ring_of = [sum(closes[0:n]) for n in range(len(pieces))]
+
         def weights(n):
             unit, c0, w, gated, needs = pieces[n]
             q0 = unit[1][c0 // N][1] + c0 % N
@@ -342,7 +350,7 @@ def tile_rows_a_silu_kb_mask_cap_kernel(tc, qT, kT, t, v, kb, mask, out):
                 ("weights", n),
                 needs + [("mt", r) for r in range(PACK)],
                 lambda: nc.vector.tensor_tensor(
-                    out=w_ring[n % 4][:, 0:w, :].rearrange("p (c i) r -> p c r i", i=4),
+                    out=w_ring[ring_of[n] % 4][:, c0 % WINDOW : c0 % WINDOW + w, :].rearrange("p (c i) r -> p c r i", i=4),
                     in0=gated.rearrange("p r (c i) -> p c r i", i=4),
                     in1=mt[:, :, q0 : q0 + w].rearrange("p r (c i) -> p c r i", i=4),
                     op=ALU.mult,
@@ -351,7 +359,8 @@ def tile_rows_a_silu_kb_mask_cap_kernel(tc, qT, kT, t, v, kb, mask, out):
 
         def w_quant(n):
             unit, c0, w = pieces[n][0:3]
-            return quantise(("w", n), [], w_mx[unit], every, c0, w, w_ring[n % 4][:, 0:w, :].rearrange("p n j -> p (n j)"))
+            c0, w = c0 - c0 % WINDOW, w + c0 % WINDOW
+            return quantise(("w", n), [], w_mx[unit], every, c0, w, w_ring[ring_of[n] % 4][:, 0:w, :].rearrange("p n j -> p (n j)"))
 
         groups = [[(unit, 0, 1) for unit in first], [(unit, 0, 2) for unit in second]] + [[(unit, 0, len(unit[1]))] for unit in whole]
         groups = groups + [[(last[0], 0, 1)], [(last[0], 1, 1)], [(last[1], 0, 1)]]
@@ -362,7 +371,7 @@ def tile_rows_a_silu_kb_mask_cap_kernel(tc, qT, kT, t, v, kb, mask, out):
             place = 0
             for unit, b0, count in groups[i]:
                 for b in range(b0, b0 + count):
-                    made = [("w", n) for n, piece in enumerate(pieces) if piece[0] == unit and piece[1] < (b + 1) * N and piece[1] + piece[2] > b * N]
+                    made = [("w", n) for n, piece in enumerate(pieces) if closes[n] and piece[0] == unit and piece[1] < (b + 1) * N and piece[1] + piece[2] > b * N]
 
                     def call(dst=y_banks[i % 2][:, place, :], unit=unit, b=b):
                         nc.tensor.matmul_mx(
@@ -384,7 +393,9 @@ def tile_rows_a_silu_kb_mask_cap_kernel(tc, qT, kT, t, v, kb, mask, out):
             res = res_room[i][:].rearrange("p r n -> p (r n)")[:, 0 : len(cols) * D].rearrange("p (c e) -> p c e", e=D)
             y = y_banks[i % 2][:, 0 : len(cols), :]
             start = 0
-            for e in range(1, len(cols) + 1):
+            if i == 0:
+                stores[i] = [dma(("out", i), [("res", i)], out[3:5, 0:N, :].rearrange("h p e -> p h e"), res)]
+            for e in range(1, len(cols) + 1 if i else 0):
                 if e == len(cols) or cols[e][0] != cols[start][0]:
                     head, q0 = cols[start][0:2]
                     rows = out[head, q0 : q0 + (e - start) * N, :].rearrange("(c p) e -> p c e", p=P)
@@ -452,7 +463,7 @@ def tile_rows_a_silu_kb_mask_cap_kernel(tc, qT, kT, t, v, kb, mask, out):
         last_cast = interleave("last_cast", [("last_raw", 0), ("last_raw", 1)], q_bf[low, 0:N, :], edge_raw[low])
         last_quant = q_quant("last", [], "last", low, 0, N, 0)
 
-        vector.extend(paired[0:1] + [q_quant(("mid", 1), [], "mid", every, HALF, N, N + HALF)] + paired[1:] + single[0:2])
+        vector.extend(paired[0:1] + [q_quant(("mid", 2), [], "mid", every, HALF, N, N + HALF)] + paired[1:] + single[0:2])
         vector.extend(side_by_side(single[2:], [mask_t(r) for r in range(PACK)]))
         ahead = {LATE_AT: [late_cast, w_quant(LATE_AT - 2), late_quant, v_cast], LAST_AT: [last_cast]}
         behind = {LATE_AT: [v_quant], LAST_AT: [last_quant]}
@@ -464,10 +475,12 @@ def tile_rows_a_silu_kb_mask_cap_kernel(tc, qT, kT, t, v, kb, mask, out):
             vector.append(weights(n))
             if 1 <= n <= tail and n - 1 not in PROMPT and n != LATE_AT - 1:
                 vector.append(w_quant(n - 1))
-            vector.extend(behind.get(n, []))
-            if n in PROMPT:
+            if n in PROMPT and n in FIRST:
                 vector.append(w_quant(n))
-        vector.extend(w_quant(n) for n in range(tail, len(pieces)))
+            vector.extend(behind.get(n, []))
+            if n in PROMPT and n not in FIRST:
+                vector.append(w_quant(n))
+        vector.extend(w_quant(n) for n in range(tail, len(pieces)) if closes[n])
         for i in range(len(RES_AT), len(groups)):
             on_scalar = i < len(groups) - 1
             (scalar if on_scalar else vector).append(result_out(i, on_scalar))
@@ -493,8 +506,9 @@ def tile_rows_a_silu_kb_mask_cap_kernel(tc, qT, kT, t, v, kb, mask, out):
             for g in Y_AFTER.get(i, []):
                 tensor.extend(products(g))
         tensor.extend(side_by_side(lane_of(fills_of(last[1])), passes(fills_of(whole[-1])[2])))
-        tensor.extend(passes(fills_of(whole[-1])[3]) + products(5) + lane_of(fills_of(last[0])))
-        for g in range(6, len(groups)):
+        tensor.extend(passes(fills_of(whole[-1])[3]) + products(5) + lane_of(fills_of(last[0])[0:3]))
+        tensor.extend(products(6) + passes(fills_of(last[0])[3]))
+        for g in range(7, len(groups)):
             tensor.extend(products(g))
 
         queues = [sync, vector, scalar, tensor]

@@ -23,17 +23,17 @@ HALF = 256
 BANKS = 3
 SHIFT = -5.5
 POLY = 320
-WIDE = 2
+WIDE = 3
 LATE_AT = 3
 LAST_AT = 5
-HELD = 5
-RES_AT = (4, 5, 7, 8, 11, 13, 14)
-PROMPT = (5, 7, 9, 11, 13)
+HELD = 4
+RES_AT = (4, 5, 7, 8, 10, 11, 14)
+PROMPT = (5, 7, 8, 10, 12)
 Y_AFTER = {1: (0,), 2: (1,), 3: (3,), 4: (4,)}
 Y_BETWEEN = {3: 2}
 SHARE = 96
 WINDOW = 64
-FIRST = (13,)
+FIRST = ()
 
 
 def tanh_factors():
@@ -112,7 +112,7 @@ def tile_rows_a_silu_kb_mask_cap_kernel(tc, qT, kT, t, v, kb, mask, out):
         y_banks = [psum.tile([P, PACK, D], F32, name="y%d" % b) for b in range(2)]
         every = slice(0, P)
 
-        sync, scalar, vector, tensor = [], [], [], []
+        sync, scalar, vector, tensor, pool = [], [], [], [], []
 
         def features(ap):
             return ap.rearrange("h (p j) n -> (h p) j n", j=PACK)
@@ -153,19 +153,20 @@ def tile_rows_a_silu_kb_mask_cap_kernel(tc, qT, kT, t, v, kb, mask, out):
             return dst, src
 
         scalar.append(dma("kb_raw", ["first_raw"], kb_raw[:], per_token(kb), nc.scalar))
-        scalar.append(dma("t_raw", [], t_raw[:], per_token(t), nc.scalar))
         vector.append(("zero", ["first_raw"], lambda: nc.vector.memset(zero[:], 0.0)))
         scalar.append(
             (
                 "edge_zero",
                 ["zero"],
                 lambda: nc.scalar.activation(
-                    out=edge_raw[rows_of(0)].rearrange("p j n -> p (j n)"),
-                    in_=zero[rows_of(0)].to_broadcast([ROWS, PACK * N]),
+                    out=edge_raw[rows_of(0), 0, :],
+                    in_=zero[rows_of(0)].to_broadcast([ROWS, N]),
                     func=ACT.Silu,
                 ),
             )
         )
+        scalar.append(dma("t_raw", [], t_raw[:], per_token(t), nc.scalar))
+        pool.append(("edge_rest", ["first_raw"], lambda: nc.gpsimd.memset(edge_raw[rows_of(0), 1:PACK, :], 0.0)))
         vector.append((("k_zero", 0), [], lambda: nc.vector.memset(k_raw[rows_of(0)], 0.0)))
         for name in ("mid", "late"):
             vector.append((("plane", name), [], lambda name=name: nc.vector.memset(q_mx[name][0][:, q_mx[name][1] :], 0)))
@@ -212,7 +213,7 @@ def tile_rows_a_silu_kb_mask_cap_kernel(tc, qT, kT, t, v, kb, mask, out):
         vector.append((("k_cast", 0), ["k_raw"], lambda: nc.vector.tensor_copy(out=dst0, in_=src0)))
         scalar.append((("k_cast", 1), ["k_raw", ("k_zero", 0)], lambda: nc.scalar.copy(out=dst1, in_=src1)))
         scalar.append(("kb_half", ["kb_raw"], lambda: nc.scalar.activation(out=kb_half[:], in_=kb_raw[:], func=ACT.Copy, scale=0.5)))
-        vector.append(interleave("first_cast", ["first_raw", "edge_zero"], q_bf[low, 0:N, :], edge_raw[low]))
+        vector.append(interleave("first_cast", ["first_raw", "edge_zero", "edge_rest"], q_bf[low, 0:N, :], edge_raw[low]))
         vector.append(k_quant(0))
         vector.append(q_quant("first", [], "first", low, 0, N, 0))
         vector.extend(k_quant(r) for r in range(1, PACK))
@@ -251,12 +252,14 @@ def tile_rows_a_silu_kb_mask_cap_kernel(tc, qT, kT, t, v, kb, mask, out):
         for i in range(1, len(whole)):
             unit, before = whole[i], whole[i - 1]
             if i <= WIDE:
-                order = order + caps(unit, 0, 1) + gate(before, 0, NQ) + caps(unit, 2, 3)
-            else:
+                order = order + caps(unit, 0) + gate(before, 0, NQ) + caps(unit, 1, 2, 3)
+            elif unit != whole[-1]:
                 order = order + caps(unit, 0) + gate(before, 0, HALF) + gate(before, HALF, HALF) + caps(unit, 1, 2, 3)
+            else:
+                order = order + caps(unit, 0) + gate(before, 0, HALF) + caps(unit, 1) + gate(before, HALF, HALF) + caps(unit, 2, 3)
         order = order + caps(last[0], 0) + gate(whole[-1], 0, N) + caps(last[0], 1) + gate(whole[-1], N, N) + caps(last[0], 2, 3) + gate(whole[-1], HALF, N)
         order = order + gate(last[0], 0, N) + caps(last[1], 0, 1) + gate(last[0], N, N // 2) + caps(last[1], 2, 3)
-        order = order + gate(last[0], N + N // 2, N // 2) + gate(last[1], 0, N // 2) + gate(last[1], N // 2, N // 4) + gate(last[1], 3 * N // 4, N // 4)
+        order = order + gate(last[0], N + N // 2, N // 2) + gate(last[1], 0, N // 2) + gate(last[1], N // 2, N // 2)
 
         def fills_of(unit):
             per_bank = NQ // (N * len(unit[1])) if unit == last[1] else 1
@@ -506,12 +509,11 @@ def tile_rows_a_silu_kb_mask_cap_kernel(tc, qT, kT, t, v, kb, mask, out):
             for g in Y_AFTER.get(i, []):
                 tensor.extend(products(g))
         tensor.extend(side_by_side(lane_of(fills_of(last[1])), passes(fills_of(whole[-1])[2])))
-        tensor.extend(passes(fills_of(whole[-1])[3]) + products(5) + lane_of(fills_of(last[0])[0:3]))
-        tensor.extend(products(6) + passes(fills_of(last[0])[3]))
-        for g in range(7, len(groups)):
+        tensor.extend(passes(fills_of(whole[-1])[3]) + products(5) + lane_of(fills_of(last[0])))
+        for g in range(6, len(groups)):
             tensor.extend(products(g))
 
-        queues = [sync, vector, scalar, tensor]
+        queues = [sync, pool, vector, scalar, tensor]
         heads = [0] * len(queues)
         done = set()
         while any(h < len(queue) for h, queue in zip(heads, queues)):

@@ -22,18 +22,19 @@ N = 128
 HALF = 256
 BANKS = 3
 SHIFT = -5.5
-POLY = 320
+POLY = 448
 WIDE = 3
 LATE_AT = 3
 LAST_AT = 5
 HELD = 4
-RES_AT = (4, 5, 7, 8, 10, 11, 14)
+RES_AT = (4, 6, 7, 8, 10, 11, 14)
 PROMPT = (5, 7, 8, 10, 12)
-Y_AFTER = {1: (0,), 2: (1,), 3: (3,), 4: (4,)}
+Y_AFTER = {2: (1,), 3: (3,), 4: (4,)}
 Y_BETWEEN = {3: 2}
 SHARE = 96
 WINDOW = 64
 FIRST = ()
+V_AT = 3
 
 
 def tanh_factors():
@@ -248,8 +249,13 @@ def tile_rows_a_silu_kb_mask_cap_kernel(tc, qT, kT, t, v, kb, mask, out):
         order = order + [("silu", "first", POLY, 3 * HALF), ("silu", "first", 3 * HALF, 4 * HALF)]
         for r in range(PACK):
             order = order + caps(second[0], r) + caps(second[1], r)
-        order = order + gate("second", 0, 3 * NQ) + caps(whole[0], 0) + gate("second", 3 * NQ, 4 * NQ) + caps(whole[0], 1, 2, 3)
-        for i in range(1, len(whole)):
+        order = order + gate("second", 0, 3 * NQ) + gate("second", 3 * NQ, 4 * NQ)
+        for r in range(PACK):
+            order = order + caps(whole[0], r) + caps(whole[1], r)
+        order = order + gate(whole[0], 0, NQ) + gate(whole[1], 0, NQ)
+        order = order + caps(whole[2], 0, 1, 2) + caps(whole[3], 0) + caps(whole[2], 3) + caps(whole[3], 1)
+        order = order + gate(whole[2], 0, NQ) + caps(whole[3], 2, 3)
+        for i in range(4, len(whole)):
             unit, before = whole[i], whole[i - 1]
             if i <= WIDE:
                 order = order + caps(unit, 0) + gate(before, 0, NQ) + caps(unit, 1, 2, 3)
@@ -437,14 +443,23 @@ def tile_rows_a_silu_kb_mask_cap_kernel(tc, qT, kT, t, v, kb, mask, out):
 
         u_all, p_all = first_capped[:].rearrange(flat), first_gated[:].rearrange(flat)
         spare = mid_raw[0][:].rearrange("p j n -> p (j n)")
-        room = [k_raw[:, e, 0:POLY] for e in range(PACK)] + [spare[:, e * NQ : e * NQ + POLY] for e in range(2)]
-        room = room + [room[0]]
+        wide = [k_raw[:, e, :] for e in range(PACK)] + [spare[:, e * NQ : (e + 1) * NQ] for e in range(2)]
+        wide = wide + [wide[0]]
+        room = [x[:, 0:POLY] for x in wide]
         lane = POLY // 2
         lanes = [poly_steps(u_all[:, c : c + lane], p_all[:, c : c + lane], [x[:, c : c + lane] for x in room]) for c in (0, lane)]
         ready = [("k_cast", 1)] + [("cap", unit, r) for unit in first for r in range((POLY + HALF - 1) // HALF)]
         steps = poly_steps(u_all[:, 0:POLY], p_all[:, 0:POLY], room)
         paired = [(("poly", e, i), ready, lanes[i][e]) for e in range(3) for i in range(2)]
-        single = [(("poly", e) if e < 9 else "poly", ready, steps[e]) for e in range(3, 10)]
+        single = [(("poly", e), ready, steps[e]) for e in range(3, 9)]
+
+        def two_slots(ap):
+            return ap.rearrange("p (r n) -> p r n", r=2)[:, :, 0:N]
+
+        ends = [poly_steps(two_slots(u_all[:, 0:NQ]), two_slots(p_all[:, 0:NQ]), [two_slots(x) for x in wide])[9]]
+        for c0, c1 in ((N, HALF), (HALF + N, POLY)):
+            ends.append(poly_steps(u_all[:, c0:c1], p_all[:, c0:c1], [x[:, c0:c1] for x in wide])[9])
+        single = single + [(("poly", 9, e) if e < 2 else "poly", ready, call) for e, call in enumerate(ends)]
 
         def mask_t(r):
             return (
@@ -468,8 +483,9 @@ def tile_rows_a_silu_kb_mask_cap_kernel(tc, qT, kT, t, v, kb, mask, out):
 
         vector.extend(paired[0:1] + [q_quant(("mid", 2), [], "mid", every, HALF, N, N + HALF)] + paired[1:] + single[0:2])
         vector.extend(side_by_side(single[2:], [mask_t(r) for r in range(PACK)]))
-        ahead = {LATE_AT: [late_cast, w_quant(LATE_AT - 2), late_quant, v_cast], LAST_AT: [last_cast]}
-        behind = {LATE_AT: [v_quant], LAST_AT: [last_quant]}
+        ahead = {LATE_AT: [late_cast, w_quant(LATE_AT - 2), late_quant], LAST_AT: [last_cast]}
+        ahead.setdefault(V_AT, []).append(v_cast)
+        behind = {V_AT: [v_quant], LAST_AT: [last_quant]}
         for i, n in enumerate(RES_AT):
             behind.setdefault(n, []).append(result_out(i, False))
         tail = len(pieces) - HELD
@@ -497,15 +513,15 @@ def tile_rows_a_silu_kb_mask_cap_kernel(tc, qT, kT, t, v, kb, mask, out):
             tensor.extend(side_by_side(passes(a), passes(b)))
         for a, b in zip(fills_of(second[0]), fills_of(second[1])):
             tensor.extend(side_by_side(passes(a), passes(b)))
-        tensor.extend(lane_of(fills_of(whole[0])[0:2]))
-        for i, unit in enumerate(whole[:-1]):
-            if i == 1:
-                tensor.extend(lane_of(fills_of(unit)[2:4] + fills_of(whole[i + 1])[0:2]))
-            else:
-                for r in range(2):
-                    tensor.extend(side_by_side(passes(fills_of(whole[i + 1])[r]), passes(fills_of(unit)[2 + r])))
-                    if r == 0 and i in Y_BETWEEN:
-                        tensor.extend(products(Y_BETWEEN[i]))
+        for a, b in zip(fills_of(whole[1]), fills_of(whole[0])):
+            tensor.extend(side_by_side(passes(a), passes(b)))
+        tensor.extend(lane_of(fills_of(whole[2])[0:2]) + products(0))
+        for i in range(2, len(whole) - 1):
+            unit = whole[i]
+            for r in range(2):
+                tensor.extend(side_by_side(passes(fills_of(whole[i + 1])[r]), passes(fills_of(unit)[2 + r])))
+                if r == 0 and i in Y_BETWEEN:
+                    tensor.extend(products(Y_BETWEEN[i]))
             for g in Y_AFTER.get(i, []):
                 tensor.extend(products(g))
         tensor.extend(side_by_side(lane_of(fills_of(last[1])), passes(fills_of(whole[-1])[2])))

@@ -22,19 +22,13 @@ N = 128
 HALF = 256
 BANKS = 3
 SHIFT = -5.5
-POLY = 448
+POLY = 416
 WIDE = 3
-LATE_AT = 3
-LAST_AT = 5
-HELD = 4
-RES_AT = (4, 6, 7, 8, 10, 11, 14)
-PROMPT = (5, 7, 8, 10, 12)
-Y_AFTER = {2: (1,), 3: (3,), 4: (4,)}
-Y_BETWEEN = {3: 2}
+JOINED = (0, 2, 4, 6)
+ON_VECTOR = 7
+Y_AFTER = {2: (0, 1), 3: (2, 3), 4: (4,)}
+Y_BETWEEN = {}
 SHARE = 96
-WINDOW = 64
-FIRST = ()
-V_AT = 3
 
 
 def tanh_factors():
@@ -249,13 +243,8 @@ def tile_rows_a_silu_kb_mask_cap_kernel(tc, qT, kT, t, v, kb, mask, out):
         order = order + [("silu", "first", POLY, 3 * HALF), ("silu", "first", 3 * HALF, 4 * HALF)]
         for r in range(PACK):
             order = order + caps(second[0], r) + caps(second[1], r)
-        order = order + gate("second", 0, 3 * NQ) + gate("second", 3 * NQ, 4 * NQ)
-        for r in range(PACK):
-            order = order + caps(whole[0], r) + caps(whole[1], r)
-        order = order + gate(whole[0], 0, NQ) + gate(whole[1], 0, NQ)
-        order = order + caps(whole[2], 0, 1, 2) + caps(whole[3], 0) + caps(whole[2], 3) + caps(whole[3], 1)
-        order = order + gate(whole[2], 0, NQ) + caps(whole[3], 2, 3)
-        for i in range(4, len(whole)):
+        order = order + gate("second", 0, 3 * NQ) + caps(whole[0], 0) + gate("second", 3 * NQ, 4 * NQ) + caps(whole[0], 1, 2, 3)
+        for i in range(1, len(whole)):
             unit, before = whole[i], whole[i - 1]
             if i <= WIDE:
                 order = order + caps(unit, 0) + gate(before, 0, NQ) + caps(unit, 1, 2, 3)
@@ -345,21 +334,27 @@ def tile_rows_a_silu_kb_mask_cap_kernel(tc, qT, kT, t, v, kb, mask, out):
                     c += width
             scalar.append((step, [], lambda dst=dst, src=src: nc.scalar.activation(out=dst, in_=src, func=ACT.Silu, scale=2.0)))
 
-        w_mx = {}
-        for i, unit in enumerate(first + second + whole + last):
-            w_mx[unit] = mx_tile("w_mx%d" % i, N * len(unit[1]))
+        w_mx, w_col = {}, {}
+        for i, together in enumerate([first, second] + [[unit] for unit in whole + last]):
+            width = N * len(together[0][1])
+            sheet = mx_tile("w_mx%d" % i, width * len(together))
+            for e, unit in enumerate(together):
+                w_mx[unit], w_col[unit] = sheet, e * width
 
-        closes = [(piece[1] + piece[2]) % WINDOW == 0 for piece in pieces]
-        ring_of = [sum(closes[0:n]) for n in range(len(pieces))]
+        batch_of = [n - sum(1 for m in JOINED if m < n) for n in range(len(pieces))]
+
+        def batch(n):
+            return [m for m in range(len(pieces)) if batch_of[m] == batch_of[n]]
 
         def weights(n):
             unit, c0, w, gated, needs = pieces[n]
             q0 = unit[1][c0 // N][1] + c0 % N
+            at = sum(pieces[m][2] for m in batch(n) if m < n)
             return (
                 ("weights", n),
                 needs + [("mt", r) for r in range(PACK)],
                 lambda: nc.vector.tensor_tensor(
-                    out=w_ring[ring_of[n] % 4][:, c0 % WINDOW : c0 % WINDOW + w, :].rearrange("p (c i) r -> p c r i", i=4),
+                    out=w_ring[batch_of[n] % 4][:, at : at + w, :].rearrange("p (c i) r -> p c r i", i=4),
                     in0=gated.rearrange("p r (c i) -> p c r i", i=4),
                     in1=mt[:, :, q0 : q0 + w].rearrange("p r (c i) -> p c r i", i=4),
                     op=ALU.mult,
@@ -367,9 +362,10 @@ def tile_rows_a_silu_kb_mask_cap_kernel(tc, qT, kT, t, v, kb, mask, out):
             )
 
         def w_quant(n):
-            unit, c0, w = pieces[n][0:3]
-            c0, w = c0 - c0 % WINDOW, w + c0 % WINDOW
-            return quantise(("w", n), [], w_mx[unit], every, c0, w, w_ring[ring_of[n] % 4][:, 0:w, :].rearrange("p n j -> p (n j)"))
+            unit, c0 = pieces[batch(n)[0]][0:2]
+            w = sum(pieces[m][2] for m in batch(n))
+            src = w_ring[batch_of[n] % 4][:, 0:w, :].rearrange("p n j -> p (n j)")
+            return quantise(("w", batch_of[n]), [], w_mx[unit], every, w_col[unit] + c0, w, src)
 
         groups = [[(unit, 0, 1) for unit in first], [(unit, 0, 2) for unit in second]] + [[(unit, 0, len(unit[1]))] for unit in whole]
         groups = groups + [[(last[0], 0, 1)], [(last[0], 1, 1)], [(last[1], 0, 1)]]
@@ -380,13 +376,13 @@ def tile_rows_a_silu_kb_mask_cap_kernel(tc, qT, kT, t, v, kb, mask, out):
             place = 0
             for unit, b0, count in groups[i]:
                 for b in range(b0, b0 + count):
-                    made = [("w", n) for n, piece in enumerate(pieces) if closes[n] and piece[0] == unit and piece[1] < (b + 1) * N and piece[1] + piece[2] > b * N]
+                    made = [("w", batch_of[n]) for n, piece in enumerate(pieces) if piece[0] == unit and piece[1] < (b + 1) * N and piece[1] + piece[2] > b * N]
 
                     def call(dst=y_banks[i % 2][:, place, :], unit=unit, b=b):
                         nc.tensor.matmul_mx(
                             out=dst,
-                            lhsT=words(w_mx[unit], every, b * N, N),
-                            lhsT_scale=scales(w_mx[unit], every, b * N, N),
+                            lhsT=words(w_mx[unit], every, w_col[unit] + b * N, N),
+                            lhsT_scale=scales(w_mx[unit], every, w_col[unit] + b * N, N),
                             rhs=words(v_mx, every, unit[0] * D, D),
                             rhs_scale=scales(v_mx, every, unit[0] * D, D),
                             start=True,
@@ -483,24 +479,19 @@ def tile_rows_a_silu_kb_mask_cap_kernel(tc, qT, kT, t, v, kb, mask, out):
 
         vector.extend(paired[0:1] + [q_quant(("mid", 2), [], "mid", every, HALF, N, N + HALF)] + paired[1:] + single[0:2])
         vector.extend(side_by_side(single[2:], [mask_t(r) for r in range(PACK)]))
-        ahead = {LATE_AT: [late_cast, w_quant(LATE_AT - 2), late_quant], LAST_AT: [last_cast]}
-        ahead.setdefault(V_AT, []).append(v_cast)
-        behind = {V_AT: [v_quant], LAST_AT: [last_quant]}
-        for i, n in enumerate(RES_AT):
-            behind.setdefault(n, []).append(result_out(i, False))
-        tail = len(pieces) - HELD
-        for n in range(len(pieces)):
-            vector.extend(ahead.get(n, []))
-            vector.append(weights(n))
-            if 1 <= n <= tail and n - 1 not in PROMPT and n != LATE_AT - 1:
-                vector.append(w_quant(n - 1))
-            if n in PROMPT and n in FIRST:
-                vector.append(w_quant(n))
-            vector.extend(behind.get(n, []))
-            if n in PROMPT and n not in FIRST:
-                vector.append(w_quant(n))
-        vector.extend(w_quant(n) for n in range(tail, len(pieces)) if closes[n])
-        for i in range(len(RES_AT), len(groups)):
+        def res(i):
+            return result_out(i, False)
+
+        vector.extend([weights(0), weights(1), weights(2), late_cast, w_quant(1), late_quant, v_cast, weights(3), v_quant, w_quant(3)])
+        vector.extend([weights(4), last_cast, weights(5), last_quant, w_quant(5), res(0)])
+        vector.extend([weights(6), weights(7), res(1), w_quant(7)])
+        vector.extend([weights(8), res(2), w_quant(8), res(3)])
+        vector.extend([weights(9), weights(10), w_quant(9), res(4), w_quant(10)])
+        vector.extend([weights(11), res(5), weights(12), w_quant(11), w_quant(12)])
+        vector.extend([weights(13), weights(14), w_quant(13), res(6), weights(15), w_quant(14), weights(16), w_quant(15)])
+        vector.extend([weights(17), w_quant(16), weights(18), weights(19), weights(20)])
+        vector.extend(w_quant(n) for n in range(17, 21))
+        for i in range(ON_VECTOR, len(groups)):
             on_scalar = i < len(groups) - 1
             (scalar if on_scalar else vector).append(result_out(i, on_scalar))
         for i in range(len(groups)):
@@ -513,15 +504,15 @@ def tile_rows_a_silu_kb_mask_cap_kernel(tc, qT, kT, t, v, kb, mask, out):
             tensor.extend(side_by_side(passes(a), passes(b)))
         for a, b in zip(fills_of(second[0]), fills_of(second[1])):
             tensor.extend(side_by_side(passes(a), passes(b)))
-        for a, b in zip(fills_of(whole[1]), fills_of(whole[0])):
-            tensor.extend(side_by_side(passes(a), passes(b)))
-        tensor.extend(lane_of(fills_of(whole[2])[0:2]) + products(0))
-        for i in range(2, len(whole) - 1):
-            unit = whole[i]
-            for r in range(2):
-                tensor.extend(side_by_side(passes(fills_of(whole[i + 1])[r]), passes(fills_of(unit)[2 + r])))
-                if r == 0 and i in Y_BETWEEN:
-                    tensor.extend(products(Y_BETWEEN[i]))
+        tensor.extend(lane_of(fills_of(whole[0])[0:2]))
+        for i, unit in enumerate(whole[:-1]):
+            if i == 1:
+                tensor.extend(lane_of(fills_of(unit)[2:4] + fills_of(whole[i + 1])[0:2]))
+            else:
+                for r in range(2):
+                    tensor.extend(side_by_side(passes(fills_of(whole[i + 1])[r]), passes(fills_of(unit)[2 + r])))
+                    if r == 0 and i in Y_BETWEEN:
+                        tensor.extend(products(Y_BETWEEN[i]))
             for g in Y_AFTER.get(i, []):
                 tensor.extend(products(g))
         tensor.extend(side_by_side(lane_of(fills_of(last[1])), passes(fills_of(whole[-1])[2])))

@@ -21,8 +21,7 @@ ROWS = 32
 N = 128
 HALF = 256
 BANKS = 3
-SHIFT = -5.5
-POLY = 416
+POLY = (352, 128)
 WIDE = 3
 JOINED = (0, 2, 4, 6)
 ON_VECTOR = 7
@@ -40,27 +39,33 @@ def tanh_factors():
             dd[i] = (dd[i] - dd[i - 1]) / (zs[i] - zs[i - level])
     coef = [dd[7]]
     for i in range(6, -1, -1):
-        coef = [a - zs[i] * b for a, b in zip(coef + [0.0], [0.0] + coef)]
+        coef = [x - zs[i] * w for x, w in zip(coef + [0.0], [0.0] + coef)]
         coef[-1] = coef[-1] + dd[i]
     lead = coef[0]
+    monic = [x / lead for x in coef]
 
-    def divide(p, c):
-        p = list(p)
+    def root(fun, x):
+        for step in range(30):
+            x = x - fun(x) * 1e-6 / (fun(x + 1e-6) - fun(x))
+        return x
+
+    def divide(s, e):
+        p = list(monic)
         for i in range(len(p) - 2):
-            p[i + 1] = p[i + 1] - SHIFT * p[i]
-            p[i + 2] = p[i + 2] - c * p[i]
+            p[i + 1] = p[i + 1] - s * p[i]
+            p[i + 2] = p[i + 2] - e * p[i]
         return p[:-2], p[-2], p[-1]
 
-    p, shifts, rests = [a / lead for a in coef], [], []
-    while len(p) > 2:
-        c = 0.0
-        for step in range(60):
-            r1 = divide(p, c)[1]
-            c = c - r1 * 1e-4 / (divide(p, c + 1e-4)[1] - r1)
-        p, r1, r0 = divide(p, c)
-        shifts.append(c)
-        rests.append(r0)
-    return p[1], shifts[::-1], rests[::-1], lead
+    def nest(s):
+        e = root(lambda x: divide(s, x)[1], 10.0)
+        q, r1, r0 = divide(s, e)
+        c = monic[1] - 3 * s
+        for i in range(1, len(q)):
+            q[i] = q[i] - c * q[i - 1]
+        a = q[2] - s * s
+        return (s, a, q[4], c, q[5], e, lead, r0 * lead), q[3] - a * s
+
+    return nest(root(lambda s: nest(s)[1], -1.0))[0]
 
 
 def tile_rows_a_silu_kb_mask_cap_kernel(tc, qT, kT, t, v, kb, mask, out):
@@ -195,9 +200,7 @@ def tile_rows_a_silu_kb_mask_cap_kernel(tc, qT, kT, t, v, kb, mask, out):
         sync.append(dma(("late_raw", 1), [], late_raw[rows_of(3)], features(qT[6:7])))
         sync.append(dma(("late_raw", 2), [], late_raw[rows_of(0)], features(qT[7:8])))
         sync.append(dma("v_raw", [], v_raw[:], v.rearrange("g (p j) e -> p g j e", j=PACK)))
-        for kv in range(KV):
-            head = far[kv]
-            sync.append(dma(("last_raw", kv), ["first_cast"], edge_raw[rows_of(1 + kv)], features(qT[head : head + 1, :, 0:N])))
+        sync.append(dma("last_raw", ["first_cast"], edge_raw[both], qT[2:6:3, :, 0:N]))
         sync.append(dma("late_moved", ["late"], q_mx["late_moved"][0][both].bitcast(I32), q_mx["late"][0][2 * ROWS : P].bitcast(I32)))
         sync.append(move("late_more", ["late"], "late", 0, "late_more", 2))
 
@@ -225,7 +228,7 @@ def tile_rows_a_silu_kb_mask_cap_kernel(tc, qT, kT, t, v, kb, mask, out):
         for kv in range(KV):
             capped[first[kv]] = first_capped[:, :, kv * N : (kv + 1) * N]
             capped[second[kv]] = second_capped[:, :, kv * HALF : (kv + 1) * HALF]
-        shared = {"first": (first, first_capped, first_gated, ["poly"]), "second": (second, second_capped, second_gated, [])}
+        shared = {"first": (first, first_capped, first_gated, ["poly"]), "second": (second[::-1], second_capped, second_gated, ["poly 2"])}
         for i, unit in enumerate(whole + last):
             tile = keep.tile([P, PACK, N * len(unit[1])], F32, name="capped%d" % i)
             capped[unit] = tile[:]
@@ -240,10 +243,10 @@ def tile_rows_a_silu_kb_mask_cap_kernel(tc, qT, kT, t, v, kb, mask, out):
         order = []
         for r in range(PACK):
             order = order + caps(first[0], r) + caps(first[1], r)
-        order = order + [("silu", "first", POLY, 3 * HALF), ("silu", "first", 3 * HALF, 4 * HALF)]
+        order = order + [("silu", "first", POLY[0], 3 * HALF), ("silu", "first", 3 * HALF, 4 * HALF)]
         for r in range(PACK):
             order = order + caps(second[0], r) + caps(second[1], r)
-        order = order + gate("second", 0, 3 * NQ) + caps(whole[0], 0) + gate("second", 3 * NQ, 4 * NQ) + caps(whole[0], 1, 2, 3)
+        order = order + gate("second", POLY[1], 3 * NQ) + caps(whole[0], 0) + gate("second", 3 * NQ, 4 * NQ) + caps(whole[0], 1, 2, 3)
         for i in range(1, len(whole)):
             unit, before = whole[i], whole[i - 1]
             if i <= WIDE:
@@ -321,7 +324,7 @@ def tile_rows_a_silu_kb_mask_cap_kernel(tc, qT, kT, t, v, kb, mask, out):
                 pair, src, dst, also = shared[unit]
                 width = N * len(pair[0][1])
                 if w == 2 * PACK * width:
-                    pieces.extend((pair[kv], 0, width, dst[:, :, kv * width : (kv + 1) * width], [step] + also) for kv in range(KV))
+                    pieces.extend((one, 0, width, dst[:, :, one[0] * width : (one[0] + 1) * width], [step]) for one in pair)
                 dst, src = dst[:].rearrange(flat)[:, c0:w], src[:].rearrange(flat)[:, c0:w]
             else:
                 result = keep.tile([P, PACK, w], F32, name="gated%d" % len(pieces))
@@ -335,7 +338,7 @@ def tile_rows_a_silu_kb_mask_cap_kernel(tc, qT, kT, t, v, kb, mask, out):
             scalar.append((step, [], lambda dst=dst, src=src: nc.scalar.activation(out=dst, in_=src, func=ACT.Silu, scale=2.0)))
 
         w_mx, w_col = {}, {}
-        for i, together in enumerate([first, second] + [[unit] for unit in whole + last]):
+        for i, together in enumerate([first, second[::-1]] + [[unit] for unit in whole + last]):
             width = N * len(together[0][1])
             sheet = mx_tile("w_mx%d" % i, width * len(together))
             for e, unit in enumerate(together):
@@ -367,8 +370,9 @@ def tile_rows_a_silu_kb_mask_cap_kernel(tc, qT, kT, t, v, kb, mask, out):
             src = w_ring[batch_of[n] % 4][:, 0:w, :].rearrange("p n j -> p (n j)")
             return quantise(("w", batch_of[n]), [], w_mx[unit], every, w_col[unit] + c0, w, src)
 
-        groups = [[(unit, 0, 1) for unit in first], [(unit, 0, 2) for unit in second]] + [[(unit, 0, len(unit[1]))] for unit in whole]
-        groups = groups + [[(last[0], 0, 1)], [(last[0], 1, 1)], [(last[1], 0, 1)]]
+        groups = [[(unit, 0, 1) for unit in first], [(unit, 0, 2) for unit in second]] + [[(unit, 0, 4)] for unit in whole[:-2]]
+        groups = groups + [[(whole[-2], 0, 2)], [(whole[-2], 2, 2), (whole[-1], 0, 2)], [(whole[-1], 2, 1), (last[0], 0, 1)]]
+        groups = groups + [[(last[0], 1, 1)], [(last[1], 0, 1)]]
 
         def products(i):
             free = [("res", i - 2)] if i >= 2 else []
@@ -412,56 +416,43 @@ def tile_rows_a_silu_kb_mask_cap_kernel(tc, qT, kT, t, v, kb, mask, out):
             return (("res", i), needs, lambda: nc.vector.tensor_scalar(out=res, in0=y, scalar1=1.0 / 16.0, scalar2=None, op0=ALU.mult))
 
         stores = {}
-        res_room = [first_capped, second_capped] + [own[unit] for unit in whole] + [own[last[0]], own[whole[0]], own[last[1]]]
+        res_room = [first_capped, second_capped] + [own[unit] for unit in whole] + [own[whole[0]], own[whole[1]], own[last[1]]]
 
-        def poly_steps(u, p, room):
-            g0, a, g, lead = tanh_factors()
-            z, y, y1, y2, y3, r1, r2 = room
+        s, a, b, c, d, e, lead, f = tanh_factors()
+        room = [k_raw[:, j, :] for j in range(PACK)] + [mid_raw[0][:, 2 * j : 2 * j + 2, :].rearrange("p j n -> p (j n)") for j in range(2)]
 
-            def fold(dst, src, c, other):
-                return lambda: nc.vector.scalar_tensor_tensor(out=dst, in0=src, scalar=c, in1=other, op0=ALU.add, op1=ALU.mult)
+        def polynomial(share, source, result, at, ready):
+            u, p = source[:].rearrange(flat)[:, 0 : POLY[share]], result[:].rearrange(flat)[:, 0 : POLY[share]]
+            z, y, zc, ye, r1, r2 = [x[:, at : at + POLY[share]] for x in room]
 
-            def moved(dst, c, f):
-                return lambda: nc.vector.tensor_scalar(out=dst, in0=y, scalar1=c, scalar2=f, op0=ALU.add, op1=ALU.mult)
+            def fold(name, dst, src, add, other):
+                call = lambda: nc.vector.scalar_tensor_tensor(out=dst, in0=src, scalar=add, in1=other, op0=ALU.add, op1=ALU.mult)
+                return ((name, share), ready, call)
+
+            def moved(name, dst, src, add, times):
+                call = lambda: nc.vector.tensor_scalar(out=dst, in0=src, scalar1=add, scalar2=times, op0=ALU.add, op1=ALU.mult)
+                return ((name, share), ready, call)
 
             return [
-                fold(z, u, 0.0, u),
-                fold(y, z, SHIFT, z),
-                moved(y1, a[0], 1.0),
-                moved(y2, a[1], 1.0),
-                moved(y3, a[2], lead),
-                fold(r1, z, g0, y1),
-                fold(r2, r1, g[0], y2),
-                fold(r1, r2, g[1], y3),
-                fold(r2, r1, g[2] * lead, u),
-                fold(p, r2, 1.0, u),
+                fold("z", z, u, 0.0, u),
+                fold("y", y, z, s, z),
+                moved("zc", zc, z, c, 1.0),
+                fold("degree 4", r1, y, a, y),
+                moved("ye", ye, y, e, lead),
+                fold("degree 5", r2, r1, b, zc),
+                fold("degree 7", r1, r2, d, ye),
+                fold("tanh", r2, r1, f, u),
+                fold("silu", p, r2, 1.0, u),
             ]
 
-        u_all, p_all = first_capped[:].rearrange(flat), first_gated[:].rearrange(flat)
-        spare = mid_raw[0][:].rearrange("p j n -> p (j n)")
-        wide = [k_raw[:, e, :] for e in range(PACK)] + [spare[:, e * NQ : (e + 1) * NQ] for e in range(2)]
-        wide = wide + [wide[0]]
-        room = [x[:, 0:POLY] for x in wide]
-        lane = POLY // 2
-        lanes = [poly_steps(u_all[:, c : c + lane], p_all[:, c : c + lane], [x[:, c : c + lane] for x in room]) for c in (0, lane)]
-        ready = [("k_cast", 1)] + [("cap", unit, r) for unit in first for r in range((POLY + HALF - 1) // HALF)]
-        steps = poly_steps(u_all[:, 0:POLY], p_all[:, 0:POLY], room)
-        paired = [(("poly", e, i), ready, lanes[i][e]) for e in range(3) for i in range(2)]
-        single = [(("poly", e), ready, steps[e]) for e in range(3, 9)]
+        one = polynomial(0, first_capped, first_gated, 0, [("k_cast", 1)] + [("cap", unit, r) for unit in first for r in range(2)])
+        two = polynomial(1, second_capped, second_gated, POLY[0], [("cap", second[0], 0)])
 
-        def two_slots(ap):
-            return ap.rearrange("p (r n) -> p r n", r=2)[:, :, 0:N]
-
-        ends = [poly_steps(two_slots(u_all[:, 0:NQ]), two_slots(p_all[:, 0:NQ]), [two_slots(x) for x in wide])[9]]
-        for c0, c1 in ((N, HALF), (HALF + N, POLY)):
-            ends.append(poly_steps(u_all[:, c0:c1], p_all[:, c0:c1], [x[:, c0:c1] for x in wide])[9])
-        single = single + [(("poly", 9, e) if e < 2 else "poly", ready, call) for e, call in enumerate(ends)]
-
-        def mask_t(r):
+        def mask_t(r, c0=0, c1=NQ):
             return (
-                ("mt", r),
+                ("mt", r) if c0 == 0 else ("mt", r, c0),
                 [("mask", r // 2), "t_raw"],
-                lambda: nc.vector.tensor_scalar(out=mt[:, r, :], in0=mt[:, r, :], scalar1=t_raw[:, r : r + 1], scalar2=None, op0=ALU.mult),
+                lambda: nc.vector.tensor_scalar(out=mt[:, r, c0:c1], in0=mt[:, r, c0:c1], scalar1=t_raw[:, r : r + 1], scalar2=None, op0=ALU.mult),
             )
 
         v_cast = (
@@ -474,21 +465,23 @@ def tile_rows_a_silu_kb_mask_cap_kernel(tc, qT, kT, t, v, kb, mask, out):
         v_quant = quantise("v", [], v_mx, every, 0, KV * D, v_bf[:].rearrange("p g e j -> p (g e j)"))
         late_cast = interleave("late_cast", [("late_raw", e) for e in range(3)], q_bf[:], late_raw[:])
         late_quant = q_quant("late", [], "late", every, 0, NQ, 0)
-        last_cast = interleave("last_cast", [("last_raw", 0), ("last_raw", 1)], q_bf[low, 0:N, :], edge_raw[low])
+        last_cast = interleave("last_cast", ["last_raw"], q_bf[low, 0:N, :], edge_raw[low])
         last_quant = q_quant("last", [], "last", low, 0, N, 0)
 
-        vector.extend(paired[0:1] + [q_quant(("mid", 2), [], "mid", every, HALF, N, N + HALF)] + paired[1:] + single[0:2])
-        vector.extend(side_by_side(single[2:], [mask_t(r) for r in range(PACK)]))
+        vector.extend([one[0], q_quant(("mid", 2), [], "mid", every, HALF, N, N + HALF)] + one[1:5])
+        vector.extend([two[0], one[5], mask_t(0), two[1], one[6], two[2], mask_t(1), two[3], one[7], two[4], mask_t(2), two[5]])
+        vector.extend([mask_t(3, 0, N), one[8], two[6], mask_t(3, N, NQ)])
+
         def res(i):
             return result_out(i, False)
 
-        vector.extend([weights(0), weights(1), weights(2), late_cast, w_quant(1), late_quant, v_cast, weights(3), v_quant, w_quant(3)])
-        vector.extend([weights(4), last_cast, weights(5), last_quant, w_quant(5), res(0)])
+        vector.extend([weights(0), two[7], weights(1), two[8], weights(2), late_cast, w_quant(1), late_quant, v_cast, weights(3), v_quant, w_quant(3)])
+        vector.extend([weights(4), last_cast, weights(5), last_quant, res(0), w_quant(5)])
         vector.extend([weights(6), weights(7), res(1), w_quant(7)])
         vector.extend([weights(8), res(2), w_quant(8), res(3)])
         vector.extend([weights(9), weights(10), w_quant(9), res(4), w_quant(10)])
         vector.extend([weights(11), res(5), weights(12), w_quant(11), w_quant(12)])
-        vector.extend([weights(13), weights(14), w_quant(13), res(6), weights(15), w_quant(14), weights(16), w_quant(15)])
+        vector.extend([weights(13), res(6), weights(14), w_quant(13), weights(15), w_quant(14), weights(16), w_quant(15)])
         vector.extend([weights(17), w_quant(16), weights(18), weights(19), weights(20)])
         vector.extend(w_quant(n) for n in range(17, 21))
         for i in range(ON_VECTOR, len(groups)):

@@ -21,7 +21,7 @@ ROWS = 32
 N = 128
 HALF = 256
 BANKS = 3
-POLY = (352, 128)
+POLY = (352, 112)
 WIDE = 3
 JOINED = (0, 2, 4, 6)
 ON_VECTOR = 7
@@ -200,7 +200,9 @@ def tile_rows_a_silu_kb_mask_cap_kernel(tc, qT, kT, t, v, kb, mask, out):
         sync.append(dma(("late_raw", 1), [], late_raw[rows_of(3)], features(qT[6:7])))
         sync.append(dma(("late_raw", 2), [], late_raw[rows_of(0)], features(qT[7:8])))
         sync.append(dma("v_raw", [], v_raw[:], v.rearrange("g (p j) e -> p g j e", j=PACK)))
-        sync.append(dma("last_raw", ["first_cast"], edge_raw[both], qT[2:6:3, :, 0:N]))
+        for kv in range(KV):
+            head = far[kv]
+            sync.append(dma(("last_raw", kv), ["first_cast"], edge_raw[rows_of(1 + kv)], features(qT[head : head + 1, :, 0:N])))
         sync.append(dma("late_moved", ["late"], q_mx["late_moved"][0][both].bitcast(I32), q_mx["late"][0][2 * ROWS : P].bitcast(I32)))
         sync.append(move("late_more", ["late"], "late", 0, "late_more", 2))
 
@@ -370,9 +372,8 @@ def tile_rows_a_silu_kb_mask_cap_kernel(tc, qT, kT, t, v, kb, mask, out):
             src = w_ring[batch_of[n] % 4][:, 0:w, :].rearrange("p n j -> p (n j)")
             return quantise(("w", batch_of[n]), [], w_mx[unit], every, w_col[unit] + c0, w, src)
 
-        groups = [[(unit, 0, 1) for unit in first], [(unit, 0, 2) for unit in second]] + [[(unit, 0, 4)] for unit in whole[:-2]]
-        groups = groups + [[(whole[-2], 0, 2)], [(whole[-2], 2, 2), (whole[-1], 0, 2)], [(whole[-1], 2, 1), (last[0], 0, 1)]]
-        groups = groups + [[(last[0], 1, 1)], [(last[1], 0, 1)]]
+        groups = [[(unit, 0, 1) for unit in first], [(unit, 0, 2) for unit in second]] + [[(unit, 0, len(unit[1]))] for unit in whole]
+        groups = groups + [[(last[0], 0, 1)], [(last[0], 1, 1)], [(last[1], 0, 1)]]
 
         def products(i):
             free = [("res", i - 2)] if i >= 2 else []
@@ -416,7 +417,7 @@ def tile_rows_a_silu_kb_mask_cap_kernel(tc, qT, kT, t, v, kb, mask, out):
             return (("res", i), needs, lambda: nc.vector.tensor_scalar(out=res, in0=y, scalar1=1.0 / 16.0, scalar2=None, op0=ALU.mult))
 
         stores = {}
-        res_room = [first_capped, second_capped] + [own[unit] for unit in whole] + [own[whole[0]], own[whole[1]], own[last[1]]]
+        res_room = [first_capped, second_capped] + [own[unit] for unit in whole] + [own[last[0]], own[whole[0]], own[last[1]]]
 
         s, a, b, c, d, e, lead, f = tanh_factors()
         room = [k_raw[:, j, :] for j in range(PACK)] + [mid_raw[0][:, 2 * j : 2 * j + 2, :].rearrange("p j n -> p (j n)") for j in range(2)]
@@ -465,7 +466,7 @@ def tile_rows_a_silu_kb_mask_cap_kernel(tc, qT, kT, t, v, kb, mask, out):
         v_quant = quantise("v", [], v_mx, every, 0, KV * D, v_bf[:].rearrange("p g e j -> p (g e j)"))
         late_cast = interleave("late_cast", [("late_raw", e) for e in range(3)], q_bf[:], late_raw[:])
         late_quant = q_quant("late", [], "late", every, 0, NQ, 0)
-        last_cast = interleave("last_cast", ["last_raw"], q_bf[low, 0:N, :], edge_raw[low])
+        last_cast = interleave("last_cast", [("last_raw", 0), ("last_raw", 1)], q_bf[low, 0:N, :], edge_raw[low])
         last_quant = q_quant("last", [], "last", low, 0, N, 0)
 
         vector.extend([one[0], q_quant(("mid", 2), [], "mid", every, HALF, N, N + HALF)] + one[1:5])
@@ -481,7 +482,7 @@ def tile_rows_a_silu_kb_mask_cap_kernel(tc, qT, kT, t, v, kb, mask, out):
         vector.extend([weights(8), res(2), w_quant(8), res(3)])
         vector.extend([weights(9), weights(10), w_quant(9), res(4), w_quant(10)])
         vector.extend([weights(11), res(5), weights(12), w_quant(11), w_quant(12)])
-        vector.extend([weights(13), res(6), weights(14), w_quant(13), weights(15), w_quant(14), weights(16), w_quant(15)])
+        vector.extend([weights(13), weights(14), w_quant(13), res(6), weights(15), w_quant(14), weights(16), w_quant(15)])
         vector.extend([weights(17), w_quant(16), weights(18), weights(19), weights(20)])
         vector.extend(w_quant(n) for n in range(17, 21))
         for i in range(ON_VECTOR, len(groups)):

@@ -21,7 +21,7 @@ ROWS = 32
 N = 128
 HALF = 256
 BANKS = 3
-POLY = (352, 112)
+POLY = (352, 128)
 WIDE = 3
 JOINED = (0, 2, 4, 6)
 ON_VECTOR = 7
@@ -477,8 +477,8 @@ def tile_rows_a_silu_kb_mask_cap_kernel(tc, qT, kT, t, v, kb, mask, out):
             return result_out(i, False)
 
         vector.extend([weights(0), two[7], weights(1), two[8], weights(2), late_cast, w_quant(1), late_quant, v_cast, weights(3), v_quant, w_quant(3)])
-        vector.extend([weights(4), last_cast, weights(5), last_quant, res(0), w_quant(5)])
-        vector.extend([weights(6), weights(7), res(1), w_quant(7)])
+        vector.extend([weights(4), weights(5), last_cast, w_quant(5), last_quant])
+        vector.extend([weights(6), res(0), weights(7), res(1), w_quant(7)])
         vector.extend([weights(8), res(2), w_quant(8), res(3)])
         vector.extend([weights(9), weights(10), w_quant(9), res(4), w_quant(10)])
         vector.extend([weights(11), res(5), weights(12), w_quant(11), w_quant(12)])
@@ -500,7 +500,10 @@ def tile_rows_a_silu_kb_mask_cap_kernel(tc, qT, kT, t, v, kb, mask, out):
             tensor.extend(side_by_side(passes(a), passes(b)))
         tensor.extend(lane_of(fills_of(whole[0])[0:2]))
         for i, unit in enumerate(whole[:-1]):
-            if i == 1:
+            if i == 0:
+                tensor.extend(side_by_side(passes(fills_of(whole[1])[0]), passes(fills_of(unit)[2])))
+                tensor.extend(passes(fills_of(unit)[3]) + passes(fills_of(whole[1])[1]))
+            elif i in (1, 2):
                 tensor.extend(lane_of(fills_of(unit)[2:4] + fills_of(whole[i + 1])[0:2]))
             else:
                 for r in range(2):

@@ -28,6 +28,7 @@ ON_VECTOR = 7
 Y_AFTER = {2: (0, 1), 3: (2, 3), 4: (4,)}
 Y_BETWEEN = {}
 SHARE = 96
+SHARE2 = 16
 
 
 def tanh_factors():
@@ -207,7 +208,8 @@ def tile_rows_a_silu_kb_mask_cap_kernel(tc, qT, kT, t, v, kb, mask, out):
         sync.append(move("late_more", ["late"], "late", 0, "late_more", 2))
 
         dst0, src0 = k_cast_views(0, 0, SHARE)
-        dst1, src1 = k_cast_views(1, 0, N)
+        dst1, src1 = k_cast_views(1, SHARE2, N)
+        dst3, src3 = k_cast_views(1, 0, SHARE2)
         dst2, src2 = k_cast_views(0, SHARE, N)
         scalar.append(("k_rest", ["k_raw", ("k_zero", 0)], lambda: nc.scalar.copy(out=dst2, in_=src2)))
         vector.append((("k_cast", 0), ["k_raw"], lambda: nc.vector.tensor_copy(out=dst0, in_=src0)))
@@ -215,6 +217,7 @@ def tile_rows_a_silu_kb_mask_cap_kernel(tc, qT, kT, t, v, kb, mask, out):
         scalar.append(("kb_half", ["kb_raw"], lambda: nc.scalar.activation(out=kb_half[:], in_=kb_raw[:], func=ACT.Copy, scale=0.5)))
         vector.append(interleave("first_cast", ["first_raw", "edge_zero", "edge_rest"], q_bf[low, 0:N, :], edge_raw[low]))
         vector.append(k_quant(0))
+        vector.append(("k_more", [], lambda: nc.vector.tensor_copy(out=dst3, in_=src3)))
         vector.append(q_quant("first", [], "first", low, 0, N, 0))
         vector.extend(k_quant(r) for r in range(1, PACK))
         for b in range(2):

import math
from contextlib import ExitStack

import concourse.mybir as mybir

H, KV, D, NQ, NT = 8, 2, 128, 512, 512
FLOPS = 2 * 2 * H * NQ * NT * D

F32 = mybir.dt.float32
BF16 = mybir.dt.bfloat16
U32 = mybir.dt.uint32
I32 = mybir.dt.int32
U8 = mybir.dt.uint8
FP8X4 = mybir.dt.float8_e4m3fn_x4
ACT = mybir.ActivationFunctionType
ALU = mybir.AluOpType

P = 128
PACK = 4
ROWS = 32
N = 128
HALF = 256
BANKS = 3
POLY = (352, 128)
WIDE = 3
JOINED = (0, 2, 4, 6)
ON_VECTOR = 7
Y_AFTER = {2: (0, 1), 3: (2, 3), 4: (4,)}
Y_BETWEEN = {}
SHARE = 96
SHARE2 = 16


def tanh_factors():
    nodes = [math.cos((2 * k + 1) * math.pi / 18) for k in range(9)]
    zs = [(x - nodes[-1]) / (1 - nodes[-1]) for x in nodes[:-1]]
    dd = [math.tanh(math.sqrt(z)) / math.sqrt(z) for z in zs]
    for level in range(1, 8):
        for i in range(7, level - 1, -1):
            dd[i] = (dd[i] - dd[i - 1]) / (zs[i] - zs[i - level])
    coef = [dd[7]]
    for i in range(6, -1, -1):
        coef = [x - zs[i] * w for x, w in zip(coef + [0.0], [0.0] + coef)]
        coef[-1] = coef[-1] + dd[i]
    lead = coef[0]
    monic = [x / lead for x in coef]

    def root(fun, x):
        for step in range(30):
            x = x - fun(x) * 1e-6 / (fun(x + 1e-6) - fun(x))
        return x

    def divide(s, e):
        p = list(monic)
        for i in range(len(p) - 2):
            p[i + 1] = p[i + 1] - s * p[i]
            p[i + 2] = p[i + 2] - e * p[i]
        return p[:-2], p[-2], p[-1]

    def nest(s):
        e = root(lambda x: divide(s, x)[1], 10.0)
        q, r1, r0 = divide(s, e)
        c = monic[1] - 3 * s
        for i in range(1, len(q)):
            q[i] = q[i] - c * q[i - 1]
        a = q[2] - s * s
        return (s, a, q[4], c, q[5], e, lead, r0 * lead), q[3] - a * s

    return nest(root(lambda s: nest(s)[1], -1.0))[0]


def tile_rows_a_silu_kb_mask_cap_kernel(tc, qT, kT, t, v, kb, mask, out):
    nc = tc.nc
    with ExitStack() as ctx:
        keep = ctx.enter_context(tc.tile_pool(name="keep", bufs=1))
        psum = ctx.enter_context(tc.psum_pool(name="psum", bufs=1))
        ctx.enter_context(tc.manual_schedule())

        low = slice(0, 3 * ROWS)
        both = slice(ROWS, 3 * ROWS)
        MID = NQ - N

        def rows_of(g):
            return slice(g * ROWS, (g + 1) * ROWS)

        def mx_tile(name, w):
            return keep.tile([P, w + w // 4], U32, name=name, align_bytes=64), w

        def words(mx, rows, c0, w):
            return mx[0][rows, c0 : c0 + w].bitcast(FP8X4)

        def scales(mx, rows, c0, w):
            return mx[0][rows, mx[1] : mx[1] + mx[1] // 4].bitcast(U8)[:, c0 : c0 + w]

        k_raw = keep.tile([P, PACK, NT], F32, name="k_raw")
        k_bf = keep.tile([P, PACK, N, PACK], BF16, name="k_bf", align_bytes=64)
        k_mx = mx_tile("k_mx", NT)
        edge_raw = keep.tile([P, PACK, N], F32, name="edge_raw")
        mid_raw = [keep.tile([P, PACK, w], F32, name="mid_raw%d" % w) for w in (HALF, N)]
        late_raw = keep.tile([P, PACK, NQ], F32, name="late_raw")
        q_bf = keep.tile([P, NQ, PACK], BF16, name="q_bf", align_bytes=64)
        q_mx = {name: mx_tile(name, w) for name, w in (("first", N), ("last", N), ("mid", MID), ("mid_moved", MID), ("late", NQ), ("late_moved", NQ), ("late_more", NQ))}
        v_raw = keep.tile([P, KV, PACK, D], F32, name="v_raw")
        v_bf = keep.tile([P, KV, D, PACK], BF16, name="v_bf", align_bytes=64)
        v_mx = mx_tile("v_mx", KV * D)
        mt = keep.tile([P, PACK, NQ], F32, name="mt")
        kb_raw = keep.tile([P, PACK], F32, name="kb_raw")
        kb_half = keep.tile([P, PACK], F32, name="kb_half")
        t_raw = keep.tile([P, PACK], F32, name="t_raw")
        zero = keep.tile([P, 1], F32, name="zero")
        w_ring = [keep.tile([P, NQ, PACK], BF16, name="w_bf%d" % i, align_bytes=64) for i in range(4)]
        score_banks = [[psum.tile([P, NQ], F32, name="sc%d_%d" % (kv, b)) for b in range(BANKS)] for kv in range(KV)]
        y_banks = [psum.tile([P, PACK, D], F32, name="y%d" % b) for b in range(2)]
        every = slice(0, P)

        sync, scalar, vector, tensor, pool = [], [], [], [], []

        def features(ap):
            return ap.rearrange("h (p j) n -> (h p) j n", j=PACK)

        def tokens(ap):
            return ap.rearrange("(p j) n -> p j n", j=PACK)

        def per_token(ap):
            return ap.rearrange("(p j) o -> p (j o)", j=PACK)

        def dma(name, needs, dst, src, queue=nc.sync):
            return (name, needs, lambda: queue.dma_start(out=dst, in_=src))

        def move(name, needs, source, g, into, target):
            return dma(name, needs, q_mx[into][0][rows_of(target)].bitcast(I32), q_mx[source][0][rows_of(g)].bitcast(I32))

        def interleave(name, needs, dst, src):
            return (
                name,
                needs,
                lambda: nc.vector.tensor_copy(
                    out=dst.rearrange("p (c i) j -> p c j i", i=4), in_=src.rearrange("p j (c i) -> p c j i", i=4)
                ),
            )

        def quantise(name, needs, mx, rows, c0, w, src):
            return (name, needs, lambda: nc.vector.quantize_mx(out=words(mx, rows, c0, w), scales=scales(mx, rows, c0, w), in_=src))

        def q_quant(name, needs, source, rows, c0, w, bf0):
            return quantise(name, needs, q_mx[source], rows, c0, w, q_bf[rows, bf0 : bf0 + w, :].rearrange("p n j -> p (n j)"))

        def k_quant(r):
            return quantise(("k", r), [("k_cast", r // 2), "k_rest"], k_mx, low, r * N, N, k_bf[low, r].rearrange("p s j -> p (s j)"))

        def k_cast_views(a, s0, s1):
            dst = k_bf[low, 2 * a : 2 * a + 2, s0:s1].rearrange("p r s j -> p s j r")
            src = k_raw[low].rearrange("p j (s r) -> p s j r", r=PACK)[:, s0:s1, :, 2 * a : 2 * a + 2]
            return dst, src

        scalar.append(dma("kb_raw", ["first_raw"], kb_raw[:], per_token(kb), nc.scalar))
        vector.append(("zero", ["first_raw"], lambda: nc.vector.memset(zero[:], 0.0)))
        scalar.append(
            (
                "edge_zero",
                ["zero"],
                lambda: nc.scalar.activation(
                    out=edge_raw[rows_of(0), 0, :],
                    in_=zero[rows_of(0)].to_broadcast([ROWS, N]),
                    func=ACT.Silu,
                ),
            )
        )
        scalar.append(dma("t_raw", [], t_raw[:], per_token(t), nc.scalar))
        pool.append(("edge_rest", ["first_raw"], lambda: nc.gpsimd.memset(edge_raw[rows_of(0), 1:PACK, :], 0.0)))
        vector.append((("k_zero", 0), [], lambda: nc.vector.memset(k_raw[rows_of(0)], 0.0)))
        for name in ("mid", "late"):
            vector.append((("plane", name), [], lambda name=name: nc.vector.memset(q_mx[name][0][:, q_mx[name][1] :], 0)))

        def blocks(head, q0, count, source, c0):
            return tuple((head, q0 + i * N, source, c0 + i * N) for i in range(count))

        near, far = (3, 4), (2, 5)
        first = [(kv, blocks(near[kv], 0, 1, "first", 0)) for kv in range(KV)]
        second = [(kv, blocks(near[kv], N, 2, "mid", 0)) for kv in range(KV)]
        whole = [(kv, blocks(far[kv], N, 3, "mid_moved", 0) + blocks(near[kv], 3 * N, 1, "mid", HALF)) for kv in range(KV)]
        whole = whole + [(0, blocks(0, 0, 4, "late", 0)), (1, blocks(6, 0, 4, "late_moved", 0))]
        whole = whole + [(0, blocks(1, 0, 4, "late_moved", 0)), (1, blocks(7, 0, 3, "late_more", 0))]
        last = [(1, blocks(7, 3 * N, 1, "late_more", 3 * N) + blocks(far[1], 0, 1, "last", 0)), (0, blocks(far[0], 0, 1, "last", 0))]

        def operand_ready(kv, block):
            source = block[2]
            if source == "mid":
                return ("mid", block[3] // N)
            return (source, block[0]) if source == "mid_moved" else source

        sync.append(dma("k_raw", [], k_raw[both], features(kT)))
        sync.append(dma("first_raw", [], edge_raw[both], features(qT[3:5, :, 0:N])))
        sync.append(dma(("mid_raw", 0), [], mid_raw[0][:], features(qT[2:6, :, N : N + HALF])))
        sync.append(dma(("mid_raw", 1), [], mid_raw[1][:], features(qT[2:6, :, N + HALF : NQ])))
        sync.append(dma(("mask", 0), [], mt[:, 0:2, :], tokens(mask)[:, 0:2, :]))
        sync.append(dma(("mask", 1), [], mt[:, 2:4, :], tokens(mask)[:, 2:4, :]))
        sync.append(move(("mid_moved", 2), [("mid", 2)], "mid", 0, "mid_moved", 1))
        sync.append(move(("mid_moved", 5), [("mid", 2)], "mid", 3, "mid_moved", 2))
        sync.append(dma(("late_raw", 0), [], late_raw[both], features(qT[0:2])))
        sync.append(dma(("late_raw", 1), [], late_raw[rows_of(3)], features(qT[6:7])))
        sync.append(dma(("late_raw", 2), [], late_raw[rows_of(0)], features(qT[7:8])))
        sync.append(dma("v_raw", [], v_raw[:], v.rearrange("g (p j) e -> p g j e", j=PACK)))
        for kv in range(KV):
            head = far[kv]
            sync.append(dma(("last_raw", kv), ["first_cast"], edge_raw[rows_of(1 + kv)], features(qT[head : head + 1, :, 0:N])))
        sync.append(dma("late_moved", ["late"], q_mx["late_moved"][0][both].bitcast(I32), q_mx["late"][0][2 * ROWS : P].bitcast(I32)))
        sync.append(move("late_more", ["late"], "late", 0, "late_more", 2))

        dst0, src0 = k_cast_views(0, 0, SHARE)
        dst1, src1 = k_cast_views(1, SHARE2, N)
        dst3, src3 = k_cast_views(1, 0, SHARE2)
        dst2, src2 = k_cast_views(0, SHARE, N)
        scalar.append(("k_rest", ["k_raw", ("k_zero", 0)], lambda: nc.scalar.copy(out=dst2, in_=src2)))
        vector.append((("k_cast", 0), ["k_raw"], lambda: nc.vector.tensor_copy(out=dst0, in_=src0)))
        scalar.append((("k_cast", 1), ["k_raw", ("k_zero", 0)], lambda: nc.scalar.copy(out=dst1, in_=src1)))
        scalar.append(("kb_half", ["kb_raw"], lambda: nc.scalar.activation(out=kb_half[:], in_=kb_raw[:], func=ACT.Copy, scale=0.5)))
        vector.append(interleave("first_cast", ["first_raw", "edge_zero", "edge_rest"], q_bf[low, 0:N, :], edge_raw[low]))
        vector.append(k_quant(0))
        vector.append(("k_more", [], lambda: nc.vector.tensor_copy(out=dst3, in_=src3)))
        vector.append(q_quant("first", [], "first", low, 0, N, 0))
        vector.extend(k_quant(r) for r in range(1, PACK))
        for b in range(2):
            vector.append(interleave(("mid_cast", 0, b), [("mid_raw", 0)], q_bf[:, (1 + b) * N : (2 + b) * N, :], mid_raw[0][:, :, b * N : (b + 1) * N]))
        vector.extend(q_quant(("mid", b), [], "mid", every, b * N, N, (1 + b) * N) for b in range(2))
        vector.append(interleave(("mid_cast", 1), [("mid_raw", 1)], q_bf[:, N + HALF : NQ, :], mid_raw[1][:]))

        capped, own = {}, {}
        first_capped = keep.tile([P, PACK, 2 * N], F32, name="first_capped")
        first_gated = keep.tile([P, PACK, 2 * N], F32, name="first_gated")
        second_capped = keep.tile([P, PACK, NQ], F32, name="second_capped")
        second_gated = keep.tile([P, PACK, NQ], F32, name="second_gated")
        for kv in range(KV):
            capped[first[kv]] = first_capped[:, :, kv * N : (kv + 1) * N]
            capped[second[kv]] = second_capped[:, :, kv * HALF : (kv + 1) * HALF]
        shared = {"first": (first, first_capped, first_gated, ["poly"]), "second": (second[::-1], second_capped, second_gated, ["poly 2"])}
        for i, unit in enumerate(whole + last):
            tile = keep.tile([P, PACK, N * len(unit[1])], F32, name="capped%d" % i)
            capped[unit] = tile[:]
            own[unit] = tile

        def caps(unit, *slots):
            return [("cap", unit, r) for r in slots]

        def gate(unit, c0, w):
            return [("silu", unit, c0, w)]

        order = []
        for r in range(PACK):
            order = order + caps(first[0], r) + caps(first[1], r)
        order = order + [("silu", "first", POLY[0], 3 * HALF), ("silu", "first", 3 * HALF, 4 * HALF)]
        for r in range(PACK):
            order = order + caps(second[0], r) + caps(second[1], r)
        order = order + gate("second", POLY[1], 3 * NQ) + caps(whole[0], 0) + gate("second", 3 * NQ, 4 * NQ) + caps(whole[0], 1, 2, 3)
        for i in range(1, len(whole)):
            unit, before = whole[i], whole[i - 1]
            if i <= WIDE:
                order = order + caps(unit, 0) + gate(before, 0, NQ) + caps(unit, 1, 2, 3)
            elif unit != whole[-1]:
                order = order + caps(unit, 0) + gate(before, 0, HALF) + gate(before, HALF, HALF) + caps(unit, 1, 2, 3)
            else:
                order = order + caps(unit, 0) + gate(before, 0, HALF) + caps(unit, 1) + gate(before, HALF, HALF) + caps(unit, 2, 3)
        order = order + caps(last[0], 0) + gate(whole[-1], 0, N) + caps(last[0], 1) + gate(whole[-1], N, N) + caps(last[0], 2, 3) + gate(whole[-1], HALF, N)
        order = order + gate(last[0], 0, N) + caps(last[1], 0, 1) + gate(last[0], N, N // 2) + caps(last[1], 2, 3)
        order = order + gate(last[0], N + N // 2, N // 2) + gate(last[1], 0, N // 2) + gate(last[1], N // 2, N // 2)

        def fills_of(unit):
            per_bank = NQ // (N * len(unit[1])) if unit == last[1] else 1
            return [(unit, tuple(range(r, r + per_bank))) for r in range(0, PACK, per_bank)]

        bank_of, before_in_bank = {}, {}
        for kv in range(KV):
            row = [fill for unit in first + second + whole + last if unit[0] == kv for fill in fills_of(unit)]
            for i, fill in enumerate(row):
                bank_of[fill] = score_banks[kv][i % BANKS]
                before_in_bank[fill] = row[i - BANKS] if i >= BANKS else None

        def passes(fill):
            (kv, cols), slots = fill
            rows = rows_of(1 + kv)
            old = before_in_bank[fill]
            free = [("cap", old[0], r) for r in old[1]] if old else []
            result = []
            for e, r in enumerate(slots):
                for b, block in enumerate(cols):
                    c = (e * len(cols) + b) * N

                    def call(dst=bank_of[fill][:, c : c + N], r=r, block=block):
                        nc.tensor.matmul_mx(
                            out=dst,
                            lhsT=words(k_mx, rows, r * N, N),
                            lhsT_scale=scales(k_mx, rows, r * N, N),
                            rhs=words(q_mx[block[2]], rows, block[3], N),
                            rhs_scale=scales(q_mx[block[2]], rows, block[3], N),
                            start=True,
                            stop=True,
                        )

                    result.append((("pass", fill, r, b), free + [("k", r), operand_ready(kv, block)], call))
            return result

        def side_by_side(a, b):
            result = []
            for i in range(max(len(a), len(b))):
                result = result + a[i : i + 1] + b[i : i + 1]
            return result

        def cap(unit, r):
            fill = [f for f in fills_of(unit) if r in f[1]][0]
            w = N * len(unit[1])
            e = fill[1].index(r)
            needs = ["kb_half"] + [("pass", fill, s, b) for s in fill[1] for b in range(len(unit[1]))]
            return (
                ("cap", unit, r),
                needs,
                lambda: nc.scalar.activation(
                    out=capped[unit][:, r, :], in_=bank_of[fill][:, e * w : (e + 1) * w], func=ACT.Tanh, scale=0.5, bias=kb_half[:, r : r + 1]
                ),
            )

        pieces = []
        flat = "p r n -> p (r n)"
        for step in order:
            if step[0] == "cap":
                scalar.append(cap(step[1], step[2]))
                continue
            unit, c0, w = step[1:]
            if unit in shared:
                pair, src, dst, also = shared[unit]
                width = N * len(pair[0][1])
                if w == 2 * PACK * width:
                    pieces.extend((one, 0, width, dst[:, :, one[0] * width : (one[0] + 1) * width], [step]) for one in pair)
                dst, src = dst[:].rearrange(flat)[:, c0:w], src[:].rearrange(flat)[:, c0:w]
            else:
                result = keep.tile([P, PACK, w], F32, name="gated%d" % len(pieces))
                dst, src = result[:], capped[unit][:, :, c0 : c0 + w]
                c = c0
                while c < c0 + w:
                    head = unit[1][c // N][0]
                    width = min(c0 + w, N * max(b + 1 for b, block in enumerate(unit[1]) if block[0] == head)) - c
                    pieces.append((unit, c, width, result[:, :, c - c0 : c - c0 + width], [step]))
                    c += width
            scalar.append((step, [], lambda dst=dst, src=src: nc.scalar.activation(out=dst, in_=src, func=ACT.Silu, scale=2.0)))

        w_mx, w_col = {}, {}
        for i, together in enumerate([first, second[::-1]] + [[unit] for unit in whole + last]):
            width = N * len(together[0][1])
            sheet = mx_tile("w_mx%d" % i, width * len(together))
            for e, unit in enumerate(together):
                w_mx[unit], w_col[unit] = sheet, e * width

        batch_of = [n - sum(1 for m in JOINED if m < n) for n in range(len(pieces))]

        def batch(n):
            return [m for m in range(len(pieces)) if batch_of[m] == batch_of[n]]

        def weights(n):
            unit, c0, w, gated, needs = pieces[n]
            q0 = unit[1][c0 // N][1] + c0 % N
            at = sum(pieces[m][2] for m in batch(n) if m < n)
            return (
                ("weights", n),
                needs + [("mt", r) for r in range(PACK)],
                lambda: nc.vector.tensor_tensor(
                    out=w_ring[batch_of[n] % 4][:, at : at + w, :].rearrange("p (c i) r -> p c r i", i=4),
                    in0=gated.rearrange("p r (c i) -> p c r i", i=4),
                    in1=mt[:, :, q0 : q0 + w].rearrange("p r (c i) -> p c r i", i=4),
                    op=ALU.mult,
                ),
            )

        def w_quant(n):
            unit, c0 = pieces[batch(n)[0]][0:2]
            w = sum(pieces[m][2] for m in batch(n))
            src = w_ring[batch_of[n] % 4][:, 0:w, :].rearrange("p n j -> p (n j)")
            return quantise(("w", batch_of[n]), [], w_mx[unit], every, w_col[unit] + c0, w, src)

        groups = [[(unit, 0, 1) for unit in first], [(unit, 0, 2) for unit in second]] + [[(unit, 0, len(unit[1]))] for unit in whole]
        groups = groups + [[(last[0], 0, 1)], [(last[0], 1, 1)], [(last[1], 0, 1)]]

        def products(i):
            free = [("res", i - 2)] if i >= 2 else []
            result = []
            place = 0
            for unit, b0, count in groups[i]:
                for b in range(b0, b0 + count):
                    made = [("w", batch_of[n]) for n, piece in enumerate(pieces) if piece[0] == unit and piece[1] < (b + 1) * N and piece[1] + piece[2] > b * N]

                    def call(dst=y_banks[i % 2][:, place, :], unit=unit, b=b):
                        nc.tensor.matmul_mx(
                            out=dst,
                            lhsT=words(w_mx[unit], every, w_col[unit] + b * N, N),
                            lhsT_scale=scales(w_mx[unit], every, w_col[unit] + b * N, N),
                            rhs=words(v_mx, every, unit[0] * D, D),
                            rhs_scale=scales(v_mx, every, unit[0] * D, D),
                            start=True,
                            stop=True,
                        )

                    result.append((("y", i, place), free + made + ["v"], call))
                    place += 1
            return result

        def result_out(i, on_scalar):
            cols = [unit[1][b] for unit, b0, count in groups[i] for b in range(b0, b0 + count)]
            res = res_room[i][:].rearrange("p r n -> p (r n)")[:, 0 : len(cols) * D].rearrange("p (c e) -> p c e", e=D)
            y = y_banks[i % 2][:, 0 : len(cols), :]
            start = 0
            if i == 0:
                stores[i] = [dma(("out", i), [("res", i)], out[3:5, 0:N, :].rearrange("h p e -> p h e"), res)]
            for e in range(1, len(cols) + 1 if i else 0):
                if e == len(cols) or cols[e][0] != cols[start][0]:
                    head, q0 = cols[start][0:2]
                    rows = out[head, q0 : q0 + (e - start) * N, :].rearrange("(c p) e -> p c e", p=P)
                    stores.setdefault(i, []).append(dma(("out", i, start), [("res", i)], rows, res[:, start:e, :]))
                    start = e
            needs = [("y", i, e) for e in range(len(cols))]
            if on_scalar:
                return (("res", i), needs, lambda: nc.scalar.activation(out=res, in_=y, func=ACT.Copy, scale=1.0 / 16.0))
            return (("res", i), needs, lambda: nc.vector.tensor_scalar(out=res, in0=y, scalar1=1.0 / 16.0, scalar2=None, op0=ALU.mult))

        stores = {}
        res_room = [first_capped, second_capped] + [own[unit] for unit in whole] + [own[last[0]], own[whole[0]], own[last[1]]]

        s, a, b, c, d, e, lead, f = tanh_factors()
        room = [k_raw[:, j, :] for j in range(PACK)] + [mid_raw[0][:, 2 * j : 2 * j + 2, :].rearrange("p j n -> p (j n)") for j in range(2)]

        def polynomial(share, source, result, at, ready):
            u, p = source[:].rearrange(flat)[:, 0 : POLY[share]], result[:].rearrange(flat)[:, 0 : POLY[share]]
            z, y, zc, ye, r1, r2 = [x[:, at : at + POLY[share]] for x in room]

            def fold(name, dst, src, add, other):
                call = lambda: nc.vector.scalar_tensor_tensor(out=dst, in0=src, scalar=add, in1=other, op0=ALU.add, op1=ALU.mult)
                return ((name, share), ready, call)

            def moved(name, dst, src, add, times):
                call = lambda: nc.vector.tensor_scalar(out=dst, in0=src, scalar1=add, scalar2=times, op0=ALU.add, op1=ALU.mult)
                return ((name, share), ready, call)

            return [
                fold("z", z, u, 0.0, u),
                fold("y", y, z, s, z),
                moved("zc", zc, z, c, 1.0),
                fold("degree 4", r1, y, a, y),
                moved("ye", ye, y, e, lead),
                fold("degree 5", r2, r1, b, zc),
                fold("degree 7", r1, r2, d, ye),
                fold("tanh", r2, r1, f, u),
                fold("silu", p, r2, 1.0, u),
            ]

        one = polynomial(0, first_capped, first_gated, 0, [("k_cast", 1)] + [("cap", unit, r) for unit in first for r in range(2)])
        two = polynomial(1, second_capped, second_gated, POLY[0], [("cap", second[0], 0)])

        def mask_t(r, c0=0, c1=NQ):
            return (
                ("mt", r) if c0 == 0 else ("mt", r, c0),
                [("mask", r // 2), "t_raw"],
                lambda: nc.vector.tensor_scalar(out=mt[:, r, c0:c1], in0=mt[:, r, c0:c1], scalar1=t_raw[:, r : r + 1], scalar2=None, op0=ALU.mult),
            )

        v_cast = (
            "v_cast",
            ["v_raw"],
            lambda: nc.vector.tensor_copy(
                out=v_bf[:].rearrange("p g (c i) j -> p g c j i", i=4), in_=v_raw[:].rearrange("p g j (c i) -> p g c j i", i=4)
            ),
        )
        v_quant = quantise("v", [], v_mx, every, 0, KV * D, v_bf[:].rearrange("p g e j -> p (g e j)"))
        late_cast = interleave("late_cast", [("late_raw", e) for e in range(3)], q_bf[:], late_raw[:])
        late_quant = q_quant("late", [], "late", every, 0, NQ, 0)
        last_cast = interleave("last_cast", [("last_raw", 0), ("last_raw", 1)], q_bf[low, 0:N, :], edge_raw[low])
        last_quant = q_quant("last", [], "last", low, 0, N, 0)

        vector.extend([one[0], q_quant(("mid", 2), [], "mid", every, HALF, N, N + HALF)] + one[1:5])
        vector.extend([two[0], one[5], mask_t(0), two[1], one[6], two[2], mask_t(1), two[3], one[7], two[4], mask_t(2), two[5]])
        vector.extend([mask_t(3, 0, N), one[8], two[6], mask_t(3, N, NQ)])

        def res(i):
            return result_out(i, False)

        vector.extend([weights(0), two[7], weights(1), two[8], weights(2), late_cast, w_quant(1), late_quant, v_cast, weights(3), v_quant, w_quant(3)])
        vector.extend([weights(4), weights(5), last_cast, w_quant(5), last_quant])
        vector.extend([weights(6), res(0), weights(7), res(1), w_quant(7)])
        vector.extend([weights(8), res(2), w_quant(8), res(3)])
        vector.extend([weights(9), weights(10), w_quant(9), res(4), w_quant(10)])
        vector.extend([weights(11), res(5), weights(12), w_quant(11), w_quant(12)])
        vector.extend([weights(13), weights(14), w_quant(13), res(6), weights(15), w_quant(14), weights(16), w_quant(15)])
        vector.extend([weights(17), w_quant(16), weights(18), weights(19), weights(20)])
        vector.extend(w_quant(n) for n in range(17, 21))
        for i in range(ON_VECTOR, len(groups)):
            on_scalar = i < len(groups) - 1
            (scalar if on_scalar else vector).append(result_out(i, on_scalar))
        for i in range(len(groups)):
            sync.extend(stores[i])

        def lane_of(fills):
            return [call for fill in fills for call in passes(fill)]

        for a, b in zip(fills_of(first[0]), fills_of(first[1])):
            tensor.extend(side_by_side(passes(a), passes(b)))
        for a, b in zip(fills_of(second[0]), fills_of(second[1])):
            tensor.extend(side_by_side(passes(a), passes(b)))
        tensor.extend(lane_of(fills_of(whole[0])[0:2]))
        for i, unit in enumerate(whole[:-1]):
            if i == 0:
                tensor.extend(side_by_side(passes(fills_of(whole[1])[0]), passes(fills_of(unit)[2])))
                tensor.extend(passes(fills_of(unit)[3]) + passes(fills_of(whole[1])[1]))
            elif i in (1, 2):
                tensor.extend(lane_of(fills_of(unit)[2:4] + fills_of(whole[i + 1])[0:2]))
            else:
                for r in range(2):
                    tensor.extend(side_by_side(passes(fills_of(whole[i + 1])[r]), passes(fills_of(unit)[2 + r])))
                    if r == 0 and i in Y_BETWEEN:
                        tensor.extend(products(Y_BETWEEN[i]))
            for g in Y_AFTER.get(i, []):
                tensor.extend(products(g))
        tensor.extend(side_by_side(lane_of(fills_of(last[1])), passes(fills_of(whole[-1])[2])))
        tensor.extend(passes(fills_of(whole[-1])[3]) + products(5) + lane_of(fills_of(last[0])))
        for g in range(6, len(groups)):
            tensor.extend(products(g))

        queues = [sync, pool, vector, scalar, tensor]
        heads = [0] * len(queues)
        done = set()
        while any(h < len(queue) for h, queue in zip(heads, queues)):
            moved_on = False
            for e, queue in enumerate(queues):
                while heads[e] < len(queue) and all(need in done for need in queue[heads[e]][1]):
                    name, needs, call = queue[heads[e]]
                    call()
                    done.add(name)
                    heads[e] += 1
                    moved_on = True
            assert moved_on, [queue[h][0:2] for h, queue in zip(heads, queues) if h < len(queue)]
